import numpy as np
import ml_dtypes


def mxq(x, axis, fmt="e4m3"):
    dtype, down = {"e4m3": (ml_dtypes.float8_e4m3fn, 7), "e5m2": (ml_dtypes.float8_e5m2, 14)}[fmt]
    v = np.moveaxis(np.asarray(x, np.float32).astype(ml_dtypes.bfloat16).astype(np.float64), axis, -1)
    blocks = v.reshape(v.shape[:-1] + (-1, 32))
    amax = np.abs(blocks).max(-1, keepdims=True)
    byte = np.maximum(np.where(amax > 0, np.frexp(amax)[1] - 1 + 127, 0) - down, 1)
    scale = np.exp2(byte - 127.0)
    codes = (blocks / scale).astype(np.float32).astype(dtype).astype(np.float64)
    return np.moveaxis((codes * scale).reshape(v.shape), -1, axis)


WIDE = False


def mx_kscale(k):
    if not WIDE:
        return np.ones(k)
    levels = np.array([10, -10, 5, -5, 0])
    if k % 512:
        return np.exp2(np.random.permutation(np.resize(levels, k // 32))).repeat(32)
    a = np.empty((k // 512, 16))
    for p in range(k // 512):
        a[p, :8] = np.random.permutation(np.resize(levels, 8))
        for g in range(8):
            far = levels[np.abs(levels - a[p, g]) >= 10]
            a[p, g + 8] = far[np.random.randint(len(far))]
    return np.exp2(a.ravel()).repeat(32)


def f64(x):
    return np.asarray(x).astype(np.float64)


def striped(idx):
    return np.tile(idx.reshape(-1, 16).T, (8, 1)).astype(np.uint16)


def unstriped(offs):
    return offs[:16].T.reshape(-1).astype(np.int64)


E2M1 = np.array([0.0, 0.5, 1.0, 1.5, 2.0, 3.0, 4.0, 6.0, -0.0, -0.5, -1.0, -1.5, -2.0, -3.0, -4.0, -6.0])


def pack_weight(w, fmt):
    k, n = w.shape
    w = f64(np.asarray(w, np.float32).astype(ml_dtypes.bfloat16)).reshape(k // 32, 32, n)
    amax = np.abs(w).max(1)
    if fmt == "e4m3":
        byte = np.frexp(amax)[1] - 1 + 127 - 7
    else:
        mant, ex = np.frexp(amax / 6.0)
        byte = np.where(mant > 0.5, ex, ex - 1) + 127
    byte = np.clip(np.where(amax > 0, byte, 1), 1, 254)
    scaled = (w * np.exp2(127.0 - byte)[:, None, :]).reshape(k, n).astype(np.float32)
    by_word = np.ascontiguousarray(scaled.reshape(k // 512, 128, 4, n).transpose(0, 1, 3, 2))
    if fmt == "e4m3":
        words = by_word.astype(ml_dtypes.float8_e4m3fn).view(np.uint8)
    else:
        c = by_word.astype(ml_dtypes.float4_e2m1fn).view(np.uint8) & 0xF
        words = (c[..., 0::2] | (c[..., 1::2] << 4)).reshape(k // 512, 128, 2 * n)
    return np.ascontiguousarray(words), np.ascontiguousarray(byte.astype(np.uint8).reshape(k // 512, 16, n))


def unpack_weight(words, scales, fmt):
    g, _, n = scales.shape
    words = np.ascontiguousarray(words).reshape(g, 128, n, -1)
    if fmt == "e4m3":
        vals = words.view(ml_dtypes.float8_e4m3fn).astype(np.float64)
    else:
        nib = np.empty((g, 128, n, 4), np.uint8)
        nib[..., 0::2] = words & 0xF
        nib[..., 1::2] = words >> 4
        vals = E2M1[nib]
    vals = vals * np.repeat(np.exp2(scales.astype(np.float64) - 127.0), 8, axis=1)[..., None]
    return vals.transpose(0, 1, 3, 2).reshape(g * 512, n)


def gelu(v):
    return 0.5 * v * (1.0 + np.tanh(np.sqrt(2.0 / np.pi) * (v + 0.044715 * v**3)))


def bf(x):
    return np.asarray(x, np.float32).astype(ml_dtypes.bfloat16)


def planes(Y):
    n, m = Y.shape
    b = f64(bf(Y)).reshape(n // 32, 32, m)
    amax = np.abs(b).max(1)
    byte = np.clip(np.where(amax > 0, np.frexp(amax)[1] - 1 + 127 - 7, 1), 1, 254)
    codes = (b * np.exp2(127.0 - byte)[:, None, :]).reshape(n, m).astype(np.float32).astype(ml_dtypes.float8_e4m3fn).view(np.uint8)
    words = codes.reshape(n // 512, 128, 4, m).transpose(0, 1, 3, 2)
    return np.ascontiguousarray(words), np.ascontiguousarray(byte.astype(np.uint8).reshape(n // 512, 16, m))


K, H, N, T, S, PART = 1024, 1024, 512, 2048, 1024, 128


def setup_inputs():
    n = np.random.standard_normal
    s = mx_kscale(K)[:, None]
    u = mx_kscale(H)[:, None]
    size = np.exp(0.8 * n(N))
    tab_words, tab_scales = pack_weight(n((K, T)) * s, "e4m3")
    w1_words, w1_scales = pack_weight(n((K, H)) / np.sqrt(K) / s, "e2m1")
    w3_words, w3_scales = pack_weight(2.0 * n((H, N)) / np.sqrt(H) / u * size, "e4m3")
    return {
        "tab_words": tab_words, "tab_scales": tab_scales,
        "offs": striped(np.random.permutation(T)[:S]),
        "w1_words": w1_words, "w1_scales": w1_scales,
        "w2": (n((K, H)) / np.sqrt(K) / s).astype(np.float32),
        "gain": (np.exp(0.3 * n(H)) * u[:, 0]).astype(np.float32),
        "w3_words": w3_words, "w3_scales": w3_scales,
        "wgo": np.exp(0.3 * n((PART, S))).astype(np.float32),
        "offs2": striped(np.random.permutation(S)),
        "x0": (n((N, S)) * size[:, None]).astype(np.float32),
    }


def reference(tab_words, tab_scales, offs, w1_words, w1_scales, w2, gain,
              w3_words, w3_scales, wgo, offs2, x0):
    v = unpack_weight(tab_words, tab_scales, "e4m3")[:, unstriped(offs)]
    a = unpack_weight(w1_words, w1_scales, "e2m1").T @ v
    b = mxq(f64(w2), 0, "e4m3").T @ v
    h = f64(gain)[:, None] * (a - b) / (0.5 + np.abs(a) + np.abs(b))
    d = unpack_weight(w3_words, w3_scales, "e4m3").T @ mxq(h, 0, "e4m3")
    page = np.zeros((N, S))
    page[:, unstriped(offs2)] = np.tile(f64(wgo), (N // PART, 1)) * d
    y = np.maximum(page, f64(x0))
    words, scales = planes(y)
    return y, words, scales

@@ -1,0 +1,313 @@
+from contextlib import ExitStack
+
+import concourse.mybir as mybir
+from concourse.masks import make_identity
+
+K, H, N, T, S = 1024, 1024, 512, 2048, 1024
+FLOPS = 2 * S * (2 * K * H + H * N)
+
+F32 = mybir.dt.float32
+BF16 = mybir.dt.bfloat16
+I32 = mybir.dt.int32
+U32 = mybir.dt.uint32
+U16 = mybir.dt.uint16
+U8 = mybir.dt.uint8
+E4M3 = mybir.dt.float8_e4m3fn_x4
+E2M1 = mybir.dt.float4_e2m1fn_x4
+ACT = mybir.ActivationFunctionType
+ALU = mybir.AluOpType
+
+P = 128
+PACK = 4
+KP = P * PACK
+PASSES = 2
+QUADS = 4
+JT = 128
+GATHER = 256
+YCH = 256
+
+
+def load_scales(queue, plane, scales):
+    for q in range(QUADS):
+        queue.dma_start(
+            out=plane[32 * q : 32 * q + 4, :].bitcast(I32).rearrange("r (a c) -> r a c", a=PASSES),
+            in_=scales[:, 4 * q : 4 * q + 4, :].bitcast(I32).rearrange("a r c -> r a c"),
+        )
+
+
+def tile_list_loom_contrast_kernel(
+    tc, tab_words, tab_scales, offs, w1_words, w1_scales, w2, gain,
+    w3_words, w3_scales, wgo, offs2, x0, out_0, out_1, out_2,
+):
+    nc = tc.nc
+    with ExitStack() as ctx:
+        keep = ctx.enter_context(tc.tile_pool(name="keep", bufs=1))
+        ring = ctx.enter_context(tc.tile_pool(name="ring", bufs=2))
+        psum = ctx.enter_context(tc.psum_pool(name="psum", bufs=1))
+
+        picks = keep.tile([P, S // 16], U16, name="picks")
+        places = keep.tile([P, S // 16], U16, name="places")
+        tab_plane = keep.tile([P, PASSES * T], U8, name="tab_plane", align_bytes=64)
+        w1_plane = keep.tile([P, PASSES * H], U8, name="w1_plane", align_bytes=64)
+        w3_plane_raw = keep.tile([P, PASSES * N], U8, name="w3_plane_raw", align_bytes=64)
+        nc.vector.memset(tab_plane[:].bitcast(I32), 0)
+        nc.gpsimd.memset(w1_plane[:].bitcast(I32), 0)
+        nc.gpsimd.memset(w3_plane_raw[:].bitcast(I32), 0)
+        half = keep.tile([P, 1], F32, name="half")
+        nc.gpsimd.memset(half[:], 0.5)
+        ident = keep.tile([P, P], F32, name="ident")
+        make_identity(nc, ident[:])
+        warm = keep.tile([P, 1], F32, name="warm")
+        nc.scalar.activation(warm[:], half[:], ACT.Abs_reciprocal_sqrt, bias=half[:])
+
+        tab = [keep.tile([P, T], I32, name="tab%d" % a, align_bytes=64) for a in range(PASSES)]
+        w2_raw = {}
+
+        def load_w2(a, b):
+            raw = keep.tile([P, PACK, KP], F32, name="w2_raw%d%d" % (a, b))
+            nc.sync.dma_start(
+                out=raw[:],
+                in_=w2[KP * a : KP * (a + 1), KP * b : KP * (b + 1)].rearrange("(p i) c -> p i c", i=PACK),
+            )
+            w2_raw[a, b] = raw
+
+        def load_tab(a):
+            nc.sync.dma_start(
+                out=tab[a][:], in_=tab_words[a].rearrange("p t i -> p (t i)").bitcast(I32)
+            )
+
+        nc.sync.dma_start(picks[:], offs)
+        load_scales(nc.sync, tab_plane, tab_scales)
+        load_w2(0, 0)
+        load_tab(0)
+        load_w2(1, 0)
+        load_tab(1)
+        load_scales(nc.sync, w1_plane, w1_scales)
+        w1 = keep.tile([P, PASSES * 2 * H], U8, name="w1", align_bytes=64)
+        nc.sync.dma_start(
+            out=w1[:].bitcast(I32).rearrange("p (a c) -> p a c", a=PASSES),
+            in_=w1_words.bitcast(I32).rearrange("a p c -> p a c"),
+        )
+        gains = keep.tile([P, PASSES, PACK], F32, name="gains")
+        nc.sync.dma_start(out=gains[:], in_=gain.rearrange("(b p t) -> p b t", b=PASSES, t=PACK))
+        load_w2(0, 1)
+        load_w2(1, 1)
+        w3_raw = keep.tile([P, PASSES * N], I32, name="w3_raw", align_bytes=64)
+        nc.sync.dma_start(
+            out=w3_raw[:].rearrange("p (a c) -> p a c", a=PASSES),
+            in_=w3_words.rearrange("a p c i -> p a (c i)").bitcast(I32),
+        )
+        load_scales(nc.sync, w3_plane_raw, w3_scales)
+        nc.sync.dma_start(places[:], offs2)
+        factor = keep.tile([P, PACK, S], F32, name="factor")
+        for q in range(QUADS):
+            nc.sync.dma_start(
+                out=factor[32 * q : 32 * (q + 1), :, :],
+                in_=wgo.rearrange("(r t) j -> r t j", t=PACK),
+            )
+        y = keep.tile([P, PACK, S], F32, name="y")
+        x0_rows = x0.rearrange("(p t) m -> p t m", t=PACK)
+        for t in range(PACK):
+            nc.sync.dma_start(out=y[:, t, :], in_=x0_rows[:, t, :])
+
+        v_plane = []
+        for a in range(PASSES):
+            plane = keep.tile([P, S], U8, name="v_plane%d" % a, align_bytes=64)
+            nc.vector.tensor_copy(plane[:], tab_plane[:, T * a : T * (a + 1)].indirect(picks[:]))
+            v_plane.append(plane)
+
+        w2_codes, w2_plane = {}, {}
+
+        def quantise_w2(a, b, cast):
+            grouped = ring.tile([P, KP, PACK], BF16, name="w2_grouped", align_bytes=64)
+            cast(
+                grouped[:].rearrange("p (c e) i -> p c i e", e=2),
+                w2_raw[a, b][:].rearrange("p i (c e) -> p c i e", e=2),
+            )
+            codes = keep.tile([P, KP], U32, name="w2_codes%d%d" % (a, b), align_bytes=64)
+            plane = keep.tile([P, KP], U8, name="w2_plane%d%d" % (a, b), align_bytes=64)
+            nc.vector.quantize_mx(
+                out=codes[:].bitcast(E4M3), scales=plane[:], in_=grouped[:].rearrange("p c i -> p (c i)")
+            )
+            w2_codes[a, b], w2_plane[a, b] = codes, plane
+
+
+        v_words = {}
+
+        for a in range(PASSES):
+            quantise_w2(a, 0, nc.scalar.copy)
+            for g in range(S // GATHER):
+                cols = slice(g * GATHER // 16, (g + 1) * GATHER // 16)
+                words = keep.tile([P, GATHER], U32, name="v_words%d%d" % (a, g), align_bytes=64)
+                nc.vector.tensor_copy(words[:], tab[a][:].bitcast(U32).indirect(picks[:, cols]))
+                v_words[a, g] = words
+
+        w3 = keep.tile([P, PASSES * N], I32, name="w3", align_bytes=64)
+        w3_plane = keep.tile([P, PASSES * N], U8, name="w3_plane", align_bytes=64)
+
+        def deal_w3():
+            nc.vector.tensor_copy(
+                w3[:].rearrange("p (a t m) -> p a t m", a=PASSES, t=PACK),
+                w3_raw[:].rearrange("p (a m t) -> p a t m", a=PASSES, t=PACK),
+            )
+            nc.vector.tensor_copy(
+                w3_plane[:].rearrange("p (a t m) -> p a t m", a=PASSES, t=PACK),
+                w3_plane_raw[:].rearrange("p (a m t) -> p a t m", a=PASSES, t=PACK),
+            )
+
+        pages = [keep.tile([P, S], F32, name="page%d" % t) for t in range(PACK)]
+        sums = {}
+        h_codes, h_plane = {}, {}
+
+        banks = {}
+
+        def products(jt, b):
+            g, lo = divmod(jt * JT, GATHER)
+            a_ps = psum.tile([P, KP], F32, name="a_ps")
+            b_ps = psum.tile([P, KP], F32, name="b_ps")
+            for a in range(PASSES):
+                nc.tensor.matmul_mx(
+                    out=a_ps[:],
+                    lhsT=v_words[a, g][:, lo : lo + JT].bitcast(E4M3),
+                    lhsT_scale=v_plane[a][:, jt * JT : (jt + 1) * JT],
+                    rhs=w1[:, 2 * (H * a + KP * b) : 2 * (H * a + KP * (b + 1))].bitcast(E2M1),
+                    rhs_scale=w1_plane[:, H * a + KP * b : H * a + KP * (b + 1)],
+                    start=(a == 0),
+                    stop=(a == PASSES - 1),
+                )
+            for a in range(PASSES):
+                nc.tensor.matmul_mx(
+                    out=b_ps[:],
+                    lhsT=v_words[a, g][:, lo : lo + JT].bitcast(E4M3),
+                    lhsT_scale=v_plane[a][:, jt * JT : (jt + 1) * JT],
+                    rhs=w2_codes[a, b][:].bitcast(E4M3),
+                    rhs_scale=w2_plane[a, b][:],
+                    start=(a == 0),
+                    stop=(a == PASSES - 1),
+                )
+            banks[jt, b] = (a_ps, b_ps)
+
+        terms = {}
+
+        def evacuate(jt, b):
+            a_ps, b_ps = banks[jt, b]
+            a_dealt = a_ps[:].rearrange("j (p t) -> j t p", t=PACK)
+            b_dealt = b_ps[:].rearrange("j (p t) -> j t p", t=PACK)
+            a_pos = ring.tile([P, PACK, P], F32, name="a_pos")
+            a_abs = ring.tile([P, PACK, P], F32, name="a_abs")
+            b_neg = ring.tile([P, PACK, P], F32, name="b_neg")
+            b_abs = ring.tile([P, PACK, P], F32, name="b_abs")
+            nc.scalar.activation(a_pos[:], a_dealt, ACT.Copy)
+            nc.scalar.activation(a_abs[:], a_dealt, ACT.Abs)
+            nc.scalar.activation(b_neg[:], b_dealt, ACT.Copy, scale=-1.0)
+            nc.scalar.activation(b_abs[:], b_dealt, ACT.Abs)
+            terms[jt, b] = (a_pos, a_abs, b_neg, b_abs)
+
+        def turn(jt, b):
+            a_pos, a_abs, b_neg, b_abs = terms[jt, b]
+            diff = psum.tile([P, PACK, JT], F32, name="diff", bufs=3)
+            total = psum.tile([P, PACK, JT], F32, name="total", bufs=3)
+            for acc, first, second in ((diff, a_pos, b_neg), (total, a_abs, b_abs)):
+                for t in range(PACK):
+                    nc.tensor.matmul(acc[:, t, :], first[:, t, :], ident[:], start=True, stop=False, is_transpose=True)
+                    nc.tensor.matmul(acc[:, t, :], second[:, t, :], ident[:], start=False, stop=True, is_transpose=True)
+            sums[jt, b] = (diff, total)
+
+        def contrast(jt, b):
+            diff, total = sums[jt, b]
+            root = ring.tile([P, PACK, JT], F32, name="root", bufs=4)
+            nc.scalar.activation(root[:], total[:], ACT.Abs_reciprocal_sqrt, bias=half[:])
+            part = ring.tile([P, PACK, JT], F32, name="part")
+            for t in range(PACK):
+                nc.vector.scalar_tensor_tensor(
+                    part[:, t, :], diff[:, t, :], gains[:, b, t : t + 1], root[:, t, :], ALU.mult, ALU.mult
+                )
+            h = ring.tile([P, JT, PACK], BF16, name="h", align_bytes=64)
+            nc.vector.tensor_tensor(
+                h[:].rearrange("p (c e) t -> p c t e", e=2),
+                part[:].rearrange("p t (c e) -> p c t e", e=2),
+                root[:].rearrange("p t (c e) -> p c t e", e=2),
+                ALU.mult,
+            )
+            codes = ring.tile([P, JT], U32, name="h_codes", align_bytes=64, bufs=6)
+            plane = ring.tile([P, JT], U8, name="h_plane", align_bytes=64, bufs=6)
+            nc.vector.quantize_mx(
+                out=codes[:].bitcast(E4M3), scales=plane[:], in_=h[:].rearrange("p j t -> p (j t)")
+            )
+            h_codes[jt, b], h_plane[jt, b] = codes, plane
+
+        def second_stage(jt, d_ps):
+            for t in range(PACK):
+                for b in range(PASSES):
+                    cols = slice(N * b + P * t, N * b + P * (t + 1))
+                    nc.tensor.matmul_mx(
+                        out=d_ps[:, t, :],
+                        lhsT=w3[:, cols].bitcast(E4M3),
+                        lhsT_scale=w3_plane[:, cols],
+                        rhs=h_codes[jt, b][:].bitcast(E4M3),
+                        rhs_scale=h_plane[jt, b][:],
+                        start=(b == 0),
+                        stop=(b == PASSES - 1),
+                    )
+            d = ring.tile([P, PACK, JT], F32, name="d", bufs=3)
+            nc.scalar.copy(d[:], d_ps[:])
+            cols = slice(jt * JT // 16, (jt + 1) * JT // 16)
+            for t in range(PACK):
+                nc.vector.tensor_tensor(
+                    pages[t][:].indirect(places[:, cols]),
+                    d[:, t, :],
+                    factor[:, t, jt * JT : (jt + 1) * JT],
+                    ALU.mult,
+                )
+
+        steps = [(0, 0), (1, 0), (0, 1), (1, 1)] + [(jt, b) for jt in range(2, S // JT) for b in range(PASSES)]
+        follows = {3: 0, 5: 1}
+        for jt in range(2, S // JT - 1):
+            follows[2 * jt + 3] = jt
+        products(*steps[0])
+        for i, step in enumerate(steps):
+            if i == 1:
+                quantise_w2(0, 1, nc.vector.tensor_copy)
+                quantise_w2(1, 1, nc.vector.tensor_copy)
+            if i == 3:
+                deal_w3()
+            evacuate(*step)
+            if i + 1 < len(steps):
+                products(*steps[i + 1])
+            turn(*step)
+            if i >= 1:
+                contrast(*steps[i - 1])
+                if i - 1 in follows:
+                    second_stage(follows[i - 1], sums[steps[i - 1]][1])
+        contrast(*steps[-1])
+        second_stage(follows[len(steps) - 1], sums[steps[-1]][1])
+        second_stage(steps[-1][0], psum.tile([P, PACK, JT], F32, name="total", bufs=3))
+
+        out_rows = out_0.rearrange("(p t) m -> p t m", t=PACK)
+        for t in range(PACK):
+            nc.vector.tensor_tensor(y[:, t, :], pages[t][:], y[:, t, :], ALU.max)
+            nc.sync.dma_start(out=out_rows[:, t, :], in_=y[:, t, :])
+        y_codes = keep.tile([P, S], U32, name="y_codes", align_bytes=64)
+        y_plane = keep.tile([P, S], U8, name="y_plane", align_bytes=64)
+        out_words = out_1[0].rearrange("p m t -> p (m t)").bitcast(I32)
+        for c in range(S // YCH):
+            cols = slice(c * YCH, (c + 1) * YCH)
+            grouped = ring.tile([P, YCH, PACK], BF16, name="y_grouped", align_bytes=64, bufs=4)
+            dst = grouped[:].rearrange("p (c e) t -> p c t e", e=2)
+            src = y[:, :, cols].rearrange("p t (c e) -> p c t e", e=2)
+            if c % 2 == 0:
+                nc.scalar.copy(dst, src)
+            else:
+                nc.vector.tensor_copy(dst, src)
+            nc.vector.quantize_mx(
+                out=y_codes[:, cols].bitcast(E4M3),
+                scales=y_plane[:, cols],
+                in_=grouped[:].rearrange("p m t -> p (m t)"),
+            )
+            nc.sync.dma_start(out=out_words[:, cols], in_=y_codes[:, cols].bitcast(I32))
+        for q in range(QUADS):
+            queue = nc.scalar if q % 2 else nc.sync
+            queue.dma_start(
+                out=out_2[0, 4 * q : 4 * q + 4, :].bitcast(I32),
+                in_=y_plane[32 * q : 32 * q + 4, :].bitcast(I32),
+            )

@@ -23,8 +23,19 @@ KP = P * PACK
 PASSES = 2
 QUADS = 4
 JT = 128
-GATHER = 256
+GATHERS = ((0, 256), (256, 512), (512, 1024))
 YCH = 256
+LAG = 2
+SIDES = ("a", "b")
+TAIL = 1
+FIRST = 2
+
+
+def load_scale_pass(queue, plane, scales):
+    for q in range(QUADS):
+        queue.dma_start(
+            out=plane[32 * q : 32 * q + 4, :].bitcast(I32), in_=scales[4 * q : 4 * q + 4, :].bitcast(I32)
+        )
 
 
 def load_scales(queue, plane, scales):
@@ -47,11 +58,12 @@ def tile_list_loom_contrast_kernel(
 
         picks = keep.tile([P, S // 16], U16, name="picks")
         places = keep.tile([P, S // 16], U16, name="places")
-        tab_plane = keep.tile([P, PASSES * T], U8, name="tab_plane", align_bytes=64)
+        tab_plane = [keep.tile([P, T], U8, name="tab_plane%d" % a, align_bytes=64) for a in range(PASSES)]
         w1_plane = keep.tile([P, PASSES * H], U8, name="w1_plane", align_bytes=64)
         w3_plane_raw = keep.tile([P, PASSES * N], U8, name="w3_plane_raw", align_bytes=64)
-        nc.vector.memset(tab_plane[:].bitcast(I32), 0)
-        nc.gpsimd.memset(w1_plane[:].bitcast(I32), 0)
+        for a in range(PASSES):
+            nc.vector.memset(tab_plane[a][:].bitcast(I32), 0)
+        nc.vector.memset(w1_plane[:].bitcast(I32), 0)
         nc.gpsimd.memset(w3_plane_raw[:].bitcast(I32), 0)
         half = keep.tile([P, 1], F32, name="half")
         nc.gpsimd.memset(half[:], 0.5)
@@ -63,13 +75,13 @@ def tile_list_loom_contrast_kernel(
         tab = [keep.tile([P, T], I32, name="tab%d" % a, align_bytes=64) for a in range(PASSES)]
         w2_raw = {}
 
-        def load_w2(a, b):
-            raw = keep.tile([P, PACK, KP], F32, name="w2_raw%d%d" % (a, b))
+        def load_w2(a, b, lo=0, hi=KP):
+            raw = keep.tile([P, PACK, hi - lo], F32, name="w2_raw%d%d%d" % (a, b, lo))
             nc.sync.dma_start(
                 out=raw[:],
-                in_=w2[KP * a : KP * (a + 1), KP * b : KP * (b + 1)].rearrange("(p i) c -> p i c", i=PACK),
+                in_=w2[KP * a : KP * (a + 1), KP * b + lo : KP * b + hi].rearrange("(p i) c -> p i c", i=PACK),
             )
-            w2_raw[a, b] = raw
+            w2_raw.setdefault((a, b), []).append((lo, hi, raw))
 
         def load_tab(a):
             nc.sync.dma_start(
@@ -77,10 +89,16 @@ def tile_list_loom_contrast_kernel(
             )
 
         nc.sync.dma_start(picks[:], offs)
-        load_scales(nc.sync, tab_plane, tab_scales)
-        load_w2(0, 0)
+        nc.sync.dma_start(places[:], offs2)
+        gains = keep.tile([P, PASSES, PACK], F32, name="gains")
+        nc.sync.dma_start(out=gains[:], in_=gain.rearrange("(b p t) -> p b t", b=PASSES, t=PACK))
+        load_w2(0, 0, 0, KP // 2)
+        load_scale_pass(nc.sync, tab_plane[0], tab_scales[0])
+        load_w2(0, 0, KP // 2, KP)
+        load_w2(1, 0, 0, KP // 2)
+        load_scale_pass(nc.sync, tab_plane[1], tab_scales[1])
+        load_w2(1, 0, KP // 2, KP)
         load_tab(0)
-        load_w2(1, 0)
         load_tab(1)
         load_scales(nc.sync, w1_plane, w1_scales)
         w1 = keep.tile([P, PASSES * 2 * H], U8, name="w1", align_bytes=64)
@@ -88,17 +106,15 @@ def tile_list_loom_contrast_kernel(
             out=w1[:].bitcast(I32).rearrange("p (a c) -> p a c", a=PASSES),
             in_=w1_words.bitcast(I32).rearrange("a p c -> p a c"),
         )
-        gains = keep.tile([P, PASSES, PACK], F32, name="gains")
-        nc.sync.dma_start(out=gains[:], in_=gain.rearrange("(b p t) -> p b t", b=PASSES, t=PACK))
         load_w2(0, 1)
-        load_w2(1, 1)
+        load_w2(1, 1, 0, KP // 2)
+        load_w2(1, 1, KP // 2, KP)
         w3_raw = keep.tile([P, PASSES * N], I32, name="w3_raw", align_bytes=64)
         nc.sync.dma_start(
             out=w3_raw[:].rearrange("p (a c) -> p a c", a=PASSES),
             in_=w3_words.rearrange("a p c i -> p a (c i)").bitcast(I32),
         )
         load_scales(nc.sync, w3_plane_raw, w3_scales)
-        nc.sync.dma_start(places[:], offs2)
         factor = keep.tile([P, PACK, S], F32, name="factor")
         for q in range(QUADS):
             nc.sync.dma_start(
@@ -113,17 +129,18 @@ def tile_list_loom_contrast_kernel(
         v_plane = []
         for a in range(PASSES):
             plane = keep.tile([P, S], U8, name="v_plane%d" % a, align_bytes=64)
-            nc.vector.tensor_copy(plane[:], tab_plane[:, T * a : T * (a + 1)].indirect(picks[:]))
+            nc.vector.tensor_copy(plane[:], tab_plane[a][:].indirect(picks[:]))
             v_plane.append(plane)
 
         w2_codes, w2_plane = {}, {}
 
         def quantise_w2(a, b, cast):
             grouped = ring.tile([P, KP, PACK], BF16, name="w2_grouped", align_bytes=64)
-            cast(
-                grouped[:].rearrange("p (c e) i -> p c i e", e=2),
-                w2_raw[a, b][:].rearrange("p i (c e) -> p c i e", e=2),
-            )
+            for lo, hi, raw in w2_raw[a, b]:
+                cast(
+                    grouped[:, lo:hi, :].rearrange("p (c e) i -> p c i e", e=2),
+                    raw[:].rearrange("p i (c e) -> p c i e", e=2),
+                )
             codes = keep.tile([P, KP], U32, name="w2_codes%d%d" % (a, b), align_bytes=64)
             plane = keep.tile([P, KP], U8, name="w2_plane%d%d" % (a, b), align_bytes=64)
             nc.vector.quantize_mx(
@@ -134,13 +151,16 @@ def tile_list_loom_contrast_kernel(
 
         v_words = {}
 
+        def gather_words(a, lo, hi):
+            words = ring.tile([P, hi - lo], U32, name="v_words%d" % a, align_bytes=64)
+            nc.vector.tensor_copy(words[:], tab[a][:].bitcast(U32).indirect(picks[:, lo // 16 : hi // 16]))
+            for j in range(lo, hi, JT):
+                v_words[a, j // JT] = words[:, j - lo : j - lo + JT]
+
         for a in range(PASSES):
             quantise_w2(a, 0, nc.scalar.copy)
-            for g in range(S // GATHER):
-                cols = slice(g * GATHER // 16, (g + 1) * GATHER // 16)
-                words = keep.tile([P, GATHER], U32, name="v_words%d%d" % (a, g), align_bytes=64)
-                nc.vector.tensor_copy(words[:], tab[a][:].bitcast(U32).indirect(picks[:, cols]))
-                v_words[a, g] = words
+            for lo, hi in GATHERS[:2]:
+                gather_words(a, lo, hi)
 
         w3 = keep.tile([P, PASSES * N], I32, name="w3", align_bytes=64)
         w3_plane = keep.tile([P, PASSES * N], U8, name="w3_plane", align_bytes=64)
@@ -161,57 +181,49 @@ def tile_list_loom_contrast_kernel(
 
         banks = {}
 
-        def products(jt, b):
-            g, lo = divmod(jt * JT, GATHER)
-            a_ps = psum.tile([P, KP], F32, name="a_ps")
-            b_ps = psum.tile([P, KP], F32, name="b_ps")
+        def product(side, jt, b):
+            bank = psum.tile([P, KP], F32, name=side + "_ps")
             for a in range(PASSES):
+                if side == "a":
+                    rhs = w1[:, 2 * (H * a + KP * b) : 2 * (H * a + KP * (b + 1))].bitcast(E2M1)
+                    rhs_scale = w1_plane[:, H * a + KP * b : H * a + KP * (b + 1)]
+                else:
+                    rhs = w2_codes[a, b][:].bitcast(E4M3)
+                    rhs_scale = w2_plane[a, b][:]
                 nc.tensor.matmul_mx(
-                    out=a_ps[:],
-                    lhsT=v_words[a, g][:, lo : lo + JT].bitcast(E4M3),
+                    out=bank[:],
+                    lhsT=v_words[a, jt].bitcast(E4M3),
                     lhsT_scale=v_plane[a][:, jt * JT : (jt + 1) * JT],
-                    rhs=w1[:, 2 * (H * a + KP * b) : 2 * (H * a + KP * (b + 1))].bitcast(E2M1),
-                    rhs_scale=w1_plane[:, H * a + KP * b : H * a + KP * (b + 1)],
+                    rhs=rhs,
+                    rhs_scale=rhs_scale,
                     start=(a == 0),
                     stop=(a == PASSES - 1),
                 )
-            for a in range(PASSES):
-                nc.tensor.matmul_mx(
-                    out=b_ps[:],
-                    lhsT=v_words[a, g][:, lo : lo + JT].bitcast(E4M3),
-                    lhsT_scale=v_plane[a][:, jt * JT : (jt + 1) * JT],
-                    rhs=w2_codes[a, b][:].bitcast(E4M3),
-                    rhs_scale=w2_plane[a, b][:],
-                    start=(a == 0),
-                    stop=(a == PASSES - 1),
-                )
-            banks[jt, b] = (a_ps, b_ps)
+            banks[side, jt, b] = bank
 
-        terms = {}
+        def evacuate(side, jt, b):
+            dealt = banks[side, jt, b][:].rearrange("j (p t) -> j t p", t=PACK)
+            signed = ring.tile([P, PACK, P], F32, name=side + "_signed")
+            size = ring.tile([P, PACK, P], F32, name=side + "_size")
+            nc.scalar.activation(signed[:], dealt, ACT.Copy, scale=1.0 if side == SIDES[0] else -1.0)
+            nc.scalar.activation(size[:], dealt, ACT.Abs)
+            return signed, size
 
-        def evacuate(jt, b):
-            a_ps, b_ps = banks[jt, b]
-            a_dealt = a_ps[:].rearrange("j (p t) -> j t p", t=PACK)
-            b_dealt = b_ps[:].rearrange("j (p t) -> j t p", t=PACK)
-            a_pos = ring.tile([P, PACK, P], F32, name="a_pos")
-            a_abs = ring.tile([P, PACK, P], F32, name="a_abs")
-            b_neg = ring.tile([P, PACK, P], F32, name="b_neg")
-            b_abs = ring.tile([P, PACK, P], F32, name="b_abs")
-            nc.scalar.activation(a_pos[:], a_dealt, ACT.Copy)
-            nc.scalar.activation(a_abs[:], a_dealt, ACT.Abs)
-            nc.scalar.activation(b_neg[:], b_dealt, ACT.Copy, scale=-1.0)
-            nc.scalar.activation(b_abs[:], b_dealt, ACT.Abs)
-            terms[jt, b] = (a_pos, a_abs, b_neg, b_abs)
-
-        def turn(jt, b):
-            a_pos, a_abs, b_neg, b_abs = terms[jt, b]
-            diff = psum.tile([P, PACK, JT], F32, name="diff", bufs=3)
-            total = psum.tile([P, PACK, JT], F32, name="total", bufs=3)
-            for acc, first, second in ((diff, a_pos, b_neg), (total, a_abs, b_abs)):
+        def turn(side, jt, b, addends):
+            if side == SIDES[0]:
+                diff = psum.tile([P, PACK, JT], F32, name="diff", bufs=3)
+                total = psum.tile([P, PACK, JT], F32, name="total", bufs=3)
+                sums[jt, b] = (diff, total)
+            for acc, addend in zip(sums[jt, b], addends):
                 for t in range(PACK):
-                    nc.tensor.matmul(acc[:, t, :], first[:, t, :], ident[:], start=True, stop=False, is_transpose=True)
-                    nc.tensor.matmul(acc[:, t, :], second[:, t, :], ident[:], start=False, stop=True, is_transpose=True)
-            sums[jt, b] = (diff, total)
+                    nc.tensor.matmul(
+                        acc[:, t, :], addend[:, t, :], ident[:],
+                        start=(side == SIDES[0] and t == 0),
+                        stop=(side == SIDES[1] and t == PACK - 1),
+                        is_transpose=True,
+                    )
+
+        h_tiles = {}
 
         def contrast(jt, b):
             diff, total = sums[jt, b]
@@ -222,37 +234,43 @@ def tile_list_loom_contrast_kernel(
                 nc.vector.scalar_tensor_tensor(
                     part[:, t, :], diff[:, t, :], gains[:, b, t : t + 1], root[:, t, :], ALU.mult, ALU.mult
                 )
-            h = ring.tile([P, JT, PACK], BF16, name="h", align_bytes=64)
+            if b == 0:
+                h_tiles[jt] = ring.tile([P, PASSES, JT, PACK], BF16, name="h", align_bytes=64, bufs=4)
+            h = h_tiles[jt]
             nc.vector.tensor_tensor(
-                h[:].rearrange("p (c e) t -> p c t e", e=2),
+                h[:, b].rearrange("p (c e) t -> p c t e", e=2),
                 part[:].rearrange("p t (c e) -> p c t e", e=2),
                 root[:].rearrange("p t (c e) -> p c t e", e=2),
                 ALU.mult,
             )
-            codes = ring.tile([P, JT], U32, name="h_codes", align_bytes=64, bufs=6)
-            plane = ring.tile([P, JT], U8, name="h_plane", align_bytes=64, bufs=6)
-            nc.vector.quantize_mx(
-                out=codes[:].bitcast(E4M3), scales=plane[:], in_=h[:].rearrange("p j t -> p (j t)")
-            )
-            h_codes[jt, b], h_plane[jt, b] = codes, plane
+            if b == PASSES - 1:
+                codes = ring.tile([P, PASSES * JT], U32, name="h_codes", align_bytes=64, bufs=3)
+                plane = ring.tile([P, PASSES * JT], U8, name="h_plane", align_bytes=64, bufs=3)
+                nc.vector.quantize_mx(
+                    out=codes[:].bitcast(E4M3), scales=plane[:], in_=h[:].rearrange("p b j t -> p (b j t)")
+                )
+                h_codes[jt], h_plane[jt] = codes, plane
 
-        def second_stage(jt, d_ps):
-            for t in range(PACK):
+        def second_stage(jt, slots, d_ps):
+            for t in slots:
                 for b in range(PASSES):
                     cols = slice(N * b + P * t, N * b + P * (t + 1))
                     nc.tensor.matmul_mx(
                         out=d_ps[:, t, :],
                         lhsT=w3[:, cols].bitcast(E4M3),
                         lhsT_scale=w3_plane[:, cols],
-                        rhs=h_codes[jt, b][:].bitcast(E4M3),
-                        rhs_scale=h_plane[jt, b][:],
+                        rhs=h_codes[jt][:, JT * b : JT * (b + 1)].bitcast(E4M3),
+                        rhs_scale=h_plane[jt][:, JT * b : JT * (b + 1)],
                         start=(b == 0),
                         stop=(b == PASSES - 1),
                     )
-            d = ring.tile([P, PACK, JT], F32, name="d", bufs=3)
-            nc.scalar.copy(d[:], d_ps[:])
+            d = ring.tile([P, PACK, JT], F32, name="d", bufs=4)
+            nc.scalar.copy(d[:, slots[0] : slots[-1] + 1, :], d_ps[:, slots[0] : slots[-1] + 1, :])
+            return d
+
+        def put_back(jt, slots, d):
             cols = slice(jt * JT // 16, (jt + 1) * JT // 16)
-            for t in range(PACK):
+            for t in slots:
                 nc.vector.tensor_tensor(
                     pages[t][:].indirect(places[:, cols]),
                     d[:, t, :],
@@ -260,28 +278,46 @@ def tile_list_loom_contrast_kernel(
                     ALU.mult,
                 )
 
-        steps = [(0, 0), (1, 0), (0, 1), (1, 1)] + [(jt, b) for jt in range(2, S // JT) for b in range(PASSES)]
-        follows = {3: 0, 5: 1}
-        for jt in range(2, S // JT - 1):
-            follows[2 * jt + 3] = jt
-        products(*steps[0])
-        for i, step in enumerate(steps):
-            if i == 1:
+        steps = [(jt, b) for b in range(PASSES) for jt in range(FIRST)]
+        steps += [(jt, b) for jt in range(FIRST, S // JT) for b in range(PASSES)]
+        follows = {FIRST + jt: (jt, range(PACK)) for jt in range(FIRST)}
+        for jt in range(FIRST, S // JT):
+            follows[2 * jt + LAG] = (jt, range(0, 2))
+            follows[2 * jt + LAG + 1] = (jt, range(2, 4))
+        waiting = []
+        for side in SIDES:
+            product(side, *steps[0])
+        for i in range(max(follows) + 2):
+            if i == FIRST - 1:
                 quantise_w2(0, 1, nc.vector.tensor_copy)
                 quantise_w2(1, 1, nc.vector.tensor_copy)
-            if i == 3:
+            if i == FIRST:
                 deal_w3()
-            evacuate(*step)
-            if i + 1 < len(steps):
-                products(*steps[i + 1])
-            turn(*step)
-            if i >= 1:
+            if i == FIRST + 1:
+                for a in range(PASSES):
+                    gather_words(a, *GATHERS[2])
+            if 1 <= i <= len(steps):
                 contrast(*steps[i - 1])
-                if i - 1 in follows:
-                    second_stage(follows[i - 1], sums[steps[i - 1]][1])
-        contrast(*steps[-1])
-        second_stage(follows[len(steps) - 1], sums[steps[-1]][1])
-        second_stage(steps[-1][0], psum.tile([P, PACK, JT], F32, name="total", bufs=3))
+            if i < len(steps):
+                for side in SIDES:
+                    addends = evacuate(side, *steps[i])
+                    if i + 1 < len(steps):
+                        product(side, *steps[i + 1])
+                    turn(side, *steps[i], addends)
+            for item in waiting:
+                put_back(*item)
+            waiting = []
+            if i - 1 in follows:
+                jt, slots = follows[i - 1]
+                if i - 1 < len(steps) - TAIL:
+                    bank = sums[steps[i - 1]][1]
+                elif i - 1 == len(steps) - TAIL:
+                    bank = sums[steps[-1]][0]
+                else:
+                    bank = psum.tile([P, PACK, JT], F32, name="total", bufs=3)
+                waiting = [(jt, slots, second_stage(jt, slots, bank))]
+        for item in waiting:
+            put_back(*item)
 
         out_rows = out_0.rearrange("(p t) m -> p t m", t=PACK)
         for t in range(PACK):

@@ -23,11 +23,23 @@ KP = P * PACK
 PASSES = 2
 QUADS = 4
 JT = 128
-GATHERS = ((0, 256), (256, 512), (512, 1024))
+GATHERS = ((0, 256), (256, 1024))
 YCH = 256
 LAG = 2
 SIDES = ("a", "b")
 TAIL = 1
+ORDER = "sABt0CDuv1EFGwH"
+CAST = "ssssvvvv"
+MERGE = ()
+WIDE = ()
+RB = 3
+CRIT = ()
+GB = 2
+LATER = {}
+DB = 3
+TB = 3
+XV = (5,9,13)
+YS = "svsv"
 FIRST = 2
 
 
@@ -61,12 +73,12 @@ def tile_list_loom_contrast_kernel(
         tab_plane = [keep.tile([P, T], U8, name="tab_plane%d" % a, align_bytes=64) for a in range(PASSES)]
         w1_plane = keep.tile([P, PASSES * H], U8, name="w1_plane", align_bytes=64)
         w3_plane_raw = keep.tile([P, PASSES * N], U8, name="w3_plane_raw", align_bytes=64)
-        for a in range(PASSES):
-            nc.vector.memset(tab_plane[a][:].bitcast(I32), 0)
+        half = keep.tile([P, 1], F32, name="half")
+        nc.vector.memset(half[:], 0.5)
+        nc.gpsimd.memset(tab_plane[0][:].bitcast(I32), 0)
+        nc.vector.memset(tab_plane[1][:].bitcast(I32), 0)
         nc.vector.memset(w1_plane[:].bitcast(I32), 0)
         nc.gpsimd.memset(w3_plane_raw[:].bitcast(I32), 0)
-        half = keep.tile([P, 1], F32, name="half")
-        nc.gpsimd.memset(half[:], 0.5)
         ident = keep.tile([P, P], F32, name="ident")
         make_identity(nc, ident[:])
         warm = keep.tile([P, 1], F32, name="warm")
@@ -92,23 +104,28 @@ def tile_list_loom_contrast_kernel(
         nc.sync.dma_start(places[:], offs2)
         gains = keep.tile([P, PASSES, PACK], F32, name="gains")
         nc.sync.dma_start(out=gains[:], in_=gain.rearrange("(b p t) -> p b t", b=PASSES, t=PACK))
-        load_w2(0, 0, 0, KP // 2)
-        load_scale_pass(nc.sync, tab_plane[0], tab_scales[0])
-        load_w2(0, 0, KP // 2, KP)
-        load_w2(1, 0, 0, KP // 2)
-        load_scale_pass(nc.sync, tab_plane[1], tab_scales[1])
-        load_w2(1, 0, KP // 2, KP)
-        load_tab(0)
-        load_tab(1)
-        load_scales(nc.sync, w1_plane, w1_scales)
-        w1 = keep.tile([P, PASSES * 2 * H], U8, name="w1", align_bytes=64)
-        nc.sync.dma_start(
-            out=w1[:].bitcast(I32).rearrange("p (a c) -> p a c", a=PASSES),
-            in_=w1_words.bitcast(I32).rearrange("a p c -> p a c"),
-        )
-        load_w2(0, 1)
-        load_w2(1, 1, 0, KP // 2)
-        load_w2(1, 1, KP // 2, KP)
+        w1 = [keep.tile([P, PASSES * 2 * KP], U8, name="w1_%d" % b, align_bytes=64) for b in range(PASSES)]
+
+        def load_w1(b):
+            nc.sync.dma_start(
+                out=w1[b][:].bitcast(I32).rearrange("p (a c) -> p a c", a=PASSES),
+                in_=w1_words[:, :, 2 * KP * b : 2 * KP * (b + 1)].bitcast(I32).rearrange("a p c -> p a c"),
+            )
+
+        HALF = KP // 2
+        todo = {
+            "A": lambda: load_w2(0, 0, 0, HALF), "B": lambda: load_w2(0, 0, HALF, KP),
+            "C": lambda: load_w2(1, 0, 0, HALF), "D": lambda: load_w2(1, 0, HALF, KP),
+            "E": lambda: load_w2(0, 1, 0, HALF), "F": lambda: load_w2(0, 1, HALF, KP),
+            "G": lambda: load_w2(1, 1, 0, HALF), "H": lambda: load_w2(1, 1, HALF, KP),
+            "s": lambda: load_scale_pass(nc.sync, tab_plane[0], tab_scales[0]),
+            "t": lambda: load_scale_pass(nc.sync, tab_plane[1], tab_scales[1]),
+            "u": lambda: load_scales(nc.sync, w1_plane, w1_scales),
+            "0": lambda: load_tab(0), "1": lambda: load_tab(1),
+            "v": lambda: load_w1(0), "w": lambda: load_w1(1),
+        }
+        for letter in ORDER:
+            todo[letter]()
         w3_raw = keep.tile([P, PASSES * N], I32, name="w3_raw", align_bytes=64)
         nc.sync.dma_start(
             out=w3_raw[:].rearrange("p (a c) -> p a c", a=PASSES),
@@ -134,9 +151,10 @@ def tile_list_loom_contrast_kernel(
 
         w2_codes, w2_plane = {}, {}
 
-        def quantise_w2(a, b, cast):
-            grouped = ring.tile([P, KP, PACK], BF16, name="w2_grouped", align_bytes=64)
+        def quantise_w2(a, b):
+            grouped = ring.tile([P, KP, PACK], BF16, name="w2_grouped", align_bytes=64, bufs=3)
             for lo, hi, raw in w2_raw[a, b]:
+                cast = nc.scalar.copy if CAST[4 * b + 2 * a + lo // HALF] == "s" else nc.vector.tensor_copy
                 cast(
                     grouped[:, lo:hi, :].rearrange("p (c e) i -> p c i e", e=2),
                     raw[:].rearrange("p i (c e) -> p c i e", e=2),
@@ -152,14 +170,14 @@ def tile_list_loom_contrast_kernel(
         v_words = {}
 
         def gather_words(a, lo, hi):
-            words = ring.tile([P, hi - lo], U32, name="v_words%d" % a, align_bytes=64)
+            words = ring.tile([P, hi - lo], U32, name="v_words%d" % a, align_bytes=64, bufs=GB)
             nc.vector.tensor_copy(words[:], tab[a][:].bitcast(U32).indirect(picks[:, lo // 16 : hi // 16]))
             for j in range(lo, hi, JT):
                 v_words[a, j // JT] = words[:, j - lo : j - lo + JT]
 
         for a in range(PASSES):
-            quantise_w2(a, 0, nc.scalar.copy)
-            for lo, hi in GATHERS[:2]:
+            quantise_w2(a, 0)
+            for lo, hi in GATHERS[:GB]:
                 gather_words(a, lo, hi)
 
         w3 = keep.tile([P, PASSES * N], I32, name="w3", align_bytes=64)
@@ -185,7 +203,7 @@ def tile_list_loom_contrast_kernel(
             bank = psum.tile([P, KP], F32, name=side + "_ps")
             for a in range(PASSES):
                 if side == "a":
-                    rhs = w1[:, 2 * (H * a + KP * b) : 2 * (H * a + KP * (b + 1))].bitcast(E2M1)
+                    rhs = w1[b][:, 2 * KP * a : 2 * KP * (a + 1)].bitcast(E2M1)
                     rhs_scale = w1_plane[:, H * a + KP * b : H * a + KP * (b + 1)]
                 else:
                     rhs = w2_codes[a, b][:].bitcast(E4M3)
@@ -211,8 +229,8 @@ def tile_list_loom_contrast_kernel(
 
         def turn(side, jt, b, addends):
             if side == SIDES[0]:
-                diff = psum.tile([P, PACK, JT], F32, name="diff", bufs=3)
-                total = psum.tile([P, PACK, JT], F32, name="total", bufs=3)
+                diff = psum.tile([P, PACK, JT], F32, name="diff", bufs=DB)
+                total = psum.tile([P, PACK, JT], F32, name="total", bufs=TB)
                 sums[jt, b] = (diff, total)
             for acc, addend in zip(sums[jt, b], addends):
                 for t in range(PACK):
@@ -225,24 +243,52 @@ def tile_list_loom_contrast_kernel(
 
         h_tiles = {}
 
-        def contrast(jt, b):
+        pairs = {}
+
+        def contrast(jt, b, on_scalar):
             diff, total = sums[jt, b]
-            root = ring.tile([P, PACK, JT], F32, name="root", bufs=4)
-            nc.scalar.activation(root[:], total[:], ACT.Abs_reciprocal_sqrt, bias=half[:])
-            part = ring.tile([P, PACK, JT], F32, name="part")
-            for t in range(PACK):
-                nc.vector.scalar_tensor_tensor(
-                    part[:, t, :], diff[:, t, :], gains[:, b, t : t + 1], root[:, t, :], ALU.mult, ALU.mult
-                )
+            merged = jt in MERGE
+            if merged:
+                if b == 0:
+                    pairs[jt] = (
+                        ring.tile([P, PACK, PASSES * JT], F32, name="root2", bufs=RB),
+                        ring.tile([P, PACK, PASSES * JT], F32, name="part2", bufs=2),
+                    )
+                root_all, part_all = pairs[jt]
+                root = root_all[:, :, JT * b : JT * (b + 1)]
+                part = part_all[:, :, JT * b : JT * (b + 1)]
+            else:
+                root = ring.tile([P, PACK, JT], F32, name="root", bufs=4)[:]
+                part = ring.tile([P, PACK, JT], F32, name="part")[:]
+            if on_scalar:
+                root0 = ring.tile([P, PACK, JT], F32, name="root0")
+                nc.scalar.activation(root0[:], total[:], ACT.Abs_reciprocal_sqrt, bias=half[:])
+                for t in range(PACK):
+                    nc.scalar.activation(part[:, t, :], diff[:, t, :], ACT.Copy, scale=gains[:, b, t : t + 1])
+                nc.scalar.activation(root, root0[:], ACT.Square)
+            else:
+                nc.scalar.activation(root, total[:], ACT.Abs_reciprocal_sqrt, bias=half[:])
+                for t in range(PACK):
+                    nc.vector.scalar_tensor_tensor(
+                        part[:, t, :], diff[:, t, :], gains[:, b, t : t + 1], root[:, t, :], ALU.mult, ALU.mult
+                    )
             if b == 0:
                 h_tiles[jt] = ring.tile([P, PASSES, JT, PACK], BF16, name="h", align_bytes=64, bufs=4)
             h = h_tiles[jt]
-            nc.vector.tensor_tensor(
-                h[:, b].rearrange("p (c e) t -> p c t e", e=2),
-                part[:].rearrange("p t (c e) -> p c t e", e=2),
-                root[:].rearrange("p t (c e) -> p c t e", e=2),
-                ALU.mult,
-            )
+            if not merged:
+                nc.vector.tensor_tensor(
+                    h[:, b].rearrange("p (c e) t -> p c t e", e=2),
+                    part.rearrange("p t (c e) -> p c t e", e=2),
+                    root.rearrange("p t (c e) -> p c t e", e=2),
+                    ALU.mult,
+                )
+            elif b == PASSES - 1:
+                nc.vector.tensor_tensor(
+                    h[:].rearrange("p b (c e) t -> p (b c) t e", e=2),
+                    part_all[:].rearrange("p t (c e) -> p c t e", e=2),
+                    root_all[:].rearrange("p t (c e) -> p c t e", e=2),
+                    ALU.mult,
+                )
             if b == PASSES - 1:
                 codes = ring.tile([P, PASSES * JT], U32, name="h_codes", align_bytes=64, bufs=3)
                 plane = ring.tile([P, PASSES * JT], U8, name="h_plane", align_bytes=64, bufs=3)
@@ -264,17 +310,31 @@ def tile_list_loom_contrast_kernel(
                         start=(b == 0),
                         stop=(b == PASSES - 1),
                     )
-            d = ring.tile([P, PACK, JT], F32, name="d", bufs=4)
-            nc.scalar.copy(d[:, slots[0] : slots[-1] + 1, :], d_ps[:, slots[0] : slots[-1] + 1, :])
+            rows = slice(slots[0], slots[-1] + 1)
+            if jt in WIDE or jt - 1 in WIDE:
+                if jt in WIDE:
+                    wide[slots[0]] = ring.tile([P, PACK, 2 * JT], F32, name="d_wide", bufs=4)
+                d = wide[slots[0]]
+                lo = 0 if jt in WIDE else JT
+                nc.scalar.copy(d[:, rows, lo : lo + JT], d_ps[:, rows, :])
+            else:
+                d = ring.tile([P, PACK, JT], F32, name="d", bufs=4)
+                nc.scalar.copy(d[:, rows, :], d_ps[:, rows, :])
             return d
 
+        wide = {}
+
         def put_back(jt, slots, d):
-            cols = slice(jt * JT // 16, (jt + 1) * JT // 16)
+            if jt in WIDE:
+                return
+            j0 = (jt - 1 if jt - 1 in WIDE else jt) * JT
+            j1 = (jt + 1) * JT
+            cols = slice(j0 // 16, j1 // 16)
             for t in slots:
                 nc.vector.tensor_tensor(
                     pages[t][:].indirect(places[:, cols]),
                     d[:, t, :],
-                    factor[:, t, jt * JT : (jt + 1) * JT],
+                    factor[:, t, j0:j1],
                     ALU.mult,
                 )
 
@@ -289,21 +349,24 @@ def tile_list_loom_contrast_kernel(
             product(side, *steps[0])
         for i in range(max(follows) + 2):
             if i == FIRST - 1:
-                quantise_w2(0, 1, nc.vector.tensor_copy)
-                quantise_w2(1, 1, nc.vector.tensor_copy)
+                quantise_w2(0, 1)
+                quantise_w2(1, 1)
             if i == FIRST:
                 deal_w3()
-            if i == FIRST + 1:
+            if i in LATER:
                 for a in range(PASSES):
-                    gather_words(a, *GATHERS[2])
+                    gather_words(a, *GATHERS[LATER[i]])
             if 1 <= i <= len(steps):
-                contrast(*steps[i - 1])
+                contrast(*steps[i - 1], i - 1 in XV)
             if i < len(steps):
                 for side in SIDES:
                     addends = evacuate(side, *steps[i])
+                    if i in CRIT:
+                        turn(side, *steps[i], addends)
                     if i + 1 < len(steps):
                         product(side, *steps[i + 1])
-                    turn(side, *steps[i], addends)
+                    if i not in CRIT:
+                        turn(side, *steps[i], addends)
             for item in waiting:
                 put_back(*item)
             waiting = []
@@ -314,7 +377,7 @@ def tile_list_loom_contrast_kernel(
                 elif i - 1 == len(steps) - TAIL:
                     bank = sums[steps[-1]][0]
                 else:
-                    bank = psum.tile([P, PACK, JT], F32, name="total", bufs=3)
+                    bank = psum.tile([P, PACK, JT], F32, name="total", bufs=TB)
                 waiting = [(jt, slots, second_stage(jt, slots, bank))]
         for item in waiting:
             put_back(*item)
@@ -331,7 +394,7 @@ def tile_list_loom_contrast_kernel(
             grouped = ring.tile([P, YCH, PACK], BF16, name="y_grouped", align_bytes=64, bufs=4)
             dst = grouped[:].rearrange("p (c e) t -> p c t e", e=2)
             src = y[:, :, cols].rearrange("p t (c e) -> p c t e", e=2)
-            if c % 2 == 0:
+            if YS[c] == "s":
                 nc.scalar.copy(dst, src)
             else:
                 nc.vector.tensor_copy(dst, src)

@@ -22,40 +22,39 @@ PACK = 4
 KP = P * PACK
 PASSES = 2
 QUADS = 4
+LIST_ROWS = 16
 JT = 128
-GATHERS = ((0, 256), (256, 1024))
-YCH = 256
-LAG = 2
+TILES = S // JT
+HALF = KP // 2
+FIRST_PICKS = 256
+EARLY = 2
+LAG = 3
+GAIN_ON_SCALAR = range(5, PASSES * TILES, 3)
+Y_COLS = 256
 SIDES = ("a", "b")
-TAIL = 1
-ORDER = "sABt0CDuv1EFGwH"
-CAST = "ssssvvvv"
-MERGE = ()
-WIDE = ()
-RB = 3
-CRIT = ()
-GB = 2
-LATER = {}
-DB = 3
-TB = 3
-XV = (5,9,13)
-YS = "svsv"
-FIRST = 2
 
 
-def load_scale_pass(queue, plane, scales):
+def load_plane_pass(nc, plane, scales):
     for q in range(QUADS):
-        queue.dma_start(
+        nc.sync.dma_start(
             out=plane[32 * q : 32 * q + 4, :].bitcast(I32), in_=scales[4 * q : 4 * q + 4, :].bitcast(I32)
         )
 
 
-def load_scales(queue, plane, scales):
+def load_plane(nc, plane, scales):
     for q in range(QUADS):
-        queue.dma_start(
-            out=plane[32 * q : 32 * q + 4, :].bitcast(I32).rearrange("r (a c) -> r a c", a=PASSES),
-            in_=scales[:, 4 * q : 4 * q + 4, :].bitcast(I32).rearrange("a r c -> r a c"),
+        nc.sync.dma_start(
+            out=plane[32 * q : 32 * q + 4, :].bitcast(I32).rearrange("r (g c) -> r g c", g=PASSES),
+            in_=scales[:, 4 * q : 4 * q + 4, :].bitcast(I32).rearrange("g r c -> r g c"),
         )
+
+
+def word_order(ap):
+    return ap.rearrange("p (c e) t -> p c t e", e=2)
+
+
+def slot_order(ap):
+    return ap.rearrange("p t (c e) -> p c t e", e=2)
 
 
 def tile_list_loom_contrast_kernel(
@@ -68,336 +67,268 @@ def tile_list_loom_contrast_kernel(
         ring = ctx.enter_context(tc.tile_pool(name="ring", bufs=2))
         psum = ctx.enter_context(tc.psum_pool(name="psum", bufs=1))
 
-        picks = keep.tile([P, S // 16], U16, name="picks")
-        places = keep.tile([P, S // 16], U16, name="places")
-        tab_plane = [keep.tile([P, T], U8, name="tab_plane%d" % a, align_bytes=64) for a in range(PASSES)]
+        picks = keep.tile([P, S // LIST_ROWS], U16, name="picks")
+        places = keep.tile([P, S // LIST_ROWS], U16, name="places")
+
+        tab_plane = [keep.tile([P, T], U8, name="tab_plane%d" % g, align_bytes=64) for g in range(PASSES)]
         w1_plane = keep.tile([P, PASSES * H], U8, name="w1_plane", align_bytes=64)
         w3_plane_raw = keep.tile([P, PASSES * N], U8, name="w3_plane_raw", align_bytes=64)
-        half = keep.tile([P, 1], F32, name="half")
-        nc.vector.memset(half[:], 0.5)
+        four = keep.tile([P, 1], F32, name="four")
+        nc.vector.memset(four[:], 4.0)
         nc.gpsimd.memset(tab_plane[0][:].bitcast(I32), 0)
         nc.vector.memset(tab_plane[1][:].bitcast(I32), 0)
         nc.vector.memset(w1_plane[:].bitcast(I32), 0)
         nc.gpsimd.memset(w3_plane_raw[:].bitcast(I32), 0)
         ident = keep.tile([P, P], F32, name="ident")
         make_identity(nc, ident[:])
-        warm = keep.tile([P, 1], F32, name="warm")
-        nc.scalar.activation(warm[:], half[:], ACT.Abs_reciprocal_sqrt, bias=half[:])
+        half = keep.tile([P, 1], F32, name="half")
+        nc.scalar.activation(half[:], four[:], ACT.Abs_reciprocal_sqrt)
 
-        tab = [keep.tile([P, T], I32, name="tab%d" % a, align_bytes=64) for a in range(PASSES)]
+        tab = [keep.tile([P, T], I32, name="tab%d" % g, align_bytes=64) for g in range(PASSES)]
+        gains = keep.tile([P, PASSES, PACK], F32, name="gains")
+        w1 = [keep.tile([P, PASSES * 2 * KP], U8, name="w1_%d" % rg, align_bytes=64) for rg in range(PASSES)]
         w2_raw = {}
 
-        def load_w2(a, b, lo=0, hi=KP):
-            raw = keep.tile([P, PACK, hi - lo], F32, name="w2_raw%d%d%d" % (a, b, lo))
+        def load_w2(g, rg, lo):
+            raw = keep.tile([P, PACK, HALF], F32, name="w2_raw%d%d%d" % (g, rg, lo))
             nc.sync.dma_start(
                 out=raw[:],
-                in_=w2[KP * a : KP * (a + 1), KP * b + lo : KP * b + hi].rearrange("(p i) c -> p i c", i=PACK),
+                in_=w2[KP * g : KP * (g + 1), KP * rg + lo : KP * rg + lo + HALF].rearrange("(p i) c -> p i c", i=PACK),
             )
-            w2_raw.setdefault((a, b), []).append((lo, hi, raw))
+            w2_raw[g, rg, lo] = raw
 
-        def load_tab(a):
+        def load_tab(g):
+            nc.sync.dma_start(out=tab[g][:], in_=tab_words[g].rearrange("p t i -> p (t i)").bitcast(I32))
+
+        def load_w1(rg):
             nc.sync.dma_start(
-                out=tab[a][:], in_=tab_words[a].rearrange("p t i -> p (t i)").bitcast(I32)
+                out=w1[rg][:].bitcast(I32).rearrange("p (g c) -> p g c", g=PASSES),
+                in_=w1_words[:, :, 2 * KP * rg : 2 * KP * (rg + 1)].bitcast(I32).rearrange("g p c -> p g c"),
             )
 
         nc.sync.dma_start(picks[:], offs)
         nc.sync.dma_start(places[:], offs2)
-        gains = keep.tile([P, PASSES, PACK], F32, name="gains")
-        nc.sync.dma_start(out=gains[:], in_=gain.rearrange("(b p t) -> p b t", b=PASSES, t=PACK))
-        w1 = [keep.tile([P, PASSES * 2 * KP], U8, name="w1_%d" % b, align_bytes=64) for b in range(PASSES)]
-
-        def load_w1(b):
-            nc.sync.dma_start(
-                out=w1[b][:].bitcast(I32).rearrange("p (a c) -> p a c", a=PASSES),
-                in_=w1_words[:, :, 2 * KP * b : 2 * KP * (b + 1)].bitcast(I32).rearrange("a p c -> p a c"),
-            )
-
-        HALF = KP // 2
-        todo = {
-            "A": lambda: load_w2(0, 0, 0, HALF), "B": lambda: load_w2(0, 0, HALF, KP),
-            "C": lambda: load_w2(1, 0, 0, HALF), "D": lambda: load_w2(1, 0, HALF, KP),
-            "E": lambda: load_w2(0, 1, 0, HALF), "F": lambda: load_w2(0, 1, HALF, KP),
-            "G": lambda: load_w2(1, 1, 0, HALF), "H": lambda: load_w2(1, 1, HALF, KP),
-            "s": lambda: load_scale_pass(nc.sync, tab_plane[0], tab_scales[0]),
-            "t": lambda: load_scale_pass(nc.sync, tab_plane[1], tab_scales[1]),
-            "u": lambda: load_scales(nc.sync, w1_plane, w1_scales),
-            "0": lambda: load_tab(0), "1": lambda: load_tab(1),
-            "v": lambda: load_w1(0), "w": lambda: load_w1(1),
-        }
-        for letter in ORDER:
-            todo[letter]()
+        load_plane_pass(nc, tab_plane[0], tab_scales[0])
+        load_w2(0, 0, 0)
+        load_w2(0, 0, HALF)
+        load_plane_pass(nc, tab_plane[1], tab_scales[1])
+        load_tab(0)
+        load_w2(1, 0, 0)
+        load_w2(1, 0, HALF)
+        load_plane(nc, w1_plane, w1_scales)
+        load_w1(0)
+        load_tab(1)
+        nc.sync.dma_start(out=gains[:], in_=gain.rearrange("(rg p t) -> p rg t", rg=PASSES, t=PACK))
+        load_w2(0, 1, 0)
+        load_w2(0, 1, HALF)
+        load_w2(1, 1, 0)
+        load_w1(1)
+        load_w2(1, 1, HALF)
         w3_raw = keep.tile([P, PASSES * N], I32, name="w3_raw", align_bytes=64)
         nc.sync.dma_start(
-            out=w3_raw[:].rearrange("p (a c) -> p a c", a=PASSES),
-            in_=w3_words.rearrange("a p c i -> p a (c i)").bitcast(I32),
+            out=w3_raw[:].rearrange("p (g c) -> p g c", g=PASSES),
+            in_=w3_words.rearrange("g p c i -> p g (c i)").bitcast(I32),
         )
-        load_scales(nc.sync, w3_plane_raw, w3_scales)
+        load_plane(nc, w3_plane_raw, w3_scales)
         factor = keep.tile([P, PACK, S], F32, name="factor")
         for q in range(QUADS):
-            nc.sync.dma_start(
-                out=factor[32 * q : 32 * (q + 1), :, :],
-                in_=wgo.rearrange("(r t) j -> r t j", t=PACK),
-            )
+            nc.sync.dma_start(out=factor[32 * q : 32 * (q + 1), :, :], in_=wgo.rearrange("(r t) j -> r t j", t=PACK))
         y = keep.tile([P, PACK, S], F32, name="y")
         x0_rows = x0.rearrange("(p t) m -> p t m", t=PACK)
         for t in range(PACK):
             nc.sync.dma_start(out=y[:, t, :], in_=x0_rows[:, t, :])
 
         v_plane = []
-        for a in range(PASSES):
-            plane = keep.tile([P, S], U8, name="v_plane%d" % a, align_bytes=64)
-            nc.vector.tensor_copy(plane[:], tab_plane[a][:].indirect(picks[:]))
+        for g in range(PASSES):
+            plane = keep.tile([P, S], U8, name="v_plane%d" % g, align_bytes=64)
+            nc.vector.tensor_copy(plane[:], tab_plane[g][:].indirect(picks[:]))
             v_plane.append(plane)
 
         w2_codes, w2_plane = {}, {}
 
-        def quantise_w2(a, b):
+        def quantise_w2(g, rg, round_and_group):
             grouped = ring.tile([P, KP, PACK], BF16, name="w2_grouped", align_bytes=64, bufs=3)
-            for lo, hi, raw in w2_raw[a, b]:
-                cast = nc.scalar.copy if CAST[4 * b + 2 * a + lo // HALF] == "s" else nc.vector.tensor_copy
-                cast(
-                    grouped[:, lo:hi, :].rearrange("p (c e) i -> p c i e", e=2),
-                    raw[:].rearrange("p i (c e) -> p c i e", e=2),
-                )
-            codes = keep.tile([P, KP], U32, name="w2_codes%d%d" % (a, b), align_bytes=64)
-            plane = keep.tile([P, KP], U8, name="w2_plane%d%d" % (a, b), align_bytes=64)
+            for lo in (0, HALF):
+                round_and_group(word_order(grouped[:, lo : lo + HALF, :]), slot_order(w2_raw[g, rg, lo][:]))
+            codes = keep.tile([P, KP], U32, name="w2_codes%d%d" % (g, rg), align_bytes=64)
+            plane = keep.tile([P, KP], U8, name="w2_plane%d%d" % (g, rg), align_bytes=64)
             nc.vector.quantize_mx(
                 out=codes[:].bitcast(E4M3), scales=plane[:], in_=grouped[:].rearrange("p c i -> p (c i)")
             )
-            w2_codes[a, b], w2_plane[a, b] = codes, plane
-
+            w2_codes[g, rg], w2_plane[g, rg] = codes, plane
 
         v_words = {}
-
-        def gather_words(a, lo, hi):
-            words = ring.tile([P, hi - lo], U32, name="v_words%d" % a, align_bytes=64, bufs=GB)
-            nc.vector.tensor_copy(words[:], tab[a][:].bitcast(U32).indirect(picks[:, lo // 16 : hi // 16]))
-            for j in range(lo, hi, JT):
-                v_words[a, j // JT] = words[:, j - lo : j - lo + JT]
-
-        for a in range(PASSES):
-            quantise_w2(a, 0)
-            for lo, hi in GATHERS[:GB]:
-                gather_words(a, lo, hi)
+        for g in range(PASSES):
+            quantise_w2(g, 0, nc.scalar.copy)
+            for lo, hi in ((0, FIRST_PICKS), (FIRST_PICKS, S)):
+                words = ring.tile([P, hi - lo], U32, name="v_words%d" % g, align_bytes=64)
+                nc.vector.tensor_copy(
+                    words[:], tab[g][:].bitcast(U32).indirect(picks[:, lo // LIST_ROWS : hi // LIST_ROWS])
+                )
+                for j in range(lo, hi, JT):
+                    v_words[g, j // JT] = words[:, j - lo : j - lo + JT]
 
         w3 = keep.tile([P, PASSES * N], I32, name="w3", align_bytes=64)
         w3_plane = keep.tile([P, PASSES * N], U8, name="w3_plane", align_bytes=64)
 
-        def deal_w3():
-            nc.vector.tensor_copy(
-                w3[:].rearrange("p (a t m) -> p a t m", a=PASSES, t=PACK),
-                w3_raw[:].rearrange("p (a m t) -> p a t m", a=PASSES, t=PACK),
-            )
-            nc.vector.tensor_copy(
-                w3_plane[:].rearrange("p (a t m) -> p a t m", a=PASSES, t=PACK),
-                w3_plane_raw[:].rearrange("p (a m t) -> p a t m", a=PASSES, t=PACK),
-            )
+        def sort_w3():
+            for dst, src in ((w3, w3_raw), (w3_plane, w3_plane_raw)):
+                nc.vector.tensor_copy(
+                    dst[:].rearrange("p (g t m) -> p g t m", g=PASSES, t=PACK),
+                    src[:].rearrange("p (g m t) -> p g t m", g=PASSES, t=PACK),
+                )
 
         pages = [keep.tile([P, S], F32, name="page%d" % t) for t in range(PACK)]
-        sums = {}
-        h_codes, h_plane = {}, {}
+        products, sums, h_tiles, h_codes, h_plane = {}, {}, {}, {}, {}
 
-        banks = {}
-
-        def product(side, jt, b):
-            bank = psum.tile([P, KP], F32, name=side + "_ps")
-            for a in range(PASSES):
+        def multiply(side, jt, rg):
+            bank = psum.tile([P, KP], F32, name=side + "_bank")
+            for g in range(PASSES):
                 if side == "a":
-                    rhs = w1[b][:, 2 * KP * a : 2 * KP * (a + 1)].bitcast(E2M1)
-                    rhs_scale = w1_plane[:, H * a + KP * b : H * a + KP * (b + 1)]
+                    rhs = w1[rg][:, 2 * KP * g : 2 * KP * (g + 1)].bitcast(E2M1)
+                    rhs_scale = w1_plane[:, H * g + KP * rg : H * g + KP * (rg + 1)]
                 else:
-                    rhs = w2_codes[a, b][:].bitcast(E4M3)
-                    rhs_scale = w2_plane[a, b][:]
+                    rhs = w2_codes[g, rg][:].bitcast(E4M3)
+                    rhs_scale = w2_plane[g, rg][:]
                 nc.tensor.matmul_mx(
                     out=bank[:],
-                    lhsT=v_words[a, jt].bitcast(E4M3),
-                    lhsT_scale=v_plane[a][:, jt * JT : (jt + 1) * JT],
+                    lhsT=v_words[g, jt].bitcast(E4M3),
+                    lhsT_scale=v_plane[g][:, jt * JT : (jt + 1) * JT],
                     rhs=rhs,
                     rhs_scale=rhs_scale,
-                    start=(a == 0),
-                    stop=(a == PASSES - 1),
+                    start=(g == 0),
+                    stop=(g == PASSES - 1),
                 )
-            banks[side, jt, b] = bank
+            products[side, jt, rg] = bank
 
-        def evacuate(side, jt, b):
-            dealt = banks[side, jt, b][:].rearrange("j (p t) -> j t p", t=PACK)
+        def copy_out(side, jt, rg):
+            by_slot = products[side, jt, rg][:].rearrange("j (p t) -> j t p", t=PACK)
             signed = ring.tile([P, PACK, P], F32, name=side + "_signed")
             size = ring.tile([P, PACK, P], F32, name=side + "_size")
-            nc.scalar.activation(signed[:], dealt, ACT.Copy, scale=1.0 if side == SIDES[0] else -1.0)
-            nc.scalar.activation(size[:], dealt, ACT.Abs)
+            nc.scalar.activation(signed[:], by_slot, ACT.Copy, scale=1.0 if side == "a" else -1.0)
+            nc.scalar.activation(size[:], by_slot, ACT.Abs)
             return signed, size
 
-        def turn(side, jt, b, addends):
-            if side == SIDES[0]:
-                diff = psum.tile([P, PACK, JT], F32, name="diff", bufs=DB)
-                total = psum.tile([P, PACK, JT], F32, name="total", bufs=TB)
-                sums[jt, b] = (diff, total)
-            for acc, addend in zip(sums[jt, b], addends):
+        def turn(side, jt, rg, signed, size):
+            if side == "a":
+                diff = psum.tile([P, PACK, JT], F32, name="diff", bufs=3)
+                total = psum.tile([P, PACK, JT], F32, name="total", bufs=3)
+                sums[jt, rg] = (diff, total)
+            diff, total = sums[jt, rg]
+            for bank, addend in ((total, size), (diff, signed)):
                 for t in range(PACK):
                     nc.tensor.matmul(
-                        acc[:, t, :], addend[:, t, :], ident[:],
-                        start=(side == SIDES[0] and t == 0),
-                        stop=(side == SIDES[1] and t == PACK - 1),
+                        bank[:, t, :], addend[:, t, :], ident[:],
+                        start=(side == "a" and t == 0),
+                        stop=(side == "b" and t == PACK - 1),
                         is_transpose=True,
                     )
 
-        h_tiles = {}
-
-        pairs = {}
-
-        def contrast(jt, b, on_scalar):
-            diff, total = sums[jt, b]
-            merged = jt in MERGE
-            if merged:
-                if b == 0:
-                    pairs[jt] = (
-                        ring.tile([P, PACK, PASSES * JT], F32, name="root2", bufs=RB),
-                        ring.tile([P, PACK, PASSES * JT], F32, name="part2", bufs=2),
-                    )
-                root_all, part_all = pairs[jt]
-                root = root_all[:, :, JT * b : JT * (b + 1)]
-                part = part_all[:, :, JT * b : JT * (b + 1)]
-            else:
-                root = ring.tile([P, PACK, JT], F32, name="root", bufs=4)[:]
-                part = ring.tile([P, PACK, JT], F32, name="part")[:]
-            if on_scalar:
-                root0 = ring.tile([P, PACK, JT], F32, name="root0")
-                nc.scalar.activation(root0[:], total[:], ACT.Abs_reciprocal_sqrt, bias=half[:])
+        def contrast(jt, rg, gain_on_scalar):
+            diff, total = sums[jt, rg]
+            right = ring.tile([P, PACK, JT], F32, name="right", bufs=4)
+            left = ring.tile([P, PACK, JT], F32, name="left")
+            if gain_on_scalar:
+                root = ring.tile([P, PACK, JT], F32, name="root")
+                nc.scalar.activation(root[:], total[:], ACT.Abs_reciprocal_sqrt, bias=half[:])
                 for t in range(PACK):
-                    nc.scalar.activation(part[:, t, :], diff[:, t, :], ACT.Copy, scale=gains[:, b, t : t + 1])
-                nc.scalar.activation(root, root0[:], ACT.Square)
+                    nc.scalar.activation(left[:, t, :], diff[:, t, :], ACT.Copy, scale=gains[:, rg, t : t + 1])
+                nc.scalar.activation(right[:], root[:], ACT.Square)
             else:
-                nc.scalar.activation(root, total[:], ACT.Abs_reciprocal_sqrt, bias=half[:])
+                nc.scalar.activation(right[:], total[:], ACT.Abs_reciprocal_sqrt, bias=half[:])
                 for t in range(PACK):
                     nc.vector.scalar_tensor_tensor(
-                        part[:, t, :], diff[:, t, :], gains[:, b, t : t + 1], root[:, t, :], ALU.mult, ALU.mult
+                        left[:, t, :], diff[:, t, :], gains[:, rg, t : t + 1], right[:, t, :], ALU.mult, ALU.mult
                     )
-            if b == 0:
+            if rg == 0:
                 h_tiles[jt] = ring.tile([P, PASSES, JT, PACK], BF16, name="h", align_bytes=64, bufs=4)
             h = h_tiles[jt]
-            if not merged:
-                nc.vector.tensor_tensor(
-                    h[:, b].rearrange("p (c e) t -> p c t e", e=2),
-                    part.rearrange("p t (c e) -> p c t e", e=2),
-                    root.rearrange("p t (c e) -> p c t e", e=2),
-                    ALU.mult,
-                )
-            elif b == PASSES - 1:
-                nc.vector.tensor_tensor(
-                    h[:].rearrange("p b (c e) t -> p (b c) t e", e=2),
-                    part_all[:].rearrange("p t (c e) -> p c t e", e=2),
-                    root_all[:].rearrange("p t (c e) -> p c t e", e=2),
-                    ALU.mult,
-                )
-            if b == PASSES - 1:
+            nc.vector.tensor_tensor(word_order(h[:, rg]), slot_order(left[:]), slot_order(right[:]), ALU.mult)
+            if rg == PASSES - 1:
                 codes = ring.tile([P, PASSES * JT], U32, name="h_codes", align_bytes=64, bufs=3)
                 plane = ring.tile([P, PASSES * JT], U8, name="h_plane", align_bytes=64, bufs=3)
                 nc.vector.quantize_mx(
-                    out=codes[:].bitcast(E4M3), scales=plane[:], in_=h[:].rearrange("p b j t -> p (b j t)")
+                    out=codes[:].bitcast(E4M3), scales=plane[:], in_=h[:].rearrange("p g j t -> p (g j t)")
                 )
                 h_codes[jt], h_plane[jt] = codes, plane
 
-        def second_stage(jt, slots, d_ps):
+        def mix(jt, slots, bank):
             for t in slots:
-                for b in range(PASSES):
-                    cols = slice(N * b + P * t, N * b + P * (t + 1))
+                for g in range(PASSES):
+                    cols = slice(N * g + P * t, N * g + P * (t + 1))
                     nc.tensor.matmul_mx(
-                        out=d_ps[:, t, :],
+                        out=bank[:, t, :],
                         lhsT=w3[:, cols].bitcast(E4M3),
                         lhsT_scale=w3_plane[:, cols],
-                        rhs=h_codes[jt][:, JT * b : JT * (b + 1)].bitcast(E4M3),
-                        rhs_scale=h_plane[jt][:, JT * b : JT * (b + 1)],
-                        start=(b == 0),
-                        stop=(b == PASSES - 1),
+                        rhs=h_codes[jt][:, JT * g : JT * (g + 1)].bitcast(E4M3),
+                        rhs_scale=h_plane[jt][:, JT * g : JT * (g + 1)],
+                        start=(g == 0),
+                        stop=(g == PASSES - 1),
                     )
             rows = slice(slots[0], slots[-1] + 1)
-            if jt in WIDE or jt - 1 in WIDE:
-                if jt in WIDE:
-                    wide[slots[0]] = ring.tile([P, PACK, 2 * JT], F32, name="d_wide", bufs=4)
-                d = wide[slots[0]]
-                lo = 0 if jt in WIDE else JT
-                nc.scalar.copy(d[:, rows, lo : lo + JT], d_ps[:, rows, :])
-            else:
-                d = ring.tile([P, PACK, JT], F32, name="d", bufs=4)
-                nc.scalar.copy(d[:, rows, :], d_ps[:, rows, :])
+            d = ring.tile([P, PACK, JT], F32, name="d", bufs=4)
+            nc.scalar.copy(d[:, rows, :], bank[:, rows, :])
             return d
 
-        wide = {}
-
         def put_back(jt, slots, d):
-            if jt in WIDE:
-                return
-            j0 = (jt - 1 if jt - 1 in WIDE else jt) * JT
-            j1 = (jt + 1) * JT
-            cols = slice(j0 // 16, j1 // 16)
+            cols = slice(jt * JT // LIST_ROWS, (jt + 1) * JT // LIST_ROWS)
             for t in slots:
                 nc.vector.tensor_tensor(
-                    pages[t][:].indirect(places[:, cols]),
-                    d[:, t, :],
-                    factor[:, t, j0:j1],
-                    ALU.mult,
+                    pages[t][:].indirect(places[:, cols]), d[:, t, :], factor[:, t, jt * JT : (jt + 1) * JT], ALU.mult
                 )
 
-        steps = [(jt, b) for b in range(PASSES) for jt in range(FIRST)]
-        steps += [(jt, b) for jt in range(FIRST, S // JT) for b in range(PASSES)]
-        follows = {FIRST + jt: (jt, range(PACK)) for jt in range(FIRST)}
-        for jt in range(FIRST, S // JT):
-            follows[2 * jt + LAG] = (jt, range(0, 2))
-            follows[2 * jt + LAG + 1] = (jt, range(2, 4))
-        waiting = []
+        steps = [(jt, rg) for rg in range(PASSES) for jt in range(EARLY)]
+        steps += [(jt, rg) for jt in range(EARLY, TILES) for rg in range(PASSES)]
+        mixes = {}
+        for jt in range(TILES):
+            mixes[PASSES * jt + LAG] = (jt, range(0, PACK // 2))
+            mixes[PASSES * jt + LAG + 1] = (jt, range(PACK // 2, PACK))
+
+        def mix_bank(i):
+            if i < len(steps):
+                return sums[steps[i]][1]
+            if i == len(steps):
+                return sums[steps[-1]][0]
+            return psum.tile([P, PACK, JT], F32, name="total", bufs=3)
+
         for side in SIDES:
-            product(side, *steps[0])
-        for i in range(max(follows) + 2):
-            if i == FIRST - 1:
-                quantise_w2(0, 1)
-                quantise_w2(1, 1)
-            if i == FIRST:
-                deal_w3()
-            if i in LATER:
-                for a in range(PASSES):
-                    gather_words(a, *GATHERS[LATER[i]])
+            multiply(side, *steps[0])
+        ready = None
+        for i in range(max(mixes) + 2):
+            if i == EARLY - 1:
+                for g in range(PASSES):
+                    quantise_w2(g, 1, nc.vector.tensor_copy)
+            if i == EARLY:
+                sort_w3()
             if 1 <= i <= len(steps):
-                contrast(*steps[i - 1], i - 1 in XV)
+                contrast(*steps[i - 1], i - 1 in GAIN_ON_SCALAR)
             if i < len(steps):
                 for side in SIDES:
-                    addends = evacuate(side, *steps[i])
-                    if i in CRIT:
-                        turn(side, *steps[i], addends)
+                    signed, size = copy_out(side, *steps[i])
                     if i + 1 < len(steps):
-                        product(side, *steps[i + 1])
-                    if i not in CRIT:
-                        turn(side, *steps[i], addends)
-            for item in waiting:
-                put_back(*item)
-            waiting = []
-            if i - 1 in follows:
-                jt, slots = follows[i - 1]
-                if i - 1 < len(steps) - TAIL:
-                    bank = sums[steps[i - 1]][1]
-                elif i - 1 == len(steps) - TAIL:
-                    bank = sums[steps[-1]][0]
-                else:
-                    bank = psum.tile([P, PACK, JT], F32, name="total", bufs=TB)
-                waiting = [(jt, slots, second_stage(jt, slots, bank))]
-        for item in waiting:
-            put_back(*item)
+                        multiply(side, *steps[i + 1])
+                    turn(side, *steps[i], signed, size)
+            if ready:
+                put_back(*ready)
+            ready = None
+            if i - 1 in mixes:
+                jt, slots = mixes[i - 1]
+                ready = (jt, slots, mix(jt, slots, mix_bank(i - 1)))
+        put_back(*ready)
 
         out_rows = out_0.rearrange("(p t) m -> p t m", t=PACK)
         for t in range(PACK):
             nc.vector.tensor_tensor(y[:, t, :], pages[t][:], y[:, t, :], ALU.max)
             nc.sync.dma_start(out=out_rows[:, t, :], in_=y[:, t, :])
+
         y_codes = keep.tile([P, S], U32, name="y_codes", align_bytes=64)
         y_plane = keep.tile([P, S], U8, name="y_plane", align_bytes=64)
         out_words = out_1[0].rearrange("p m t -> p (m t)").bitcast(I32)
-        for c in range(S // YCH):
-            cols = slice(c * YCH, (c + 1) * YCH)
-            grouped = ring.tile([P, YCH, PACK], BF16, name="y_grouped", align_bytes=64, bufs=4)
-            dst = grouped[:].rearrange("p (c e) t -> p c t e", e=2)
-            src = y[:, :, cols].rearrange("p t (c e) -> p c t e", e=2)
-            if YS[c] == "s":
-                nc.scalar.copy(dst, src)
-            else:
-                nc.vector.tensor_copy(dst, src)
+        for piece in range(S // Y_COLS):
+            cols = slice(piece * Y_COLS, (piece + 1) * Y_COLS)
+            grouped = ring.tile([P, Y_COLS, PACK], BF16, name="y_grouped", align_bytes=64, bufs=S // Y_COLS)
+            round_and_group = nc.vector.tensor_copy if piece % 2 else nc.scalar.copy
+            round_and_group(word_order(grouped[:]), slot_order(y[:, :, cols]))
             nc.vector.quantize_mx(
                 out=y_codes[:, cols].bitcast(E4M3),
                 scales=y_plane[:, cols],
@@ -407,6 +338,5 @@ def tile_list_loom_contrast_kernel(
         for q in range(QUADS):
             queue = nc.scalar if q % 2 else nc.sync
             queue.dma_start(
-                out=out_2[0, 4 * q : 4 * q + 4, :].bitcast(I32),
-                in_=y_plane[32 * q : 32 * q + 4, :].bitcast(I32),
+                out=out_2[0, 4 * q : 4 * q + 4, :].bitcast(I32), in_=y_plane[32 * q : 32 * q + 4, :].bitcast(I32)
             )

@@ -29,23 +29,18 @@ HALF = KP // 2
 FIRST_PICKS = 256
 EARLY = 2
 LAG = 3
-GAIN_ON_SCALAR = range(5, PASSES * TILES, 3)
+GAIN_ON_SCALAR = range(15, PASSES * TILES, 2)
+SPARE = 4
+LEAD = 2
 Y_COLS = 256
 SIDES = ("a", "b")
 
 
-def load_plane_pass(nc, plane, scales):
-    for q in range(QUADS):
-        nc.sync.dma_start(
-            out=plane[32 * q : 32 * q + 4, :].bitcast(I32), in_=scales[4 * q : 4 * q + 4, :].bitcast(I32)
-        )
-
-
 def load_plane(nc, plane, scales):
-    for q in range(QUADS):
+    for r in range(4):
         nc.sync.dma_start(
-            out=plane[32 * q : 32 * q + 4, :].bitcast(I32).rearrange("r (g c) -> r g c", g=PASSES),
-            in_=scales[:, 4 * q : 4 * q + 4, :].bitcast(I32).rearrange("g r c -> r g c"),
+            out=plane[r:P:32, :].bitcast(I32).rearrange("q (g c) -> q g c", g=PASSES),
+            in_=scales[:, r:16:4, :].bitcast(I32).rearrange("g q c -> q g c"),
         )
 
 
@@ -70,13 +65,13 @@ def tile_list_loom_contrast_kernel(
         picks = keep.tile([P, S // LIST_ROWS], U16, name="picks")
         places = keep.tile([P, S // LIST_ROWS], U16, name="places")
 
-        tab_plane = [keep.tile([P, T], U8, name="tab_plane%d" % g, align_bytes=64) for g in range(PASSES)]
+        tab_plane = keep.tile([P, PASSES * T], U8, name="tab_plane", align_bytes=64)
         w1_plane = keep.tile([P, PASSES * H], U8, name="w1_plane", align_bytes=64)
-        w3_plane_raw = keep.tile([P, PASSES * N], U8, name="w3_plane_raw", align_bytes=64)
+        w3_plane_raw = keep.tile([P, N], U8, name="w3_plane_raw", align_bytes=64)
         four = keep.tile([P, 1], F32, name="four")
         nc.vector.memset(four[:], 4.0)
-        nc.gpsimd.memset(tab_plane[0][:].bitcast(I32), 0)
-        nc.vector.memset(tab_plane[1][:].bitcast(I32), 0)
+        nc.gpsimd.memset(tab_plane[:, :T].bitcast(I32), 0)
+        nc.vector.memset(tab_plane[:, T:].bitcast(I32), 0)
         nc.vector.memset(w1_plane[:].bitcast(I32), 0)
         nc.gpsimd.memset(w3_plane_raw[:].bitcast(I32), 0)
         ident = keep.tile([P, P], F32, name="ident")
@@ -108,48 +103,63 @@ def tile_list_loom_contrast_kernel(
 
         nc.sync.dma_start(picks[:], offs)
         nc.sync.dma_start(places[:], offs2)
-        load_plane_pass(nc, tab_plane[0], tab_scales[0])
+        load_plane(nc, tab_plane, tab_scales)
         load_w2(0, 0, 0)
         load_w2(0, 0, HALF)
-        load_plane_pass(nc, tab_plane[1], tab_scales[1])
         load_tab(0)
-        load_w2(1, 0, 0)
-        load_w2(1, 0, HALF)
+        load_tab(1)
         load_plane(nc, w1_plane, w1_scales)
         load_w1(0)
-        load_tab(1)
+        load_w2(1, 0, 0)
+        load_w2(1, 0, HALF)
         nc.sync.dma_start(out=gains[:], in_=gain.rearrange("(rg p t) -> p rg t", rg=PASSES, t=PACK))
-        load_w2(0, 1, 0)
-        load_w2(0, 1, HALF)
-        load_w2(1, 1, 0)
+        for g in range(PASSES):
+            for lo in (0, HALF):
+                load_w2(g, 1, lo)
         load_w1(1)
-        load_w2(1, 1, HALF)
         w3_raw = keep.tile([P, PASSES * N], I32, name="w3_raw", align_bytes=64)
         nc.sync.dma_start(
             out=w3_raw[:].rearrange("p (g c) -> p g c", g=PASSES),
             in_=w3_words.rearrange("g p c i -> p g (c i)").bitcast(I32),
         )
-        load_plane(nc, w3_plane_raw, w3_scales)
-        factor = keep.tile([P, PACK, S], F32, name="factor")
         for q in range(QUADS):
-            nc.sync.dma_start(out=factor[32 * q : 32 * (q + 1), :, :], in_=wgo.rearrange("(r t) j -> r t j", t=PACK))
-        y = keep.tile([P, PACK, S], F32, name="y")
+            nc.sync.dma_start(
+                out=w3_plane_raw[32 * q : 32 * q + 4 * PASSES, :].bitcast(I32),
+                in_=w3_scales[:, 4 * q : 4 * q + 4, :].bitcast(I32),
+            )
+        wgo_rows = wgo.rearrange("(r t) j -> r t j", t=PACK)
+        factor = []
+        for u in range(2):
+            factor.append(keep.tile([P, PACK, S // 2], F32, name="factor%d" % u))
+            for q in (0, 2, 1, 3):
+                nc.sync.dma_start(
+                    out=factor[u][32 * q : 32 * (q + 1), :, :], in_=wgo_rows[:, :, u * S // 2 : (u + 1) * S // 2]
+                )
         x0_rows = x0.rearrange("(p t) m -> p t m", t=PACK)
-        for t in range(PACK):
-            nc.sync.dma_start(out=y[:, t, :], in_=x0_rows[:, t, :])
+        y = []
+        for piece in range(S // Y_COLS):
+            y.append(keep.tile([P, PACK, Y_COLS], F32, name="y%d" % piece))
+            nc.sync.dma_start(out=y[piece][:], in_=x0_rows[:, :, piece * Y_COLS : (piece + 1) * Y_COLS])
 
         v_plane = []
         for g in range(PASSES):
             plane = keep.tile([P, S], U8, name="v_plane%d" % g, align_bytes=64)
-            nc.vector.tensor_copy(plane[:], tab_plane[g][:].indirect(picks[:]))
+            nc.vector.tensor_copy(plane[:], tab_plane[:, g * T : (g + 1) * T].indirect(picks[:]))
             v_plane.append(plane)
 
         w2_codes, w2_plane = {}, {}
 
-        def quantise_w2(g, rg, round_and_group):
-            grouped = ring.tile([P, KP, PACK], BF16, name="w2_grouped", align_bytes=64, bufs=3)
-            for lo in (0, HALF):
-                round_and_group(word_order(grouped[:, lo : lo + HALF, :]), slot_order(w2_raw[g, rg, lo][:]))
+        w2_grouped = {}
+
+        def round_w2(g, rg, lo, copy):
+            if lo == 0:
+                w2_grouped[g, rg] = keep.tile(
+                    [P, KP, PACK], BF16, name="w2_grouped%d%d" % (g, rg), tag="stage%d" % g, align_bytes=64
+                )
+            copy(word_order(w2_grouped[g, rg][:, lo : lo + HALF, :]), slot_order(w2_raw[g, rg, lo][:]))
+
+        def quantise_w2(g, rg):
+            grouped = w2_grouped[g, rg]
             codes = keep.tile([P, KP], U32, name="w2_codes%d%d" % (g, rg), align_bytes=64)
             plane = keep.tile([P, KP], U8, name="w2_plane%d%d" % (g, rg), align_bytes=64)
             nc.vector.quantize_mx(
@@ -158,31 +168,55 @@ def tile_list_loom_contrast_kernel(
             w2_codes[g, rg], w2_plane[g, rg] = codes, plane
 
         v_words = {}
-        for g in range(PASSES):
-            quantise_w2(g, 0, nc.scalar.copy)
-            for lo, hi in ((0, FIRST_PICKS), (FIRST_PICKS, S)):
-                words = ring.tile([P, hi - lo], U32, name="v_words%d" % g, align_bytes=64)
+
+        def gather_words(lo, hi):
+            words = keep.tile([P, PASSES, hi - lo], U32, name="v_words%d" % lo, align_bytes=64)
+            for g in range(PASSES):
                 nc.vector.tensor_copy(
-                    words[:], tab[g][:].bitcast(U32).indirect(picks[:, lo // LIST_ROWS : hi // LIST_ROWS])
+                    words[:, g, :], tab[g][:].bitcast(U32).indirect(picks[:, lo // LIST_ROWS : hi // LIST_ROWS])
                 )
                 for j in range(lo, hi, JT):
-                    v_words[g, j // JT] = words[:, j - lo : j - lo + JT]
+                    v_words[g, j // JT] = words[:, g, j - lo : j - lo + JT]
+
+        for lo in (0, HALF):
+            round_w2(0, 0, lo, nc.scalar.copy)
+        quantise_w2(0, 0)
+        gather_words(0, FIRST_PICKS)
+        gather_words(FIRST_PICKS, S)
 
         w3 = keep.tile([P, PASSES * N], I32, name="w3", align_bytes=64)
-        w3_plane = keep.tile([P, PASSES * N], U8, name="w3_plane", align_bytes=64)
+        w3_plane = keep.tile([P, N], U8, name="w3_plane", align_bytes=64)
 
         def sort_w3():
-            for dst, src in ((w3, w3_raw), (w3_plane, w3_plane_raw)):
-                nc.vector.tensor_copy(
-                    dst[:].rearrange("p (g t m) -> p g t m", g=PASSES, t=PACK),
-                    src[:].rearrange("p (g m t) -> p g t m", g=PASSES, t=PACK),
-                )
+            nc.vector.tensor_copy(
+                w3[:].rearrange("p (g t m) -> p g t m", g=PASSES, t=PACK),
+                w3_raw[:].rearrange("p (g m t) -> p g t m", g=PASSES, t=PACK),
+            )
+            nc.vector.tensor_copy(
+                w3_plane[:].rearrange("p (t m) -> p t m", t=PACK),
+                w3_plane_raw[:].rearrange("p (m t) -> p t m", t=PACK),
+            )
 
         pages = [keep.tile([P, S], F32, name="page%d" % t) for t in range(PACK)]
-        products, sums, h_tiles, h_codes, h_plane = {}, {}, {}, {}, {}
+        a_bank = psum.tile([P, KP], F32, name="a_bank")
+        b_banks = [psum.tile([P, KP], F32, name="b_bank%d" % u) for u in range(2)]
+        total_banks = [psum.tile([P, KP], F32, name="total%d" % u) for u in range(2)]
+        diff_banks = [psum.tile([P, KP], F32, name="diff%d" % u) for u in range(3)]
+        steps = [(jt, rg) for rg in range(PASSES) for jt in range(EARLY)]
+        steps += [(jt, rg) for jt in range(EARLY, TILES) for rg in range(PASSES)]
+        parts, weights, h_tiles, h_codes, h_plane = {}, {}, {}, {}, {}
 
-        def multiply(side, jt, rg):
-            bank = psum.tile([P, KP], F32, name=side + "_bank")
+        def by_slot(bank):
+            return bank[:].rearrange("p (t j) -> p t j", t=PACK)
+
+        def product_bank(side, i):
+            if side == "b":
+                return b_banks[i % 2]
+            return diff_banks[i + 1] if i < LEAD else a_bank
+
+        def multiply(side, i):
+            jt, rg = steps[i]
+            bank = product_bank(side, i)
             for g in range(PASSES):
                 if side == "a":
                     rhs = w1[rg][:, 2 * KP * g : 2 * KP * (g + 1)].bitcast(E2M1)
@@ -199,51 +233,60 @@ def tile_list_loom_contrast_kernel(
                     start=(g == 0),
                     stop=(g == PASSES - 1),
                 )
-            products[side, jt, rg] = bank
 
-        def copy_out(side, jt, rg):
-            by_slot = products[side, jt, rg][:].rearrange("j (p t) -> j t p", t=PACK)
-            signed = ring.tile([P, PACK, P], F32, name=side + "_signed")
-            size = ring.tile([P, PACK, P], F32, name=side + "_size")
-            nc.scalar.activation(signed[:], by_slot, ACT.Copy, scale=1.0 if side == "a" else -1.0)
-            nc.scalar.activation(size[:], by_slot, ACT.Abs)
-            return signed, size
+        def copy_out(side, i):
+            bank = product_bank(side, i)
+            sorted_view = bank[:].rearrange("j (p t) -> j t p", t=PACK)
+            key = side
+            depth = 2
+            if side == "a" and i == SPARE:
+                side = "spare"
+                depth = 1
+            size = ring.tile([P, PACK, P], F32, name=side + "_size", bufs=depth)
+            signed = ring.tile([P, PACK, P], F32, name=side + "_signed", bufs=depth)
+            nc.scalar.activation(size[:], sorted_view, ACT.Abs)
+            nc.scalar.activation(signed[:], sorted_view, ACT.Copy, scale=-1.0 if side == "b" else 1.0)
+            parts[key, "size", i], parts[key, "signed", i] = size, signed
 
-        def turn(side, jt, rg, signed, size):
-            if side == "a":
-                diff = psum.tile([P, PACK, JT], F32, name="diff", bufs=3)
-                total = psum.tile([P, PACK, JT], F32, name="total", bufs=3)
-                sums[jt, rg] = (diff, total)
-            diff, total = sums[jt, rg]
-            for bank, addend in ((total, size), (diff, signed)):
+        def turn(kind, i):
+            bank = total_banks[i % 2] if kind == "size" else diff_banks[i % 3]
+            for side in reversed(SIDES):
                 for t in range(PACK):
                     nc.tensor.matmul(
-                        bank[:, t, :], addend[:, t, :], ident[:],
-                        start=(side == "a" and t == 0),
-                        stop=(side == "b" and t == PACK - 1),
+                        by_slot(bank)[:, t, :], parts[side, kind, i][:, t, :], ident[:],
+                        start=(side == "b" and t == 0),
+                        stop=(side == "a" and t == PACK - 1),
                         is_transpose=True,
                     )
 
-        def contrast(jt, rg, gain_on_scalar):
-            diff, total = sums[jt, rg]
-            right = ring.tile([P, PACK, JT], F32, name="right", bufs=4)
-            left = ring.tile([P, PACK, JT], F32, name="left")
-            if gain_on_scalar:
-                root = ring.tile([P, PACK, JT], F32, name="root")
-                nc.scalar.activation(root[:], total[:], ACT.Abs_reciprocal_sqrt, bias=half[:])
-                for t in range(PACK):
-                    nc.scalar.activation(left[:, t, :], diff[:, t, :], ACT.Copy, scale=gains[:, rg, t : t + 1])
-                nc.scalar.activation(right[:], root[:], ACT.Square)
+        def weigh(i):
+            rg = steps[i][1]
+            root = ring.tile([P, PACK, JT], F32, name="root", bufs=3)
+            nc.scalar.activation(root[:], by_slot(total_banks[i % 2]), ACT.Abs_reciprocal_sqrt, bias=half[:])
+            if i < last:
+                weight = ring.tile([P, PACK, JT], F32, name="weight", bufs=3)
             else:
-                nc.scalar.activation(right[:], total[:], ACT.Abs_reciprocal_sqrt, bias=half[:])
-                for t in range(PACK):
+                weight = keep.tile([P, PACK, JT], F32, name="last_weight", tag="last")
+            if i in GAIN_ON_SCALAR:
+                square = ring.tile([P, PACK, JT], F32, name="square")
+                nc.scalar.activation(square[:], root[:], ACT.Square)
+            for t in range(PACK):
+                if i in GAIN_ON_SCALAR:
+                    nc.scalar.activation(weight[:, t, :], square[:, t, :], ACT.Copy, scale=gains[:, rg, t : t + 1])
+                else:
                     nc.vector.scalar_tensor_tensor(
-                        left[:, t, :], diff[:, t, :], gains[:, rg, t : t + 1], right[:, t, :], ALU.mult, ALU.mult
+                        weight[:, t, :], root[:, t, :], gains[:, rg, t : t + 1], root[:, t, :], ALU.mult, ALU.mult
                     )
+            weights[i] = weight
+
+        def contrast(i):
+            jt, rg = steps[i]
             if rg == 0:
                 h_tiles[jt] = ring.tile([P, PASSES, JT, PACK], BF16, name="h", align_bytes=64, bufs=4)
             h = h_tiles[jt]
-            nc.vector.tensor_tensor(word_order(h[:, rg]), slot_order(left[:]), slot_order(right[:]), ALU.mult)
+            nc.vector.tensor_tensor(
+                word_order(h[:, rg]), slot_order(by_slot(diff_banks[i % 3])), slot_order(weights[i][:]), ALU.mult
+            )
             if rg == PASSES - 1:
                 codes = ring.tile([P, PASSES * JT], U32, name="h_codes", align_bytes=64, bufs=3)
                 plane = ring.tile([P, PASSES * JT], U8, name="h_plane", align_bytes=64, bufs=3)
@@ -255,88 +298,107 @@ def tile_list_loom_contrast_kernel(
         def mix(jt, slots, bank):
             for t in slots:
                 for g in range(PASSES):
-                    cols = slice(N * g + P * t, N * g + P * (t + 1))
                     nc.tensor.matmul_mx(
-                        out=bank[:, t, :],
-                        lhsT=w3[:, cols].bitcast(E4M3),
-                        lhsT_scale=w3_plane[:, cols],
+                        out=by_slot(bank)[:, t, :],
+                        lhsT=w3[:, N * g + P * t : N * g + P * (t + 1)].bitcast(E4M3),
+                        lhsT_scale=w3_plane[4 * g : P, P * t : P * (t + 1)],
                         rhs=h_codes[jt][:, JT * g : JT * (g + 1)].bitcast(E4M3),
                         rhs_scale=h_plane[jt][:, JT * g : JT * (g + 1)],
                         start=(g == 0),
                         stop=(g == PASSES - 1),
                     )
-            rows = slice(slots[0], slots[-1] + 1)
-            d = ring.tile([P, PACK, JT], F32, name="d", bufs=4)
-            nc.scalar.copy(d[:, rows, :], bank[:, rows, :])
-            return d
 
-        def put_back(jt, slots, d):
+        def put_back(jt, slots, bank, pool=ring, tag="d", bufs=4):
+            rows = slice(slots[0], slots[-1] + 1)
+            d = pool.tile([P, PACK, JT], F32, name="d", tag=tag, bufs=bufs)
+            nc.scalar.copy(d[:, rows, :], by_slot(bank)[:, rows, :])
             cols = slice(jt * JT // LIST_ROWS, (jt + 1) * JT // LIST_ROWS)
             for t in slots:
                 nc.vector.tensor_tensor(
-                    pages[t][:].indirect(places[:, cols]), d[:, t, :], factor[:, t, jt * JT : (jt + 1) * JT], ALU.mult
+                    pages[t][:].indirect(places[:, cols]), d[:, t, :], factor[jt // 4][:, t, jt % 4 * JT : (jt % 4 + 1) * JT], ALU.mult
                 )
 
-        steps = [(jt, rg) for rg in range(PASSES) for jt in range(EARLY)]
-        steps += [(jt, rg) for jt in range(EARLY, TILES) for rg in range(PASSES)]
+        last = len(steps) - 1
         mixes = {}
-        for jt in range(TILES):
-            mixes[PASSES * jt + LAG] = (jt, range(0, PACK // 2))
-            mixes[PASSES * jt + LAG + 1] = (jt, range(PACK // 2, PACK))
+        for jt in range(TILES - 1):
+            for u in range(2):
+                i = PASSES * jt + LAG + u
+                bank = b_banks[i % 2] if i <= last else total_banks[last % 2]
+                mixes[i] = (jt, range(2 * u, 2 * u + 2), bank)
 
-        def mix_bank(i):
-            if i < len(steps):
-                return sums[steps[i]][1]
-            if i == len(steps):
-                return sums[steps[-1]][0]
-            return psum.tile([P, PACK, JT], F32, name="total", bufs=3)
-
-        for side in SIDES:
-            multiply(side, *steps[0])
-        ready = None
-        for i in range(max(mixes) + 2):
-            if i == EARLY - 1:
-                for g in range(PASSES):
-                    quantise_w2(g, 1, nc.vector.tensor_copy)
+        multiply("a", 0)
+        multiply("a", 1)
+        copy_out("a", 0)
+        round_w2(1, 0, 0, nc.vector.tensor_copy)
+        round_w2(1, 0, HALF, nc.vector.tensor_copy)
+        quantise_w2(1, 0)
+        copy_out("a", 1)
+        for g in range(PASSES):
+            for lo in (0, HALF):
+                round_w2(g, 1, lo, nc.vector.tensor_copy)
+            quantise_w2(g, 1)
+        multiply("b", 0)
+        multiply("a", SPARE)
+        copy_out("a", SPARE)
+        multiply("a", LEAD)
+        for i in range(last + 2):
             if i == EARLY:
                 sort_w3()
-            if 1 <= i <= len(steps):
-                contrast(*steps[i - 1], i - 1 in GAIN_ON_SCALAR)
-            if i < len(steps):
-                for side in SIDES:
-                    signed, size = copy_out(side, *steps[i])
-                    if i + 1 < len(steps):
-                        multiply(side, *steps[i + 1])
-                    turn(side, *steps[i], signed, size)
-            if ready:
-                put_back(*ready)
-            ready = None
-            if i - 1 in mixes:
-                jt, slots = mixes[i - 1]
-                ready = (jt, slots, mix(jt, slots, mix_bank(i - 1)))
-        put_back(*ready)
+            if LEAD <= i <= last and i != SPARE:
+                copy_out("a", i)
+            if i >= 1:
+                weigh(i - 1)
+                if i - 1 in mixes:
+                    put_back(*mixes[i - 1])
+                turn("signed", i - 1)
+            if LEAD <= i < last and i + 1 != SPARE:
+                multiply("a", i + 1)
+            if i >= 1:
+                contrast(i - 1)
+            if i <= last:
+                copy_out("b", i)
+                turn("size", i)
+            if i in mixes:
+                mix(*mixes[i])
+            if i + 1 <= last:
+                multiply("b", i + 1)
+        put_back(*mixes[last + 1], keep, "last", 1)
+        free_banks = (a_bank, b_banks[0], b_banks[1], total_banks[0])
+        for t in range(PACK):
+            mix(TILES - 1, [t], free_banks[t])
+        for t in range(PACK):
+            put_back(TILES - 1, [t], free_banks[t])
 
         out_rows = out_0.rearrange("(p t) m -> p t m", t=PACK)
-        for t in range(PACK):
-            nc.vector.tensor_tensor(y[:, t, :], pages[t][:], y[:, t, :], ALU.max)
-            nc.sync.dma_start(out=out_rows[:, t, :], in_=y[:, t, :])
-
         y_codes = keep.tile([P, S], U32, name="y_codes", align_bytes=64)
         y_plane = keep.tile([P, S], U8, name="y_plane", align_bytes=64)
         out_words = out_1[0].rearrange("p m t -> p (m t)").bitcast(I32)
-        for piece in range(S // Y_COLS):
+        pieces = S // Y_COLS
+        grouped = {}
+
+        def larger(piece):
             cols = slice(piece * Y_COLS, (piece + 1) * Y_COLS)
-            grouped = ring.tile([P, Y_COLS, PACK], BF16, name="y_grouped", align_bytes=64, bufs=S // Y_COLS)
-            round_and_group = nc.vector.tensor_copy if piece % 2 else nc.scalar.copy
-            round_and_group(word_order(grouped[:]), slot_order(y[:, :, cols]))
+            for t in range(PACK):
+                nc.vector.tensor_tensor(y[piece][:, t, :], pages[t][:, cols], y[piece][:, t, :], ALU.max)
+            nc.sync.dma_start(out=out_rows[:, :, cols], in_=y[piece][:])
+            grouped[piece] = ring.tile([P, Y_COLS, PACK], BF16, name="y_grouped", align_bytes=64, bufs=pieces)
+            round_and_group = nc.vector.tensor_copy if piece == pieces - 1 else nc.scalar.copy
+            round_and_group(word_order(grouped[piece][:]), slot_order(y[piece][:]))
+
+        def encode(piece):
+            cols = slice(piece * Y_COLS, (piece + 1) * Y_COLS)
             nc.vector.quantize_mx(
                 out=y_codes[:, cols].bitcast(E4M3),
                 scales=y_plane[:, cols],
-                in_=grouped[:].rearrange("p m t -> p (m t)"),
+                in_=grouped[piece][:].rearrange("p m t -> p (m t)"),
             )
             nc.sync.dma_start(out=out_words[:, cols], in_=y_codes[:, cols].bitcast(I32))
-        for q in range(QUADS):
-            queue = nc.scalar if q % 2 else nc.sync
-            queue.dma_start(
-                out=out_2[0, 4 * q : 4 * q + 4, :].bitcast(I32), in_=y_plane[32 * q : 32 * q + 4, :].bitcast(I32)
-            )
+
+        for piece in range(pieces + 2):
+            if piece < pieces:
+                larger(piece)
+            if piece >= 2:
+                encode(piece - 2)
+        for r in range(4):
+            queue = nc.scalar if r % 2 else nc.sync
+            queue.dma_start(out=out_2[0, r:16:4, :].bitcast(I32), in_=y_plane[r:P:32, :].bitcast(I32))

@@ -349,17 +349,23 @@ def tile_list_loom_contrast_kernel(
             if i >= 1:
                 weigh(i - 1)
                 if i - 1 in mixes:
-                    put_back(*mixes[i - 1])
+                    jt, slots, bank = mixes[i - 1]
+                    put_back(jt, slots[:1], bank)
                 turn("signed", i - 1)
+                if i - 1 in mixes:
+                    mix(jt, slots[1:], bank)
             if LEAD <= i < last and i + 1 != SPARE:
                 multiply("a", i + 1)
             if i >= 1:
                 contrast(i - 1)
             if i <= last:
                 copy_out("b", i)
+            if i - 1 in mixes:
+                put_back(jt, slots[1:], bank)
+            if i <= last:
                 turn("size", i)
             if i in mixes:
-                mix(*mixes[i])
+                mix(mixes[i][0], mixes[i][1] if i > last else mixes[i][1][:1], mixes[i][2])
             if i + 1 <= last:
                 multiply("b", i + 1)
         put_back(*mixes[last + 1], keep, "last", 1)

@@ -31,6 +31,7 @@ EARLY = 2
 LAG = 3
 GAIN_ON_SCALAR = range(15, PASSES * TILES, 2)
 SPARE = 4
+FIRST_PAGES = 1
 LEAD = 2
 Y_COLS = 256
 SIDES = ("a", "b")
@@ -372,10 +373,16 @@ def tile_list_loom_contrast_kernel(
         free_banks = (a_bank, b_banks[0], b_banks[1], total_banks[0])
         for t in range(PACK):
             mix(TILES - 1, [t], free_banks[t])
+        out_rows = out_0.rearrange("(p t) m -> p t m", t=PACK)
         for t in range(PACK):
             put_back(TILES - 1, [t], free_banks[t])
+            if t < FIRST_PAGES:
+                for piece in range(S // Y_COLS):
+                    cols = slice(piece * Y_COLS, (piece + 1) * Y_COLS)
+                    nc.vector.tensor_tensor(y[piece][:, t, :], pages[t][:, cols], y[piece][:, t, :], ALU.max)
+                    if t == FIRST_PAGES - 1:
+                        nc.sync.dma_start(out=out_rows[:, :FIRST_PAGES, cols], in_=y[piece][:, :FIRST_PAGES, :])
 
-        out_rows = out_0.rearrange("(p t) m -> p t m", t=PACK)
         y_codes = keep.tile([P, S], U32, name="y_codes", align_bytes=64)
         y_plane = keep.tile([P, S], U8, name="y_plane", align_bytes=64)
         out_words = out_1[0].rearrange("p m t -> p (m t)").bitcast(I32)
@@ -384,9 +391,9 @@ def tile_list_loom_contrast_kernel(
 
         def larger(piece):
             cols = slice(piece * Y_COLS, (piece + 1) * Y_COLS)
-            for t in range(PACK):
+            for t in range(FIRST_PAGES, PACK):
                 nc.vector.tensor_tensor(y[piece][:, t, :], pages[t][:, cols], y[piece][:, t, :], ALU.max)
-            nc.sync.dma_start(out=out_rows[:, :, cols], in_=y[piece][:])
+            nc.sync.dma_start(out=out_rows[:, FIRST_PAGES:, cols], in_=y[piece][:, FIRST_PAGES:, :])
             grouped[piece] = ring.tile([P, Y_COLS, PACK], BF16, name="y_grouped", align_bytes=64, bufs=pieces)
             round_and_group = nc.vector.tensor_copy if piece == pieces - 1 else nc.scalar.copy
             round_and_group(word_order(grouped[piece][:]), slot_order(y[piece][:]))

@@ -113,11 +113,11 @@ def tile_list_loom_contrast_kernel(
         load_w1(0)
         load_w2(1, 0, 0)
         load_w2(1, 0, HALF)
-        nc.sync.dma_start(out=gains[:], in_=gain.rearrange("(rg p t) -> p rg t", rg=PASSES, t=PACK))
-        for g in range(PASSES):
-            for lo in (0, HALF):
-                load_w2(g, 1, lo)
+        load_w2(0, 1, 0)
+        load_w2(0, 1, HALF)
+        load_w2(1, 1, 0)
         load_w1(1)
+        load_w2(1, 1, HALF)
         w3_raw = keep.tile([P, PASSES * N], I32, name="w3_raw", align_bytes=64)
         nc.sync.dma_start(
             out=w3_raw[:].rearrange("p (g c) -> p g c", g=PASSES),
@@ -128,6 +128,7 @@ def tile_list_loom_contrast_kernel(
                 out=w3_plane_raw[32 * q : 32 * q + 4 * PASSES, :].bitcast(I32),
                 in_=w3_scales[:, 4 * q : 4 * q + 4, :].bitcast(I32),
             )
+        nc.sync.dma_start(out=gains[:], in_=gain.rearrange("(rg p t) -> p rg t", rg=PASSES, t=PACK))
         wgo_rows = wgo.rearrange("(r t) j -> r t j", t=PACK)
         factor = []
         for u in range(2):

@@ -28,13 +28,12 @@ TILES = S // JT
 HALF = KP // 2
 FIRST_PICKS = 256
 EARLY = 2
-LAG = 3
-GAIN_ON_SCALAR = range(15, PASSES * TILES, 2)
-SPARE = 4
-FIRST_PAGES = 1
 LEAD = 2
+SPARE = 4
+LAG = 3
+SUB_ON_VECTOR = 1
 Y_COLS = 256
-SIDES = ("a", "b")
+PIECES = S // Y_COLS
 
 
 def load_plane(nc, plane, scales):
@@ -139,7 +138,7 @@ def tile_list_loom_contrast_kernel(
                 )
         x0_rows = x0.rearrange("(p t) m -> p t m", t=PACK)
         y = []
-        for piece in range(S // Y_COLS):
+        for piece in range(PIECES):
             y.append(keep.tile([P, PACK, Y_COLS], F32, name="y%d" % piece))
             nc.sync.dma_start(out=y[piece][:], in_=x0_rows[:, :, piece * Y_COLS : (piece + 1) * Y_COLS])
 
@@ -149,9 +148,7 @@ def tile_list_loom_contrast_kernel(
             nc.vector.tensor_copy(plane[:], tab_plane[:, g * T : (g + 1) * T].indirect(picks[:]))
             v_plane.append(plane)
 
-        w2_codes, w2_plane = {}, {}
-
-        w2_grouped = {}
+        w2_grouped, w2_codes, w2_plane = {}, {}, {}
 
         def round_w2(g, rg, lo, copy):
             if lo == 0:
@@ -171,20 +168,22 @@ def tile_list_loom_contrast_kernel(
 
         v_words = {}
 
-        def gather_words(lo, hi):
-            words = keep.tile([P, PASSES, hi - lo], U32, name="v_words%d" % lo, align_bytes=64)
-            for g in range(PASSES):
-                nc.vector.tensor_copy(
-                    words[:, g, :], tab[g][:].bitcast(U32).indirect(picks[:, lo // LIST_ROWS : hi // LIST_ROWS])
-                )
-                for j in range(lo, hi, JT):
-                    v_words[g, j // JT] = words[:, g, j - lo : j - lo + JT]
+        def gather_words(g, lo, hi, tag=None):
+            name = "v_words%d%d" % (g, lo)
+            words = keep.tile([P, hi - lo], U32, name=name, tag=tag or name, align_bytes=64)
+            nc.vector.tensor_copy(
+                words[:], tab[g][:].bitcast(U32).indirect(picks[:, lo // LIST_ROWS : hi // LIST_ROWS])
+            )
+            for j in range(lo, hi, JT):
+                v_words[g, j // JT] = words[:, j - lo : j - lo + JT]
 
         for lo in (0, HALF):
             round_w2(0, 0, lo, nc.scalar.copy)
         quantise_w2(0, 0)
-        gather_words(0, FIRST_PICKS)
-        gather_words(FIRST_PICKS, S)
+        for g in range(PASSES):
+            gather_words(g, 0, FIRST_PICKS)
+        gather_words(0, FIRST_PICKS, S)
+        gather_words(1, FIRST_PICKS, S // 2)
 
         w3 = keep.tile([P, PASSES * N], I32, name="w3", align_bytes=64)
         w3_plane = keep.tile([P, N], U8, name="w3_plane", align_bytes=64)
@@ -239,25 +238,25 @@ def tile_list_loom_contrast_kernel(
         def copy_out(side, i):
             bank = product_bank(side, i)
             sorted_view = bank[:].rearrange("j (p t) -> j t p", t=PACK)
-            key = side
-            depth = 2
-            if side == "a" and i == SPARE:
-                side = "spare"
-                depth = 1
-            size = ring.tile([P, PACK, P], F32, name=side + "_size", bufs=depth)
-            signed = ring.tile([P, PACK, P], F32, name=side + "_signed", bufs=depth)
+            name, depth = ("spare", 1) if (side, i) == ("a", SPARE) else (side, 2)
+            size = ring.tile([P, PACK, P], F32, name=name + "_size", bufs=depth)
+            signed = ring.tile([P, PACK, P], F32, name=name + "_signed", bufs=depth)
             nc.scalar.activation(size[:], sorted_view, ACT.Abs)
-            nc.scalar.activation(signed[:], sorted_view, ACT.Copy, scale=-1.0 if side == "b" else 1.0)
-            parts[key, "size", i], parts[key, "signed", i] = size, signed
+            if (side, i) == ("b", SUB_ON_VECTOR):
+                nc.vector.tensor_tensor(signed[:], parts["a", "signed", i][:], sorted_view, ALU.subtract)
+            else:
+                nc.scalar.activation(signed[:], sorted_view, ACT.Copy, scale=-1.0 if side == "b" else 1.0)
+            parts[side, "size", i], parts[side, "signed", i] = size, signed
 
         def turn(kind, i):
             bank = total_banks[i % 2] if kind == "size" else diff_banks[i % 3]
-            for side in reversed(SIDES):
+            sides = ("b",) if (kind, i) == ("signed", SUB_ON_VECTOR) else ("b", "a")
+            for side in sides:
                 for t in range(PACK):
                     nc.tensor.matmul(
                         by_slot(bank)[:, t, :], parts[side, kind, i][:, t, :], ident[:],
                         start=(side == "b" and t == 0),
-                        stop=(side == "a" and t == PACK - 1),
+                        stop=(side == sides[-1] and t == PACK - 1),
                         is_transpose=True,
                     )
 
@@ -269,21 +268,17 @@ def tile_list_loom_contrast_kernel(
                 weight = ring.tile([P, PACK, JT], F32, name="weight", bufs=3)
             else:
                 weight = keep.tile([P, PACK, JT], F32, name="last_weight", tag="last")
-            if i in GAIN_ON_SCALAR:
-                square = ring.tile([P, PACK, JT], F32, name="square")
-                nc.scalar.activation(square[:], root[:], ACT.Square)
             for t in range(PACK):
-                if i in GAIN_ON_SCALAR:
-                    nc.scalar.activation(weight[:, t, :], square[:, t, :], ACT.Copy, scale=gains[:, rg, t : t + 1])
-                else:
-                    nc.vector.scalar_tensor_tensor(
-                        weight[:, t, :], root[:, t, :], gains[:, rg, t : t + 1], root[:, t, :], ALU.mult, ALU.mult
-                    )
+                nc.vector.scalar_tensor_tensor(
+                    weight[:, t, :], root[:, t, :], gains[:, rg, t : t + 1], root[:, t, :], ALU.mult, ALU.mult
+                )
             weights[i] = weight
 
         def contrast(i):
             jt, rg = steps[i]
-            if rg == 0:
+            if i == 0:
+                h_tiles[jt] = keep.tile([P, PASSES, JT, PACK], BF16, name="first_h", tag="first_h", align_bytes=64)
+            elif rg == 0:
                 h_tiles[jt] = ring.tile([P, PASSES, JT, PACK], BF16, name="h", align_bytes=64, bufs=4)
             h = h_tiles[jt]
             nc.vector.tensor_tensor(
@@ -296,6 +291,8 @@ def tile_list_loom_contrast_kernel(
                     out=codes[:].bitcast(E4M3), scales=plane[:], in_=h[:].rearrange("p g j t -> p (g j t)")
                 )
                 h_codes[jt], h_plane[jt] = codes, plane
+                if jt == 0:
+                    gather_words(1, S // 2, S, "first_h")
 
         def mix(jt, slots, bank):
             for t in slots:
@@ -316,9 +313,8 @@ def tile_list_loom_contrast_kernel(
             nc.scalar.copy(d[:, rows, :], by_slot(bank)[:, rows, :])
             cols = slice(jt * JT // LIST_ROWS, (jt + 1) * JT // LIST_ROWS)
             for t in slots:
-                nc.vector.tensor_tensor(
-                    pages[t][:].indirect(places[:, cols]), d[:, t, :], factor[jt // 4][:, t, jt % 4 * JT : (jt % 4 + 1) * JT], ALU.mult
-                )
+                wgo_part = factor[jt // 4][:, t, jt % 4 * JT : (jt % 4 + 1) * JT]
+                nc.vector.tensor_tensor(pages[t][:].indirect(places[:, cols]), d[:, t, :], wgo_part, ALU.mult)
 
         last = len(steps) - 1
         mixes = {}
@@ -367,7 +363,8 @@ def tile_list_loom_contrast_kernel(
             if i <= last:
                 turn("size", i)
             if i in mixes:
-                mix(mixes[i][0], mixes[i][1] if i > last else mixes[i][1][:1], mixes[i][2])
+                jt_next, slots_next, bank_next = mixes[i]
+                mix(jt_next, slots_next if i > last else slots_next[:1], bank_next)
             if i + 1 <= last:
                 multiply("b", i + 1)
         put_back(*mixes[last + 1], keep, "last", 1)
@@ -377,26 +374,24 @@ def tile_list_loom_contrast_kernel(
         out_rows = out_0.rearrange("(p t) m -> p t m", t=PACK)
         for t in range(PACK):
             put_back(TILES - 1, [t], free_banks[t])
-            if t < FIRST_PAGES:
-                for piece in range(S // Y_COLS):
+            if t == 0:
+                for piece in range(PIECES):
                     cols = slice(piece * Y_COLS, (piece + 1) * Y_COLS)
-                    nc.vector.tensor_tensor(y[piece][:, t, :], pages[t][:, cols], y[piece][:, t, :], ALU.max)
-                    if t == FIRST_PAGES - 1:
-                        nc.sync.dma_start(out=out_rows[:, :FIRST_PAGES, cols], in_=y[piece][:, :FIRST_PAGES, :])
+                    nc.vector.tensor_tensor(y[piece][:, 0, :], pages[0][:, cols], y[piece][:, 0, :], ALU.max)
+                    nc.sync.dma_start(out=out_rows[:, :1, cols], in_=y[piece][:, :1, :])
 
         y_codes = keep.tile([P, S], U32, name="y_codes", align_bytes=64)
         y_plane = keep.tile([P, S], U8, name="y_plane", align_bytes=64)
         out_words = out_1[0].rearrange("p m t -> p (m t)").bitcast(I32)
-        pieces = S // Y_COLS
         grouped = {}
 
         def larger(piece):
             cols = slice(piece * Y_COLS, (piece + 1) * Y_COLS)
-            for t in range(FIRST_PAGES, PACK):
+            for t in range(1, PACK):
                 nc.vector.tensor_tensor(y[piece][:, t, :], pages[t][:, cols], y[piece][:, t, :], ALU.max)
-            nc.sync.dma_start(out=out_rows[:, FIRST_PAGES:, cols], in_=y[piece][:, FIRST_PAGES:, :])
-            grouped[piece] = ring.tile([P, Y_COLS, PACK], BF16, name="y_grouped", align_bytes=64, bufs=pieces)
-            round_and_group = nc.vector.tensor_copy if piece == pieces - 1 else nc.scalar.copy
+            nc.sync.dma_start(out=out_rows[:, 1:, cols], in_=y[piece][:, 1:, :])
+            grouped[piece] = ring.tile([P, Y_COLS, PACK], BF16, name="y_grouped", align_bytes=64, bufs=PIECES)
+            round_and_group = nc.vector.tensor_copy if piece == PIECES - 1 else nc.scalar.copy
             round_and_group(word_order(grouped[piece][:]), slot_order(y[piece][:]))
 
         def encode(piece):
@@ -408,8 +403,8 @@ def tile_list_loom_contrast_kernel(
             )
             nc.sync.dma_start(out=out_words[:, cols], in_=y_codes[:, cols].bitcast(I32))
 
-        for piece in range(pieces + 2):
-            if piece < pieces:
+        for piece in range(PIECES + 2):
+            if piece < PIECES:
                 larger(piece)
             if piece >= 2:
                 encode(piece - 2)

@@ -26,12 +26,9 @@ LIST_ROWS = 16
 JT = 128
 TILES = S // JT
 HALF = KP // 2
-FIRST_PICKS = 256
-EARLY = 2
-LEAD = 2
-SPARE = 4
-LAG = 3
-SUB_ON_VECTOR = 1
+EARLY = 3
+LEAD = 5
+THREE = (7, 12)
 Y_COLS = 256
 PIECES = S // Y_COLS
 
@@ -84,13 +81,15 @@ def tile_list_loom_contrast_kernel(
         w1 = [keep.tile([P, PASSES * 2 * KP], U8, name="w1_%d" % rg, align_bytes=64) for rg in range(PASSES)]
         w2_raw = {}
 
-        def load_w2(g, rg, lo):
-            raw = keep.tile([P, PACK, HALF], F32, name="w2_raw%d%d%d" % (g, rg, lo))
+        def load_w2(g, rg, lo, width):
+            raw = keep.tile([P, PACK, width], F32, name="w2_raw%d%d%d" % (g, rg, lo), align_bytes=64)
+            first = KP * rg + lo
             nc.sync.dma_start(
                 out=raw[:],
-                in_=w2[KP * g : KP * (g + 1), KP * rg + lo : KP * rg + lo + HALF].rearrange("(p i) c -> p i c", i=PACK),
+                in_=w2[KP * g : KP * (g + 1), first : first + width].rearrange("(p i) c -> p i c", i=PACK),
             )
-            w2_raw[g, rg, lo] = raw
+            for at in range(0, width, HALF):
+                w2_raw[g, rg, lo + at] = raw[:, :, at : at + HALF]
 
         def load_tab(g):
             nc.sync.dma_start(out=tab[g][:], in_=tab_words[g].rearrange("p t i -> p (t i)").bitcast(I32))
@@ -102,21 +101,20 @@ def tile_list_loom_contrast_kernel(
             )
 
         nc.sync.dma_start(picks[:], offs)
+        load_w1(0)
+        nc.sync.dma_start(out=gains[:], in_=gain.rearrange("(rg p t) -> p rg t", rg=PASSES, t=PACK))
         nc.sync.dma_start(places[:], offs2)
         load_plane(nc, tab_plane, tab_scales)
-        load_w2(0, 0, 0)
-        load_w2(0, 0, HALF)
         load_tab(0)
         load_tab(1)
         load_plane(nc, w1_plane, w1_scales)
-        load_w1(0)
-        load_w2(1, 0, 0)
-        load_w2(1, 0, HALF)
-        load_w2(0, 1, 0)
-        load_w2(0, 1, HALF)
-        load_w2(1, 1, 0)
+        load_w2(0, 0, 0, KP)
         load_w1(1)
-        load_w2(1, 1, HALF)
+        load_w2(1, 0, 0, HALF)
+        load_w2(1, 0, HALF, HALF)
+        load_w2(0, 1, 0, KP)
+        load_w2(1, 1, 0, HALF)
+        load_w2(1, 1, HALF, HALF)
         w3_raw = keep.tile([P, PASSES * N], I32, name="w3_raw", align_bytes=64)
         nc.sync.dma_start(
             out=w3_raw[:].rearrange("p (g c) -> p g c", g=PASSES),
@@ -127,26 +125,30 @@ def tile_list_loom_contrast_kernel(
                 out=w3_plane_raw[32 * q : 32 * q + 4 * PASSES, :].bitcast(I32),
                 in_=w3_scales[:, 4 * q : 4 * q + 4, :].bitcast(I32),
             )
-        nc.sync.dma_start(out=gains[:], in_=gain.rearrange("(rg p t) -> p rg t", rg=PASSES, t=PACK))
         wgo_rows = wgo.rearrange("(r t) j -> r t j", t=PACK)
-        factor = []
-        for u in range(2):
-            factor.append(keep.tile([P, PACK, S // 2], F32, name="factor%d" % u))
+        factor = {}
+        for lo, hi in ((0, S // 4), (S // 4, S)):
+            part = keep.tile([P, PACK, hi - lo], F32, name="factor%d" % lo)
             for q in (0, 2, 1, 3):
-                nc.sync.dma_start(
-                    out=factor[u][32 * q : 32 * (q + 1), :, :], in_=wgo_rows[:, :, u * S // 2 : (u + 1) * S // 2]
-                )
+                nc.sync.dma_start(out=part[32 * q : 32 * (q + 1), :, :], in_=wgo_rows[:, :, lo:hi])
+            for j in range(lo, hi, JT):
+                factor[j // JT] = part[:, :, j - lo : j - lo + JT]
         x0_rows = x0.rearrange("(p t) m -> p t m", t=PACK)
         y = []
         for piece in range(PIECES):
             y.append(keep.tile([P, PACK, Y_COLS], F32, name="y%d" % piece))
             nc.sync.dma_start(out=y[piece][:], in_=x0_rows[:, :, piece * Y_COLS : (piece + 1) * Y_COLS])
 
-        v_plane = []
-        for g in range(PASSES):
-            plane = keep.tile([P, S], U8, name="v_plane%d" % g, align_bytes=64)
-            nc.vector.tensor_copy(plane[:], tab_plane[:, g * T : (g + 1) * T].indirect(picks[:]))
-            v_plane.append(plane)
+        v_plane = {}
+
+        def gather_plane(g, lo, hi, tag=None):
+            name = "v_plane%d%d" % (g, lo)
+            plane = keep.tile([P, hi - lo], U8, name=name, tag=tag or name, align_bytes=64)
+            nc.vector.tensor_copy(
+                plane[:], tab_plane[:, g * T : (g + 1) * T].indirect(picks[:, lo // LIST_ROWS : hi // LIST_ROWS])
+            )
+            for j in range(lo, hi, JT):
+                v_plane[g, j // JT] = plane[:, j - lo : j - lo + JT]
 
         w2_grouped, w2_codes, w2_plane = {}, {}, {}
 
@@ -155,7 +157,7 @@ def tile_list_loom_contrast_kernel(
                 w2_grouped[g, rg] = keep.tile(
                     [P, KP, PACK], BF16, name="w2_grouped%d%d" % (g, rg), tag="stage%d" % g, align_bytes=64
                 )
-            copy(word_order(w2_grouped[g, rg][:, lo : lo + HALF, :]), slot_order(w2_raw[g, rg, lo][:]))
+            copy(word_order(w2_grouped[g, rg][:, lo : lo + HALF, :]), slot_order(w2_raw[g, rg, lo]))
 
         def quantise_w2(g, rg):
             grouped = w2_grouped[g, rg]
@@ -177,13 +179,11 @@ def tile_list_loom_contrast_kernel(
             for j in range(lo, hi, JT):
                 v_words[g, j // JT] = words[:, j - lo : j - lo + JT]
 
-        for lo in (0, HALF):
-            round_w2(0, 0, lo, nc.scalar.copy)
-        quantise_w2(0, 0)
-        for g in range(PASSES):
-            gather_words(g, 0, FIRST_PICKS)
-        gather_words(0, FIRST_PICKS, S)
-        gather_words(1, FIRST_PICKS, S // 2)
+        gather_plane(0, 0, S)
+        gather_plane(1, 0, S)
+        gather_words(0, 0, S // 2)
+        gather_words(1, 0, S // 4)
+        gather_words(1, S // 4, S)
 
         w3 = keep.tile([P, PASSES * N], I32, name="w3", align_bytes=64)
         w3_plane = keep.tile([P, N], U8, name="w3_plane", align_bytes=64)
@@ -213,7 +213,10 @@ def tile_list_loom_contrast_kernel(
         def product_bank(side, i):
             if side == "b":
                 return b_banks[i % 2]
-            return diff_banks[i + 1] if i < LEAD else a_bank
+            return (diff_banks + total_banks)[i] if i < LEAD else a_bank
+
+        def total_bank(i):
+            return a_bank if i == EARLY else total_banks[i % 2]
 
         def multiply(side, i):
             jt, rg = steps[i]
@@ -228,7 +231,7 @@ def tile_list_loom_contrast_kernel(
                 nc.tensor.matmul_mx(
                     out=bank[:],
                     lhsT=v_words[g, jt].bitcast(E4M3),
-                    lhsT_scale=v_plane[g][:, jt * JT : (jt + 1) * JT],
+                    lhsT_scale=v_plane[g, jt],
                     rhs=rhs,
                     rhs_scale=rhs_scale,
                     start=(g == 0),
@@ -238,19 +241,16 @@ def tile_list_loom_contrast_kernel(
         def copy_out(side, i):
             bank = product_bank(side, i)
             sorted_view = bank[:].rearrange("j (p t) -> j t p", t=PACK)
-            name, depth = ("spare", 1) if (side, i) == ("a", SPARE) else (side, 2)
-            size = ring.tile([P, PACK, P], F32, name=name + "_size", bufs=depth)
-            signed = ring.tile([P, PACK, P], F32, name=name + "_signed", bufs=depth)
+            depth = LEAD if side == "a" else 2
+            size = ring.tile([P, PACK, P], F32, name=side + "_size", bufs=depth)
+            signed = ring.tile([P, PACK, P], F32, name=side + "_signed", bufs=depth)
             nc.scalar.activation(size[:], sorted_view, ACT.Abs)
-            if (side, i) == ("b", SUB_ON_VECTOR):
-                nc.vector.tensor_tensor(signed[:], parts["a", "signed", i][:], sorted_view, ALU.subtract)
-            else:
-                nc.scalar.activation(signed[:], sorted_view, ACT.Copy, scale=-1.0 if side == "b" else 1.0)
+            nc.scalar.activation(signed[:], sorted_view, ACT.Copy, scale=-1.0 if side == "b" else 1.0)
             parts[side, "size", i], parts[side, "signed", i] = size, signed
 
         def turn(kind, i):
-            bank = total_banks[i % 2] if kind == "size" else diff_banks[i % 3]
-            sides = ("b",) if (kind, i) == ("signed", SUB_ON_VECTOR) else ("b", "a")
+            bank = total_bank(i) if kind == "size" else diff_banks[i % 3]
+            sides = ("b", "a")
             for side in sides:
                 for t in range(PACK):
                     nc.tensor.matmul(
@@ -263,7 +263,7 @@ def tile_list_loom_contrast_kernel(
         def weigh(i):
             rg = steps[i][1]
             root = ring.tile([P, PACK, JT], F32, name="root", bufs=3)
-            nc.scalar.activation(root[:], by_slot(total_banks[i % 2]), ACT.Abs_reciprocal_sqrt, bias=half[:])
+            nc.scalar.activation(root[:], by_slot(total_bank(i)), ACT.Abs_reciprocal_sqrt, bias=half[:])
             if i < last:
                 weight = ring.tile([P, PACK, JT], F32, name="weight", bufs=3)
             else:
@@ -276,9 +276,7 @@ def tile_list_loom_contrast_kernel(
 
         def contrast(i):
             jt, rg = steps[i]
-            if i == 0:
-                h_tiles[jt] = keep.tile([P, PASSES, JT, PACK], BF16, name="first_h", tag="first_h", align_bytes=64)
-            elif rg == 0:
+            if rg == 0:
                 h_tiles[jt] = ring.tile([P, PASSES, JT, PACK], BF16, name="h", align_bytes=64, bufs=4)
             h = h_tiles[jt]
             nc.vector.tensor_tensor(
@@ -291,11 +289,9 @@ def tile_list_loom_contrast_kernel(
                     out=codes[:].bitcast(E4M3), scales=plane[:], in_=h[:].rearrange("p g j t -> p (g j t)")
                 )
                 h_codes[jt], h_plane[jt] = codes, plane
-                if jt == 0:
-                    gather_words(1, S // 2, S, "first_h")
 
-        def mix(jt, slots, bank):
-            for t in slots:
+        def mix(units, bank):
+            for jt, t in units:
                 for g in range(PASSES):
                     nc.tensor.matmul_mx(
                         out=by_slot(bank)[:, t, :],
@@ -307,73 +303,74 @@ def tile_list_loom_contrast_kernel(
                         stop=(g == PASSES - 1),
                     )
 
-        def put_back(jt, slots, bank, pool=ring, tag="d", bufs=4):
-            rows = slice(slots[0], slots[-1] + 1)
+        def put_back(units, bank, pool=ring, tag="d", bufs=4):
+            rows = slice(units[0][1], units[-1][1] + 1)
             d = pool.tile([P, PACK, JT], F32, name="d", tag=tag, bufs=bufs)
             nc.scalar.copy(d[:, rows, :], by_slot(bank)[:, rows, :])
-            cols = slice(jt * JT // LIST_ROWS, (jt + 1) * JT // LIST_ROWS)
-            for t in slots:
-                wgo_part = factor[jt // 4][:, t, jt % 4 * JT : (jt % 4 + 1) * JT]
+            for jt, t in units:
+                cols = slice(jt * JT // LIST_ROWS, (jt + 1) * JT // LIST_ROWS)
+                wgo_part = factor[jt][:, t, :]
                 nc.vector.tensor_tensor(pages[t][:].indirect(places[:, cols]), d[:, t, :], wgo_part, ALU.mult)
 
         last = len(steps) - 1
+        units = [(jt, t) for jt in range(TILES - 1) for t in range(PACK)]
         mixes = {}
-        for jt in range(TILES - 1):
-            for u in range(2):
-                i = PASSES * jt + LAG + u
-                bank = b_banks[i % 2] if i <= last else total_banks[last % 2]
-                mixes[i] = (jt, range(2 * u, 2 * u + 2), bank)
+        for i in range(EARLY + 1, last + 2):
+            count = 3 if i in THREE else 2
+            mixes[i], units = units[:count], units[count:]
 
-        multiply("a", 0)
-        multiply("a", 1)
-        copy_out("a", 0)
-        round_w2(1, 0, 0, nc.vector.tensor_copy)
-        round_w2(1, 0, HALF, nc.vector.tensor_copy)
-        quantise_w2(1, 0)
-        copy_out("a", 1)
-        for g in range(PASSES):
-            for lo in (0, HALF):
-                round_w2(g, 1, lo, nc.vector.tensor_copy)
-            quantise_w2(g, 1)
+        def mix_bank(i):
+            return b_banks[i % 2] if i <= last else total_banks[last % 2]
+
+        def halves(i):
+            units = mixes.get(i, [])
+            cut = 1 if len(units) < 3 or units[0][0] != units[1][0] or units[1][0] == units[2][0] else 2
+            return units[:cut], units[cut:]
+
+        for i in range(LEAD):
+            multiply("a", i)
+            copy_out("a", i)
+        for rg in range(PASSES):
+            for g in range(PASSES):
+                for lo in (0, HALF):
+                    round_w2(g, rg, lo, nc.vector.tensor_copy)
+                quantise_w2(g, rg)
+                if (g, rg) == (1, 0):
+                    gather_words(0, S // 2, S, "w2_raw10256")
         multiply("b", 0)
-        multiply("a", SPARE)
-        copy_out("a", SPARE)
-        multiply("a", LEAD)
         for i in range(last + 2):
             if i == EARLY:
                 sort_w3()
-            if LEAD <= i <= last and i != SPARE:
+            if LEAD <= i <= last:
                 copy_out("a", i)
             if i >= 1:
                 weigh(i - 1)
                 if i - 1 in mixes:
-                    jt, slots, bank = mixes[i - 1]
-                    put_back(jt, slots[:1], bank)
+                    put_back(halves(i - 1)[0], mix_bank(i - 1))
                 turn("signed", i - 1)
                 if i - 1 in mixes:
-                    mix(jt, slots[1:], bank)
-            if LEAD <= i < last and i + 1 != SPARE:
-                multiply("a", i + 1)
+                    mix(halves(i - 1)[1], mix_bank(i - 1))
             if i >= 1:
                 contrast(i - 1)
+            if LEAD <= i + 1 <= last:
+                multiply("a", i + 1)
             if i <= last:
                 copy_out("b", i)
             if i - 1 in mixes:
-                put_back(jt, slots[1:], bank)
+                put_back(halves(i - 1)[1], mix_bank(i - 1))
             if i <= last:
                 turn("size", i)
             if i in mixes:
-                jt_next, slots_next, bank_next = mixes[i]
-                mix(jt_next, slots_next if i > last else slots_next[:1], bank_next)
+                mix(mixes[i] if i > last else halves(i)[0], mix_bank(i))
             if i + 1 <= last:
                 multiply("b", i + 1)
-        put_back(*mixes[last + 1], keep, "last", 1)
+        put_back(mixes[last + 1], mix_bank(last + 1), keep, "last", 1)
         free_banks = (a_bank, b_banks[0], b_banks[1], total_banks[0])
         for t in range(PACK):
-            mix(TILES - 1, [t], free_banks[t])
+            mix([(TILES - 1, t)], free_banks[t])
         out_rows = out_0.rearrange("(p t) m -> p t m", t=PACK)
         for t in range(PACK):
-            put_back(TILES - 1, [t], free_banks[t])
+            put_back([(TILES - 1, t)], free_banks[t])
             if t == 0:
                 for piece in range(PIECES):
                     cols = slice(piece * Y_COLS, (piece + 1) * Y_COLS)

@@ -29,6 +29,7 @@ HALF = KP // 2
 EARLY = 3
 LEAD = 5
 THREE = (7, 12)
+EARLY_PAGES = 2
 Y_COLS = 256
 PIECES = S // Y_COLS
 
@@ -110,8 +111,7 @@ def tile_list_loom_contrast_kernel(
         load_plane(nc, w1_plane, w1_scales)
         load_w2(0, 0, 0, KP)
         load_w1(1)
-        load_w2(1, 0, 0, HALF)
-        load_w2(1, 0, HALF, HALF)
+        load_w2(1, 0, 0, KP)
         load_w2(0, 1, 0, KP)
         load_w2(1, 1, 0, HALF)
         load_w2(1, 1, HALF, HALF)
@@ -134,10 +134,13 @@ def tile_list_loom_contrast_kernel(
             for j in range(lo, hi, JT):
                 factor[j // JT] = part[:, :, j - lo : j - lo + JT]
         x0_rows = x0.rearrange("(p t) m -> p t m", t=PACK)
-        y = []
+        y, x0_early = [], []
         for piece in range(PIECES):
+            cols = slice(piece * Y_COLS, (piece + 1) * Y_COLS)
+            x0_early.append(keep.tile([P, EARLY_PAGES, Y_COLS], F32, name="x0_early%d" % piece))
+            nc.sync.dma_start(out=x0_early[piece][:], in_=x0_rows[:, :EARLY_PAGES, cols])
             y.append(keep.tile([P, PACK, Y_COLS], F32, name="y%d" % piece))
-            nc.sync.dma_start(out=y[piece][:], in_=x0_rows[:, :, piece * Y_COLS : (piece + 1) * Y_COLS])
+            nc.sync.dma_start(out=y[piece][:, EARLY_PAGES:, :], in_=x0_rows[:, EARLY_PAGES:, cols])
 
         v_plane = {}
 
@@ -190,8 +193,8 @@ def tile_list_loom_contrast_kernel(
 
         def sort_w3():
             nc.vector.tensor_copy(
-                w3[:].rearrange("p (g t m) -> p g t m", g=PASSES, t=PACK),
-                w3_raw[:].rearrange("p (g m t) -> p g t m", g=PASSES, t=PACK),
+                w3[:].rearrange("p (g t m) -> p g m t", g=PASSES, t=PACK),
+                w3_raw[:].rearrange("p (g m t) -> p g m t", g=PASSES, t=PACK),
             )
             nc.vector.tensor_copy(
                 w3_plane[:].rearrange("p (t m) -> p t m", t=PACK),
@@ -213,7 +216,7 @@ def tile_list_loom_contrast_kernel(
         def product_bank(side, i):
             if side == "b":
                 return b_banks[i % 2]
-            return (diff_banks + total_banks)[i] if i < LEAD else a_bank
+            return diff_banks[i] if i < EARLY else a_bank
 
         def total_bank(i):
             return a_bank if i == EARLY else total_banks[i % 2]
@@ -250,12 +253,12 @@ def tile_list_loom_contrast_kernel(
 
         def turn(kind, i):
             bank = total_bank(i) if kind == "size" else diff_banks[i % 3]
-            sides = ("b", "a")
+            sides = ("a", "b") if i < EARLY else ("b", "a")
             for side in sides:
                 for t in range(PACK):
                     nc.tensor.matmul(
                         by_slot(bank)[:, t, :], parts[side, kind, i][:, t, :], ident[:],
-                        start=(side == "b" and t == 0),
+                        start=(side == sides[0] and t == 0),
                         stop=(side == sides[-1] and t == PACK - 1),
                         is_transpose=True,
                     )
@@ -336,7 +339,7 @@ def tile_list_loom_contrast_kernel(
                     round_w2(g, rg, lo, nc.vector.tensor_copy)
                 quantise_w2(g, rg)
                 if (g, rg) == (1, 0):
-                    gather_words(0, S // 2, S, "w2_raw10256")
+                    gather_words(0, S // 2, S, "w2_raw100")
         multiply("b", 0)
         for i in range(last + 2):
             if i == EARLY:
@@ -369,27 +372,34 @@ def tile_list_loom_contrast_kernel(
         for t in range(PACK):
             mix([(TILES - 1, t)], free_banks[t])
         out_rows = out_0.rearrange("(p t) m -> p t m", t=PACK)
-        for t in range(PACK):
+        grouped = []
+        for t in range(EARLY_PAGES):
             put_back([(TILES - 1, t)], free_banks[t])
-            if t == 0:
-                for piece in range(PIECES):
-                    cols = slice(piece * Y_COLS, (piece + 1) * Y_COLS)
-                    nc.vector.tensor_tensor(y[piece][:, 0, :], pages[0][:, cols], y[piece][:, 0, :], ALU.max)
-                    nc.sync.dma_start(out=out_rows[:, :1, cols], in_=y[piece][:, :1, :])
+        for piece in range(PIECES):
+            cols = slice(piece * Y_COLS, (piece + 1) * Y_COLS)
+            for t in range(EARLY_PAGES):
+                nc.vector.tensor_tensor(y[piece][:, t, :], pages[t][:, cols], x0_early[piece][:, t, :], ALU.max)
+            nc.sync.dma_start(out=out_rows[:, :EARLY_PAGES, cols], in_=y[piece][:, :EARLY_PAGES, :])
+        for t in range(EARLY_PAGES, PACK):
+            put_back([(TILES - 1, t)], free_banks[t], keep, "x0_early%d" % (t - EARLY_PAGES), 1)
+        for piece in range(PIECES):
+            grouped.append(keep.tile([P, Y_COLS, PACK], BF16, name="y_grouped%d" % piece, align_bytes=64))
+            nc.scalar.copy(
+                word_order(grouped[piece][:, :, :EARLY_PAGES]), slot_order(y[piece][:, :EARLY_PAGES, :])
+            )
 
         y_codes = keep.tile([P, S], U32, name="y_codes", align_bytes=64)
         y_plane = keep.tile([P, S], U8, name="y_plane", align_bytes=64)
         out_words = out_1[0].rearrange("p m t -> p (m t)").bitcast(I32)
-        grouped = {}
 
-        def larger(piece):
+        def maxima(piece):
             cols = slice(piece * Y_COLS, (piece + 1) * Y_COLS)
-            for t in range(1, PACK):
+            for t in range(EARLY_PAGES, PACK):
                 nc.vector.tensor_tensor(y[piece][:, t, :], pages[t][:, cols], y[piece][:, t, :], ALU.max)
-            nc.sync.dma_start(out=out_rows[:, 1:, cols], in_=y[piece][:, 1:, :])
-            grouped[piece] = ring.tile([P, Y_COLS, PACK], BF16, name="y_grouped", align_bytes=64, bufs=PIECES)
-            round_and_group = nc.vector.tensor_copy if piece == PIECES - 1 else nc.scalar.copy
-            round_and_group(word_order(grouped[piece][:]), slot_order(y[piece][:]))
+            nc.sync.dma_start(out=out_rows[:, EARLY_PAGES:, cols], in_=y[piece][:, EARLY_PAGES:, :])
+
+        def round_late(piece, copy):
+            copy(word_order(grouped[piece][:, :, EARLY_PAGES:]), slot_order(y[piece][:, EARLY_PAGES:, :]))
 
         def encode(piece):
             cols = slice(piece * Y_COLS, (piece + 1) * Y_COLS)
@@ -398,13 +408,18 @@ def tile_list_loom_contrast_kernel(
                 scales=y_plane[:, cols],
                 in_=grouped[piece][:].rearrange("p m t -> p (m t)"),
             )
-            nc.sync.dma_start(out=out_words[:, cols], in_=y_codes[:, cols].bitcast(I32))
+            if piece > 0:
+                cols = slice(0, 2 * Y_COLS) if piece == 1 else cols
+                nc.sync.dma_start(out=out_words[:, cols], in_=y_codes[:, cols].bitcast(I32))
 
-        for piece in range(PIECES + 2):
-            if piece < PIECES:
-                larger(piece)
-            if piece >= 2:
-                encode(piece - 2)
+        for piece in range(PIECES):
+            maxima(piece)
+        for piece in range(PIECES - 1):
+            round_late(piece, nc.scalar.copy)
+        encode(0)
+        round_late(PIECES - 1, nc.vector.tensor_copy)
+        for piece in (1, 3, 2):
+            encode(piece)
         for r in range(4):
             queue = nc.scalar if r % 2 else nc.sync
             queue.dma_start(out=out_2[0, r:16:4, :].bitcast(I32), in_=y_plane[r:P:32, :].bitcast(I32))

@@ -29,6 +29,7 @@ HALF = KP // 2
 EARLY = 3
 LEAD = 5
 THREE = (7, 12)
+SCALAR_WEIGHS = (14, 15)
 EARLY_PAGES = 2
 Y_COLS = 256
 PIECES = S // Y_COLS
@@ -202,9 +203,10 @@ def tile_list_loom_contrast_kernel(
             )
 
         pages = [keep.tile([P, S], F32, name="page%d" % t) for t in range(PACK)]
-        a_bank = psum.tile([P, KP], F32, name="a_bank")
-        b_banks = [psum.tile([P, KP], F32, name="b_bank%d" % u) for u in range(2)]
-        total_banks = [psum.tile([P, KP], F32, name="total%d" % u) for u in range(2)]
+        a_banks = [psum.tile([P, KP], F32, name="a_bank%d" % u) for u in range(2)]
+        b_bank = psum.tile([P, KP], F32, name="b_bank")
+        d_bank = psum.tile([P, KP], F32, name="d_bank")
+        sum_bank = psum.tile([P, KP], F32, name="sum_bank")
         diff_banks = [psum.tile([P, KP], F32, name="diff%d" % u) for u in range(3)]
         steps = [(jt, rg) for rg in range(PASSES) for jt in range(EARLY)]
         steps += [(jt, rg) for jt in range(EARLY, TILES) for rg in range(PASSES)]
@@ -215,11 +217,11 @@ def tile_list_loom_contrast_kernel(
 
         def product_bank(side, i):
             if side == "b":
-                return b_banks[i % 2]
-            return diff_banks[i] if i < EARLY else a_bank
+                return d_bank if i <= EARLY and i % 2 else b_bank
+            return diff_banks[i] if i < EARLY else a_banks[i % 2]
 
         def total_bank(i):
-            return a_bank if i == EARLY else total_banks[i % 2]
+            return {1: a_banks[0], EARLY: a_banks[1]}.get(i, sum_bank)
 
         def multiply(side, i):
             jt, rg = steps[i]
@@ -244,16 +246,20 @@ def tile_list_loom_contrast_kernel(
         def copy_out(side, i):
             bank = product_bank(side, i)
             sorted_view = bank[:].rearrange("j (p t) -> j t p", t=PACK)
-            depth = LEAD if side == "a" else 2
-            size = ring.tile([P, PACK, P], F32, name=side + "_size", bufs=depth)
-            signed = ring.tile([P, PACK, P], F32, name=side + "_signed", bufs=depth)
+            if side == "a":
+                slot = i if i < LEAD else 2 + (i - LEAD) % 3
+                size = keep.tile([P, PACK, P], F32, name="a_size%d" % slot)
+                signed = keep.tile([P, PACK, P], F32, name="a_signed%d" % slot)
+            else:
+                size = ring.tile([P, PACK, P], F32, name="b_size")
+                signed = ring.tile([P, PACK, P], F32, name="b_signed")
             nc.scalar.activation(size[:], sorted_view, ACT.Abs)
             nc.scalar.activation(signed[:], sorted_view, ACT.Copy, scale=-1.0 if side == "b" else 1.0)
             parts[side, "size", i], parts[side, "signed", i] = size, signed
 
         def turn(kind, i):
             bank = total_bank(i) if kind == "size" else diff_banks[i % 3]
-            sides = ("a", "b") if i < EARLY else ("b", "a")
+            sides = ("a", "b") if i < EARLY or kind == "size" else ("b", "a")
             for side in sides:
                 for t in range(PACK):
                     nc.tensor.matmul(
@@ -271,10 +277,17 @@ def tile_list_loom_contrast_kernel(
                 weight = ring.tile([P, PACK, JT], F32, name="weight", bufs=3)
             else:
                 weight = keep.tile([P, PACK, JT], F32, name="last_weight", tag="last")
+            if i in SCALAR_WEIGHS:
+                square = ring.tile([P, PACK, JT], F32, name="square", bufs=1)
+                nc.scalar.activation(square[:], root[:], ACT.Square)
             for t in range(PACK):
-                nc.vector.scalar_tensor_tensor(
-                    weight[:, t, :], root[:, t, :], gains[:, rg, t : t + 1], root[:, t, :], ALU.mult, ALU.mult
-                )
+                gain_t = gains[:, rg, t : t + 1]
+                if i in SCALAR_WEIGHS:
+                    nc.scalar.activation(weight[:, t, :], square[:, t, :], ACT.Copy, scale=gain_t)
+                else:
+                    nc.vector.scalar_tensor_tensor(
+                        weight[:, t, :], root[:, t, :], gain_t, root[:, t, :], ALU.mult, ALU.mult
+                    )
             weights[i] = weight
 
         def contrast(i):
@@ -294,10 +307,10 @@ def tile_list_loom_contrast_kernel(
                 h_codes[jt], h_plane[jt] = codes, plane
 
         def mix(units, bank):
-            for jt, t in units:
+            for u, (jt, t) in enumerate(units):
                 for g in range(PASSES):
                     nc.tensor.matmul_mx(
-                        out=by_slot(bank)[:, t, :],
+                        out=by_slot(bank)[:, u, :],
                         lhsT=w3[:, N * g + P * t : N * g + P * (t + 1)].bitcast(E4M3),
                         lhsT_scale=w3_plane[4 * g : P, P * t : P * (t + 1)],
                         rhs=h_codes[jt][:, JT * g : JT * (g + 1)].bitcast(E4M3),
@@ -306,14 +319,20 @@ def tile_list_loom_contrast_kernel(
                         stop=(g == PASSES - 1),
                     )
 
+        def empty(units, bank, lo, hi, pool=ring, tag="d", bufs=4):
+            d = pool.tile([P, hi - lo, JT], F32, name="d", tag=tag, bufs=bufs)
+            nc.scalar.copy(d[:], by_slot(bank)[:, lo:hi, :])
+            return d
+
+        def scatter(unit, values):
+            jt, t = unit
+            cols = slice(jt * JT // LIST_ROWS, (jt + 1) * JT // LIST_ROWS)
+            nc.vector.tensor_tensor(pages[t][:].indirect(places[:, cols]), values, factor[jt][:, t, :], ALU.mult)
+
         def put_back(units, bank, pool=ring, tag="d", bufs=4):
-            rows = slice(units[0][1], units[-1][1] + 1)
-            d = pool.tile([P, PACK, JT], F32, name="d", tag=tag, bufs=bufs)
-            nc.scalar.copy(d[:, rows, :], by_slot(bank)[:, rows, :])
-            for jt, t in units:
-                cols = slice(jt * JT // LIST_ROWS, (jt + 1) * JT // LIST_ROWS)
-                wgo_part = factor[jt][:, t, :]
-                nc.vector.tensor_tensor(pages[t][:].indirect(places[:, cols]), d[:, t, :], wgo_part, ALU.mult)
+            d = empty(units, bank, 0, len(units), pool, tag, bufs)
+            for u, unit in enumerate(units):
+                scatter(unit, d[:, u, :])
 
         last = len(steps) - 1
         units = [(jt, t) for jt in range(TILES - 1) for t in range(PACK)]
@@ -321,14 +340,6 @@ def tile_list_loom_contrast_kernel(
         for i in range(EARLY + 1, last + 2):
             count = 3 if i in THREE else 2
             mixes[i], units = units[:count], units[count:]
-
-        def mix_bank(i):
-            return b_banks[i % 2] if i <= last else total_banks[last % 2]
-
-        def halves(i):
-            units = mixes.get(i, [])
-            cut = 1 if len(units) < 3 or units[0][0] != units[1][0] or units[1][0] == units[2][0] else 2
-            return units[:cut], units[cut:]
 
         for i in range(LEAD):
             multiply("a", i)
@@ -341,34 +352,37 @@ def tile_list_loom_contrast_kernel(
                 if (g, rg) == (1, 0):
                     gather_words(0, S // 2, S, "w2_raw100")
         multiply("b", 0)
-        for i in range(last + 2):
+        multiply("b", 1)
+        copy_out("b", 0)
+        turn("size", 0)
+        for i in range(last + 1):
             if i == EARLY:
                 sort_w3()
-            if LEAD <= i <= last:
-                copy_out("a", i)
-            if i >= 1:
-                weigh(i - 1)
-                if i - 1 in mixes:
-                    put_back(halves(i - 1)[0], mix_bank(i - 1))
-                turn("signed", i - 1)
-                if i - 1 in mixes:
-                    mix(halves(i - 1)[1], mix_bank(i - 1))
-            if i >= 1:
-                contrast(i - 1)
-            if LEAD <= i + 1 <= last:
-                multiply("a", i + 1)
-            if i <= last:
-                copy_out("b", i)
-            if i - 1 in mixes:
-                put_back(halves(i - 1)[1], mix_bank(i - 1))
-            if i <= last:
-                turn("size", i)
-            if i in mixes:
-                mix(mixes[i] if i > last else halves(i)[0], mix_bank(i))
-            if i + 1 <= last:
+            weigh(i)
+            units = mixes.get(i, [])
+            if 1 <= i < last:
                 multiply("b", i + 1)
-        put_back(mixes[last + 1], mix_bank(last + 1), keep, "last", 1)
-        free_banks = (a_bank, b_banks[0], b_banks[1], total_banks[0])
+            mix(units, d_bank)
+            if LEAD <= i + 2 <= last:
+                multiply("a", i + 2)
+            if i == last:
+                mix(mixes[last + 1], b_bank)
+            if units:
+                scatter(units[0], empty(units, d_bank, 0, 1)[:, 0, :])
+            turn("signed", i)
+            contrast(i)
+            if i < last:
+                copy_out("b", i + 1)
+            if units:
+                d = empty(units, d_bank, 1, len(units))
+                for u in range(1, len(units)):
+                    scatter(units[u], d[:, u - 1, :])
+            if i < last:
+                turn("size", i + 1)
+            if LEAD <= i + 2 <= last:
+                copy_out("a", i + 2)
+        put_back(mixes[last + 1], b_bank, keep, "last", 1)
+        free_banks = (a_banks[0], a_banks[1], sum_bank, d_bank)
         for t in range(PACK):
             mix([(TILES - 1, t)], free_banks[t])
         out_rows = out_0.rearrange("(p t) m -> p t m", t=PACK)

@@ -362,27 +362,30 @@ def tile_list_loom_contrast_kernel(
             units = mixes.get(i, [])
             if 1 <= i < last:
                 multiply("b", i + 1)
-            mix(units, d_bank)
+            mix(units, d_bank if i < last else b_bank)
             if LEAD <= i + 2 <= last:
                 multiply("a", i + 2)
             if i == last:
-                mix(mixes[last + 1], b_bank)
-            if units:
-                scatter(units[0], empty(units, d_bank, 0, 1)[:, 0, :])
+                mix(mixes[last + 1], sum_bank)
+                scatter(units[0], empty(units, b_bank, 0, 1)[:, 0, :])
+            elif units:
+                d = empty(units, d_bank, 0, len(units))
+                scatter(units[0], d[:, 0, :])
             turn("signed", i)
             contrast(i)
             if i < last:
                 copy_out("b", i + 1)
-            if units:
-                d = empty(units, d_bank, 1, len(units))
+            if i == last:
+                scatter(units[1], empty(units, b_bank, 1, 2, ring, "square", 1)[:, 0, :])
+            elif units:
                 for u in range(1, len(units)):
-                    scatter(units[u], d[:, u - 1, :])
+                    scatter(units[u], d[:, u, :])
             if i < last:
                 turn("size", i + 1)
             if LEAD <= i + 2 <= last:
                 copy_out("a", i + 2)
-        put_back(mixes[last + 1], b_bank, keep, "last", 1)
-        free_banks = (a_banks[0], a_banks[1], sum_bank, d_bank)
+        put_back(mixes[last + 1], sum_bank, keep, "last", 1)
+        free_banks = (a_banks[0], a_banks[1], diff_banks[1], d_bank)
         for t in range(PACK):
             mix([(TILES - 1, t)], free_banks[t])
         out_rows = out_0.rearrange("(p t) m -> p t m", t=PACK)

@@ -27,7 +27,7 @@ JT = 128
 TILES = S // JT
 HALF = KP // 2
 EARLY = 3
-LEAD = 5
+LEAD = 4
 THREE = (7, 12)
 SCALAR_WEIGHS = (14, 15)
 EARLY_PAGES = 2
@@ -247,7 +247,7 @@ def tile_list_loom_contrast_kernel(
             bank = product_bank(side, i)
             sorted_view = bank[:].rearrange("j (p t) -> j t p", t=PACK)
             if side == "a":
-                slot = i if i < LEAD else 2 + (i - LEAD) % 3
+                slot = i if i < LEAD else 1 + (i - LEAD) % 3
                 size = keep.tile([P, PACK, P], F32, name="a_size%d" % slot)
                 signed = keep.tile([P, PACK, P], F32, name="a_signed%d" % slot)
             else:

@@ -27,9 +27,11 @@ JT = 128
 TILES = S // JT
 HALF = KP // 2
 EARLY = 3
-LEAD = 4
-THREE = (7, 12)
+LEAD = 6
+THREE = ()
+GPSIMD_SCALES = ()
 SCALAR_WEIGHS = (14, 15)
+VECTOR_ENDS = (2, 3)
 EARLY_PAGES = 2
 Y_COLS = 256
 PIECES = S // Y_COLS
@@ -156,12 +158,16 @@ def tile_list_loom_contrast_kernel(
 
         w2_grouped, w2_codes, w2_plane = {}, {}, {}
 
-        def round_w2(g, rg, lo, copy):
+        def round_w2(g, rg, lo):
             if lo == 0:
                 w2_grouped[g, rg] = keep.tile(
                     [P, KP, PACK], BF16, name="w2_grouped%d%d" % (g, rg), tag="stage%d" % g, align_bytes=64
                 )
-            copy(word_order(w2_grouped[g, rg][:, lo : lo + HALF, :]), slot_order(w2_raw[g, rg, lo]))
+            grouped, raw = w2_grouped[g, rg][:, lo : lo + HALF, :], w2_raw[g, rg, lo]
+            if (g, rg) == (0, 0):
+                nc.gpsimd.tensor_scalar(grouped, raw.rearrange("p i c -> p c i"), 1.0, 1.0, ALU.mult, ALU.mult)
+            else:
+                nc.vector.tensor_copy(word_order(grouped), slot_order(raw))
 
         def quantise_w2(g, rg):
             grouped = w2_grouped[g, rg]
@@ -183,16 +189,18 @@ def tile_list_loom_contrast_kernel(
             for j in range(lo, hi, JT):
                 v_words[g, j // JT] = words[:, j - lo : j - lo + JT]
 
-        gather_plane(0, 0, S)
-        gather_plane(1, 0, S)
-        gather_words(0, 0, S // 2)
-        gather_words(1, 0, S // 4)
-        gather_words(1, S // 4, S)
-
-        w3 = keep.tile([P, PASSES * N], I32, name="w3", align_bytes=64)
-        w3_plane = keep.tile([P, N], U8, name="w3_plane", align_bytes=64)
+        first = EARLY * JT
+        gather_plane(0, 0, first)
+        gather_plane(1, 0, first)
+        gather_plane(0, first, S)
+        gather_words(0, 0, first)
+        gather_words(1, 0, JT)
+        gather_words(1, JT, first)
+        gather_words(1, first, S)
 
         def sort_w3():
+            w3 = keep.tile([P, PASSES * N], I32, name="w3", tag="stage1", align_bytes=64)
+            w3_plane = keep.tile([P, N], U8, name="w3_plane", tag="w2_raw11%d" % HALF, align_bytes=64)
             nc.vector.tensor_copy(
                 w3[:].rearrange("p (g t m) -> p g m t", g=PASSES, t=PACK),
                 w3_raw[:].rearrange("p (g m t) -> p g m t", g=PASSES, t=PACK),
@@ -201,31 +209,30 @@ def tile_list_loom_contrast_kernel(
                 w3_plane[:].rearrange("p (t m) -> p t m", t=PACK),
                 w3_plane_raw[:].rearrange("p (m t) -> p t m", t=PACK),
             )
+            return w3, w3_plane
 
         pages = [keep.tile([P, S], F32, name="page%d" % t) for t in range(PACK)]
         a_banks = [psum.tile([P, KP], F32, name="a_bank%d" % u) for u in range(2)]
-        b_bank = psum.tile([P, KP], F32, name="b_bank")
-        d_bank = psum.tile([P, KP], F32, name="d_bank")
-        sum_bank = psum.tile([P, KP], F32, name="sum_bank")
-        diff_banks = [psum.tile([P, KP], F32, name="diff%d" % u) for u in range(3)]
+        b_banks = [psum.tile([P, KP], F32, name="b_bank%d" % u) for u in range(2)]
+        sum_banks = [psum.tile([P, KP], F32, name="sum_bank%d" % u) for u in range(2)]
+        diff_banks = [psum.tile([P, KP], F32, name="diff%d" % u) for u in range(2)]
         steps = [(jt, rg) for rg in range(PASSES) for jt in range(EARLY)]
         steps += [(jt, rg) for jt in range(EARLY, TILES) for rg in range(PASSES)]
-        parts, weights, h_tiles, h_codes, h_plane = {}, {}, {}, {}, {}
+        last = len(steps) - 1
+        parts, roots, weights, h_tiles, h_codes, h_plane = {}, {}, {}, {}, {}, {}
 
         def by_slot(bank):
             return bank[:].rearrange("p (t j) -> p t j", t=PACK)
 
-        def product_bank(side, i):
-            if side == "b":
-                return d_bank if i <= EARLY and i % 2 else b_bank
-            return diff_banks[i] if i < EARLY else a_banks[i % 2]
+        def sum_bank(i):
+            return sum_banks[i % 2]
 
-        def total_bank(i):
-            return {1: a_banks[0], EARLY: a_banks[1]}.get(i, sum_bank)
+        def diff_bank(i):
+            return (a_banks if i in (2, 3) else diff_banks)[i % 2]
 
         def multiply(side, i):
             jt, rg = steps[i]
-            bank = product_bank(side, i)
+            bank = (a_banks if side == "a" else b_banks)[i % 2]
             for g in range(PASSES):
                 if side == "a":
                     rhs = w1[rg][:, 2 * KP * g : 2 * KP * (g + 1)].bitcast(E2M1)
@@ -244,67 +251,68 @@ def tile_list_loom_contrast_kernel(
                 )
 
         def copy_out(side, i):
-            bank = product_bank(side, i)
+            bank = (a_banks if side == "a" else b_banks)[i % 2]
             sorted_view = bank[:].rearrange("j (p t) -> j t p", t=PACK)
-            if side == "a":
-                slot = i if i < LEAD else 1 + (i - LEAD) % 3
-                size = keep.tile([P, PACK, P], F32, name="a_size%d" % slot)
-                signed = keep.tile([P, PACK, P], F32, name="a_signed%d" % slot)
-            else:
-                size = ring.tile([P, PACK, P], F32, name="b_size")
-                signed = ring.tile([P, PACK, P], F32, name="b_signed")
+            slot = i % 3 if side == "b" else i if i < LEAD else 1 + i % 3
+            size = keep.tile([P, PACK, P], F32, name="%s_size%d" % (side, slot), align_bytes=64)
+            signed = keep.tile([P, PACK, P], F32, name="%s_signed%d" % (side, slot), align_bytes=64)
             nc.scalar.activation(size[:], sorted_view, ACT.Abs)
             nc.scalar.activation(signed[:], sorted_view, ACT.Copy, scale=-1.0 if side == "b" else 1.0)
             parts[side, "size", i], parts[side, "signed", i] = size, signed
 
         def turn(kind, i):
-            bank = total_bank(i) if kind == "size" else diff_banks[i % 3]
-            sides = ("a", "b") if i < EARLY or kind == "size" else ("b", "a")
-            for side in sides:
+            bank = sum_bank(i) if kind == "size" else diff_bank(i)
+            for side in ("a", "b"):
                 for t in range(PACK):
                     nc.tensor.matmul(
                         by_slot(bank)[:, t, :], parts[side, kind, i][:, t, :], ident[:],
-                        start=(side == sides[0] and t == 0),
-                        stop=(side == sides[-1] and t == PACK - 1),
+                        start=(side == "a" and t == 0),
+                        stop=(side == "b" and t == PACK - 1),
                         is_transpose=True,
                     )
 
         def weigh(i):
             rg = steps[i][1]
             root = ring.tile([P, PACK, JT], F32, name="root", bufs=3)
-            nc.scalar.activation(root[:], by_slot(total_bank(i)), ACT.Abs_reciprocal_sqrt, bias=half[:])
-            if i < last:
-                weight = ring.tile([P, PACK, JT], F32, name="weight", bufs=3)
-            else:
-                weight = keep.tile([P, PACK, JT], F32, name="last_weight", tag="last")
-            if i in SCALAR_WEIGHS:
-                square = ring.tile([P, PACK, JT], F32, name="square", bufs=1)
-                nc.scalar.activation(square[:], root[:], ACT.Square)
+            nc.scalar.activation(root[:], by_slot(sum_bank(i)), ACT.Abs_reciprocal_sqrt, bias=half[:])
+            roots[i] = root
+            if i not in SCALAR_WEIGHS:
+                return
+            weight = keep.tile([P, PACK, JT], F32, name="weight", tag="last" if i == last else "weight")
+            square = ring.tile([P, PACK, JT], F32, name="square", bufs=1)
+            nc.scalar.activation(square[:], root[:], ACT.Square)
             for t in range(PACK):
-                gain_t = gains[:, rg, t : t + 1]
-                if i in SCALAR_WEIGHS:
-                    nc.scalar.activation(weight[:, t, :], square[:, t, :], ACT.Copy, scale=gain_t)
-                else:
-                    nc.vector.scalar_tensor_tensor(
-                        weight[:, t, :], root[:, t, :], gain_t, root[:, t, :], ALU.mult, ALU.mult
-                    )
+                nc.scalar.activation(weight[:, t, :], square[:, t, :], ACT.Copy, scale=gains[:, rg, t : t + 1])
             weights[i] = weight
 
         def contrast(i):
             jt, rg = steps[i]
             if rg == 0:
-                h_tiles[jt] = ring.tile([P, PASSES, JT, PACK], BF16, name="h", align_bytes=64, bufs=4)
+                h_tiles[jt] = keep.tile([P, PASSES, JT, PACK], BF16, name="h%d" % min(jt, 1 + jt % 3), align_bytes=64)
             h = h_tiles[jt]
-            nc.vector.tensor_tensor(
-                word_order(h[:, rg]), slot_order(by_slot(diff_banks[i % 3])), slot_order(weights[i][:]), ALU.mult
-            )
-            if rg == PASSES - 1:
-                codes = ring.tile([P, PASSES * JT], U32, name="h_codes", align_bytes=64, bufs=3)
-                plane = ring.tile([P, PASSES * JT], U8, name="h_plane", align_bytes=64, bufs=3)
-                nc.vector.quantize_mx(
-                    out=codes[:].bitcast(E4M3), scales=plane[:], in_=h[:].rearrange("p g j t -> p (g j t)")
+            diff = by_slot(diff_bank(i))
+            if i in SCALAR_WEIGHS:
+                nc.vector.tensor_tensor(word_order(h[:, rg]), slot_order(diff), slot_order(weights[i][:]), ALU.mult)
+                return
+            part = ring.tile([P, PACK, JT], F32, name="part", bufs=3)
+            for t in range(PACK):
+                nc.vector.scalar_tensor_tensor(
+                    part[:, t, :], diff[:, t, :], gains[:, rg, t : t + 1], roots[i][:, t, :], ALU.mult, ALU.mult
                 )
-                h_codes[jt], h_plane[jt] = codes, plane
+            if i in VECTOR_ENDS:
+                nc.vector.tensor_tensor(word_order(h[:, rg]), slot_order(part[:]), slot_order(roots[i][:]), ALU.mult)
+            else:
+                nc.gpsimd.tensor_tensor(
+                    h[:, rg], part[:].rearrange("p t j -> p j t"), roots[i][:].rearrange("p t j -> p j t"), ALU.mult
+                )
+
+        def quantise_h(jt, tag):
+            codes = keep.tile([P, PASSES * JT], U32, name="h_codes%d" % (jt % 3), align_bytes=64)
+            plane = keep.tile([P, PASSES * JT], U8, name="h_plane", tag=tag, align_bytes=64)
+            nc.vector.quantize_mx(
+                out=codes[:].bitcast(E4M3), scales=plane[:], in_=h_tiles[jt][:].rearrange("p g j t -> p (g j t)")
+            )
+            h_codes[jt], h_plane[jt] = codes, plane
 
         def mix(units, bank):
             for u, (jt, t) in enumerate(units):
@@ -319,27 +327,36 @@ def tile_list_loom_contrast_kernel(
                         stop=(g == PASSES - 1),
                     )
 
-        def empty(units, bank, lo, hi, pool=ring, tag="d", bufs=4):
-            d = pool.tile([P, hi - lo, JT], F32, name="d", tag=tag, bufs=bufs)
-            nc.scalar.copy(d[:], by_slot(bank)[:, lo:hi, :])
-            return d
-
-        def scatter(unit, values):
+        def window(unit):
             jt, t = unit
-            cols = slice(jt * JT // LIST_ROWS, (jt + 1) * JT // LIST_ROWS)
-            nc.vector.tensor_tensor(pages[t][:].indirect(places[:, cols]), values, factor[jt][:, t, :], ALU.mult)
+            return pages[t][:].indirect(places[:, jt * JT // LIST_ROWS : (jt + 1) * JT // LIST_ROWS])
 
         def put_back(units, bank, pool=ring, tag="d", bufs=4):
-            d = empty(units, bank, 0, len(units), pool, tag, bufs)
-            for u, unit in enumerate(units):
-                scatter(unit, d[:, u, :])
+            d = pool.tile([P, len(units), JT], F32, name="d", tag=tag, bufs=bufs)
+            nc.scalar.copy(d[:], by_slot(bank)[:, : len(units), :])
+            for u, (jt, t) in enumerate(units):
+                nc.vector.tensor_tensor(window((jt, t)), d[:, u, :], factor[jt][:, t, :], ALU.mult)
 
-        last = len(steps) - 1
+        def put_back_beside(units, bank, i):
+            scaled = []
+            if i in GPSIMD_SCALES:
+                d = ring.tile([P, len(units), JT], F32, name="d", bufs=4)
+                nc.scalar.copy(d[:], by_slot(bank)[:, : len(units), :])
+            for u, (jt, t) in enumerate(units):
+                scaled.append(keep.tile([P, JT], F32, name="scaled%d_%d" % (i % 4, u), align_bytes=64))
+                if i in GPSIMD_SCALES:
+                    nc.gpsimd.tensor_tensor(scaled[u][:], d[:, u, :], factor[jt][:, t, :], ALU.mult)
+                else:
+                    nc.vector.tensor_tensor(scaled[u][:], by_slot(bank)[:, u, :], factor[jt][:, t, :], ALU.mult)
+            for u, unit in enumerate(units):
+                nc.vector.tensor_copy(window(unit), scaled[u][:])
+
         units = [(jt, t) for jt in range(TILES - 1) for t in range(PACK)]
         mixes = {}
-        for i in range(EARLY + 1, last + 2):
+        for i in range(EARLY + 1, last + 1):
             count = 3 if i in THREE else 2
             mixes[i], units = units[:count], units[count:]
+        left = units
 
         for i in range(LEAD):
             multiply("a", i)
@@ -347,45 +364,47 @@ def tile_list_loom_contrast_kernel(
         for rg in range(PASSES):
             for g in range(PASSES):
                 for lo in (0, HALF):
-                    round_w2(g, rg, lo, nc.vector.tensor_copy)
+                    round_w2(g, rg, lo)
                 quantise_w2(g, rg)
-                if (g, rg) == (1, 0):
-                    gather_words(0, S // 2, S, "w2_raw100")
-        multiply("b", 0)
-        multiply("b", 1)
-        copy_out("b", 0)
-        turn("size", 0)
+        w3, w3_plane = sort_w3()
+        for i in range(2):
+            multiply("b", i)
+            copy_out("b", i)
         for i in range(last + 1):
-            if i == EARLY:
-                sort_w3()
+            jt, rg = steps[i]
+            turn("size", i)
+            turn("signed", i)
             weigh(i)
             units = mixes.get(i, [])
-            if 1 <= i < last:
-                multiply("b", i + 1)
-            mix(units, d_bank if i < last else b_bank)
+            ahead = [] if i == EARLY - 1 else [i + 1, i + 2] if i == EARLY else [i + 2] if i + 2 <= last else []
             if LEAD <= i + 2 <= last:
                 multiply("a", i + 2)
-            if i == last:
-                mix(mixes[last + 1], sum_bank)
-                scatter(units[0], empty(units, b_bank, 0, 1)[:, 0, :])
-            elif units:
-                d = empty(units, d_bank, 0, len(units))
-                scatter(units[0], d[:, 0, :])
-            turn("signed", i)
+            for later in ahead:
+                multiply("b", later)
+            d_bank = diff_bank(i - 1) if i == EARLY + 1 else sum_bank(i)
+            mix(units, d_bank)
             contrast(i)
-            if i < last:
-                copy_out("b", i + 1)
-            if i == last:
-                scatter(units[1], empty(units, b_bank, 1, 2, ring, "square", 1)[:, 0, :])
+            beside = i < min(SCALAR_WEIGHS)
+            if units and beside:
+                put_back_beside(units, d_bank, i)
             elif units:
-                for u in range(1, len(units)):
-                    scatter(units[u], d[:, u, :])
-            if i < last:
-                turn("size", i + 1)
+                put_back(units, d_bank)
+            if rg == PASSES - 1:
+                quantise_h(jt, "scaled%d_0" % (i % 4) if units and beside else "h_plane%d" % jt)
+            if i == 0:
+                gather_words(0, first, S, "a_size0")
+                gather_plane(1, first, first + 2 * JT, "a_signed0")
+            if i == EARLY:
+                gather_plane(1, first + 2 * JT, S, "h0")
             if LEAD <= i + 2 <= last:
                 copy_out("a", i + 2)
-        put_back(mixes[last + 1], sum_bank, keep, "last", 1)
-        free_banks = (a_banks[0], a_banks[1], diff_banks[1], d_bank)
+            for later in ahead:
+                copy_out("b", later)
+        mix(left[:-2], b_banks[0])
+        put_back(left[:-2], b_banks[0])
+        mix(left[-2:], sum_bank(last - 1))
+        put_back(left[-2:], sum_bank(last - 1), keep, "last", 1)
+        free_banks = (a_banks[0], a_banks[1], diff_banks[0], b_banks[1])
         for t in range(PACK):
             mix([(TILES - 1, t)], free_banks[t])
         out_rows = out_0.rearrange("(p t) m -> p t m", t=PACK)
@@ -400,7 +419,7 @@ def tile_list_loom_contrast_kernel(
         for t in range(EARLY_PAGES, PACK):
             put_back([(TILES - 1, t)], free_banks[t], keep, "x0_early%d" % (t - EARLY_PAGES), 1)
         for piece in range(PIECES):
-            grouped.append(keep.tile([P, Y_COLS, PACK], BF16, name="y_grouped%d" % piece, align_bytes=64))
+            grouped.append(keep.tile([P, Y_COLS, PACK], BF16, name="y_grouped", tag="a_signed%d" % (piece + 2), align_bytes=64))
             nc.scalar.copy(
                 word_order(grouped[piece][:, :, :EARLY_PAGES]), slot_order(y[piece][:, :EARLY_PAGES, :])
             )

@@ -26,6 +26,7 @@ LIST_ROWS = 16
 JT = 128
 TILES = S // JT
 HALF = KP // 2
+RUN = 4
 EARLY = 3
 LEAD = 6
 THREE = ()
@@ -273,11 +274,14 @@ def tile_list_loom_contrast_kernel(
 
         def weigh(i):
             rg = steps[i][1]
+            if i not in SCALAR_WEIGHS:
+                root = ring.tile([P, JT // RUN, PACK, RUN], F32, name="root", bufs=3)
+                total = by_slot(sum_bank(i)).rearrange("p t (c e) -> p c t e", e=RUN)
+                nc.scalar.activation(root[:], total, ACT.Abs_reciprocal_sqrt, bias=half[:])
+                roots[i] = root
+                return
             root = ring.tile([P, PACK, JT], F32, name="root", bufs=3)
             nc.scalar.activation(root[:], by_slot(sum_bank(i)), ACT.Abs_reciprocal_sqrt, bias=half[:])
-            roots[i] = root
-            if i not in SCALAR_WEIGHS:
-                return
             weight = keep.tile([P, PACK, JT], F32, name="weight", tag="last" if i == last else "weight")
             square = ring.tile([P, PACK, JT], F32, name="square", bufs=1)
             nc.scalar.activation(square[:], root[:], ACT.Square)
@@ -294,17 +298,18 @@ def tile_list_loom_contrast_kernel(
             if i in SCALAR_WEIGHS:
                 nc.vector.tensor_tensor(word_order(h[:, rg]), slot_order(diff), slot_order(weights[i][:]), ALU.mult)
                 return
-            part = ring.tile([P, PACK, JT], F32, name="part", bufs=3)
+            part = ring.tile([P, JT // RUN, PACK, RUN], F32, name="part", bufs=3)
             for t in range(PACK):
                 nc.vector.scalar_tensor_tensor(
-                    part[:, t, :], diff[:, t, :], gains[:, rg, t : t + 1], roots[i][:, t, :], ALU.mult, ALU.mult
+                    part[:, :, t, :],
+                    diff[:, t, :].rearrange("p (c e) -> p c e", e=RUN),
+                    gains[:, rg, t : t + 1],
+                    roots[i][:, :, t, :],
+                    ALU.mult,
+                    ALU.mult,
                 )
-            if i in VECTOR_ENDS:
-                nc.vector.tensor_tensor(word_order(h[:, rg]), slot_order(part[:]), slot_order(roots[i][:]), ALU.mult)
-            else:
-                nc.gpsimd.tensor_tensor(
-                    h[:, rg], part[:].rearrange("p t j -> p j t"), roots[i][:].rearrange("p t j -> p j t"), ALU.mult
-                )
+            engine = nc.vector if i in VECTOR_ENDS else nc.gpsimd
+            engine.tensor_tensor(h[:, rg].rearrange("p (c e) t -> p c t e", e=RUN), part[:], roots[i][:], ALU.mult)
 
         def quantise_h(jt, tag):
             codes = keep.tile([P, PASSES * JT], U32, name="h_codes%d" % (jt % 3), align_bytes=64)

@@ -32,7 +32,8 @@ LEAD = 6
 THREE = ()
 GPSIMD_SCALES = ()
 SCALAR_WEIGHS = (14, 15)
-VECTOR_ENDS = (2, 3)
+VECTOR_ENDS = (0, 1, 2, 3)
+HOLDS = (5, 6, 8, 10, 12)
 EARLY_PAGES = 2
 Y_COLS = 256
 PIECES = S // Y_COLS
@@ -80,6 +81,11 @@ def tile_list_loom_contrast_kernel(
         make_identity(nc, ident[:])
         half = keep.tile([P, 1], F32, name="half")
         nc.scalar.activation(half[:], four[:], ACT.Abs_reciprocal_sqrt)
+
+        halves = {}
+        for i in HOLDS:
+            halves[i] = keep.tile([P, 1], F32, name="half%d" % i, align_bytes=64)
+            nc.gpsimd.memset(halves[i][:], 0.5)
 
         tab = [keep.tile([P, T], I32, name="tab%d" % g, align_bytes=64) for g in range(PASSES)]
         gains = keep.tile([P, PASSES, PACK], F32, name="gains")
@@ -277,11 +283,11 @@ def tile_list_loom_contrast_kernel(
             if i not in SCALAR_WEIGHS:
                 root = ring.tile([P, JT // RUN, PACK, RUN], F32, name="root", bufs=3)
                 total = by_slot(sum_bank(i)).rearrange("p t (c e) -> p c t e", e=RUN)
-                nc.scalar.activation(root[:], total, ACT.Abs_reciprocal_sqrt, bias=half[:])
+                nc.scalar.activation(root[:], total, ACT.Abs_reciprocal_sqrt, bias=halves.get(i, half)[:])
                 roots[i] = root
                 return
             root = ring.tile([P, PACK, JT], F32, name="root", bufs=3)
-            nc.scalar.activation(root[:], by_slot(sum_bank(i)), ACT.Abs_reciprocal_sqrt, bias=half[:])
+            nc.scalar.activation(root[:], by_slot(sum_bank(i)), ACT.Abs_reciprocal_sqrt, bias=halves.get(i, half)[:])
             weight = keep.tile([P, PACK, JT], F32, name="weight", tag="last" if i == last else "weight")
             square = ring.tile([P, PACK, JT], F32, name="square", bufs=1)
             nc.scalar.activation(square[:], root[:], ACT.Square)
@@ -389,12 +395,14 @@ def tile_list_loom_contrast_kernel(
             d_bank = diff_bank(i - 1) if i == EARLY + 1 else sum_bank(i)
             mix(units, d_bank)
             contrast(i)
+            if i in HOLDS:
+                quantise_h(steps[i - 1][0], "half%d" % i)
             beside = i < min(SCALAR_WEIGHS)
             if units and beside:
                 put_back_beside(units, d_bank, i)
             elif units:
                 put_back(units, d_bank)
-            if rg == PASSES - 1:
+            if rg == PASSES - 1 and i + 1 not in HOLDS:
                 quantise_h(jt, "scaled%d_0" % (i % 4) if units and beside else "h_plane%d" % jt)
             if i == 0:
                 gather_words(0, first, S, "a_size0")

@@ -29,11 +29,11 @@ HALF = KP // 2
 RUN = 4
 EARLY = 3
 LEAD = 6
-THREE = ()
+THREE = (14,)
 GPSIMD_SCALES = ()
-SCALAR_WEIGHS = (14, 15)
+SCALAR_WEIGHS = (15,)
 VECTOR_ENDS = (0, 1, 2, 3)
-HOLDS = (5, 6, 8, 10, 12)
+HOLDS = (5, 6, 8, 10, 12, 14)
 EARLY_PAGES = 2
 Y_COLS = 256
 PIECES = S // Y_COLS
@@ -219,10 +219,10 @@ def tile_list_loom_contrast_kernel(
             return w3, w3_plane
 
         pages = [keep.tile([P, S], F32, name="page%d" % t) for t in range(PACK)]
-        a_banks = [psum.tile([P, KP], F32, name="a_bank%d" % u) for u in range(2)]
+        a_bank = psum.tile([P, KP], F32, name="a_bank")
         b_banks = [psum.tile([P, KP], F32, name="b_bank%d" % u) for u in range(2)]
         sum_banks = [psum.tile([P, KP], F32, name="sum_bank%d" % u) for u in range(2)]
-        diff_banks = [psum.tile([P, KP], F32, name="diff%d" % u) for u in range(2)]
+        diff_banks = [psum.tile([P, KP], F32, name="diff%d" % u) for u in range(3)]
         steps = [(jt, rg) for rg in range(PASSES) for jt in range(EARLY)]
         steps += [(jt, rg) for jt in range(EARLY, TILES) for rg in range(PASSES)]
         last = len(steps) - 1
@@ -235,11 +235,16 @@ def tile_list_loom_contrast_kernel(
             return sum_banks[i % 2]
 
         def diff_bank(i):
-            return (a_banks if i in (2, 3) else diff_banks)[i % 2]
+            return a_bank if i == EARLY else diff_banks[(i if i < EARLY else i - EARLY - 1) % 3]
+
+        def product_bank(side, i):
+            if side == "b":
+                return b_banks[i % 2]
+            return diff_banks[2] if i < LEAD and (LEAD - i) % 2 else a_bank
 
         def multiply(side, i):
             jt, rg = steps[i]
-            bank = (a_banks if side == "a" else b_banks)[i % 2]
+            bank = product_bank(side, i)
             for g in range(PASSES):
                 if side == "a":
                     rhs = w1[rg][:, 2 * KP * g : 2 * KP * (g + 1)].bitcast(E2M1)
@@ -258,23 +263,27 @@ def tile_list_loom_contrast_kernel(
                 )
 
         def copy_out(side, i):
-            bank = (a_banks if side == "a" else b_banks)[i % 2]
+            bank = product_bank(side, i)
             sorted_view = bank[:].rearrange("j (p t) -> j t p", t=PACK)
             slot = i % 3 if side == "b" else i if i < LEAD else 1 + i % 3
-            size = keep.tile([P, PACK, P], F32, name="%s_size%d" % (side, slot), align_bytes=64)
-            signed = keep.tile([P, PACK, P], F32, name="%s_signed%d" % (side, slot), align_bytes=64)
+            tags = ["%s_%s%d" % (side, kind, slot) for kind in ("size", "signed")]
+            if side == "b" and i >= LEAD - 1:
+                tags = ["b_part%d" % ((i + u) % 2) for u in range(2)]
+            size = keep.tile([P, PACK, P], F32, name="size", tag=tags[0], align_bytes=64)
+            signed = keep.tile([P, PACK, P], F32, name="signed", tag=tags[1], align_bytes=64)
             nc.scalar.activation(size[:], sorted_view, ACT.Abs)
             nc.scalar.activation(signed[:], sorted_view, ACT.Copy, scale=-1.0 if side == "b" else 1.0)
             parts[side, "size", i], parts[side, "signed", i] = size, signed
 
         def turn(kind, i):
             bank = sum_bank(i) if kind == "size" else diff_bank(i)
-            for side in ("a", "b"):
+            sides = ("a", "b") if i <= EARLY else ("b", "a")
+            for side in sides:
                 for t in range(PACK):
                     nc.tensor.matmul(
                         by_slot(bank)[:, t, :], parts[side, kind, i][:, t, :], ident[:],
-                        start=(side == "a" and t == 0),
-                        stop=(side == "b" and t == PACK - 1),
+                        start=(side == sides[0] and t == 0),
+                        stop=(side == sides[1] and t == PACK - 1),
                         is_transpose=True,
                     )
 
@@ -342,9 +351,9 @@ def tile_list_loom_contrast_kernel(
             jt, t = unit
             return pages[t][:].indirect(places[:, jt * JT // LIST_ROWS : (jt + 1) * JT // LIST_ROWS])
 
-        def put_back(units, bank, pool=ring, tag="d", bufs=4):
+        def put_back(units, bank, pool=ring, tag="d", bufs=4, at=0):
             d = pool.tile([P, len(units), JT], F32, name="d", tag=tag, bufs=bufs)
-            nc.scalar.copy(d[:], by_slot(bank)[:, : len(units), :])
+            nc.scalar.copy(d[:], by_slot(bank)[:, at : at + len(units), :])
             for u, (jt, t) in enumerate(units):
                 nc.vector.tensor_tensor(window((jt, t)), d[:, u, :], factor[jt][:, t, :], ALU.mult)
 
@@ -378,21 +387,24 @@ def tile_list_loom_contrast_kernel(
                     round_w2(g, rg, lo)
                 quantise_w2(g, rg)
         w3, w3_plane = sort_w3()
-        for i in range(2):
-            multiply("b", i)
-            copy_out("b", i)
+        multiply("b", 0)
+        multiply("b", 1)
+        copy_out("b", 0)
+        turn("size", 0)
+        turn("signed", 0)
+        gather_words(0, first, S, "a_size0")
+        gather_plane(1, first, first + 2 * JT, "a_signed0")
         for i in range(last + 1):
             jt, rg = steps[i]
-            turn("size", i)
-            turn("signed", i)
-            weigh(i)
             units = mixes.get(i, [])
-            ahead = [] if i == EARLY - 1 else [i + 1, i + 2] if i == EARLY else [i + 2] if i + 2 <= last else []
+            if i + 2 <= last:
+                multiply("b", i + 2)
+            if LEAD <= i + 1 <= last:
+                copy_out("a", i + 1)
             if LEAD <= i + 2 <= last:
                 multiply("a", i + 2)
-            for later in ahead:
-                multiply("b", later)
-            d_bank = diff_bank(i - 1) if i == EARLY + 1 else sum_bank(i)
+            weigh(i)
+            d_bank = diff_bank(EARLY - 1) if i == EARLY + 1 else sum_bank(i)
             mix(units, d_bank)
             contrast(i)
             if i in HOLDS:
@@ -404,20 +416,16 @@ def tile_list_loom_contrast_kernel(
                 put_back(units, d_bank)
             if rg == PASSES - 1 and i + 1 not in HOLDS:
                 quantise_h(jt, "scaled%d_0" % (i % 4) if units and beside else "h_plane%d" % jt)
-            if i == 0:
-                gather_words(0, first, S, "a_size0")
-                gather_plane(1, first, first + 2 * JT, "a_signed0")
             if i == EARLY:
                 gather_plane(1, first + 2 * JT, S, "h0")
-            if LEAD <= i + 2 <= last:
-                copy_out("a", i + 2)
-            for later in ahead:
-                copy_out("b", later)
-        mix(left[:-2], b_banks[0])
-        put_back(left[:-2], b_banks[0])
-        mix(left[-2:], sum_bank(last - 1))
-        put_back(left[-2:], sum_bank(last - 1), keep, "last", 1)
-        free_banks = (a_banks[0], a_banks[1], diff_banks[0], b_banks[1])
+            if i < last:
+                copy_out("b", i + 1)
+                turn("size", i + 1)
+                turn("signed", i + 1)
+        mix(left, b_banks[1])
+        put_back(left[:-2], b_banks[1])
+        put_back(left[-2:], b_banks[1], keep, "last", 1, len(left) - 2)
+        free_banks = (a_bank, diff_banks[0], diff_banks[1], b_banks[0])
         for t in range(PACK):
             mix([(TILES - 1, t)], free_banks[t])
         out_rows = out_0.rearrange("(p t) m -> p t m", t=PACK)

from contextlib import ExitStack

import concourse.mybir as mybir
from concourse.masks import make_identity

K, H, N, T, S = 1024, 1024, 512, 2048, 1024
FLOPS = 2 * S * (2 * K * H + H * N)

F32 = mybir.dt.float32
BF16 = mybir.dt.bfloat16
I32 = mybir.dt.int32
U32 = mybir.dt.uint32
U16 = mybir.dt.uint16
U8 = mybir.dt.uint8
E4M3 = mybir.dt.float8_e4m3fn_x4
E2M1 = mybir.dt.float4_e2m1fn_x4
ACT = mybir.ActivationFunctionType
ALU = mybir.AluOpType

P = 128
PACK = 4
KP = P * PACK
PASSES = 2
QUADS = 4
LIST_ROWS = 16
JT = 128
TILES = S // JT
HALF = KP // 2
RUN = 4
EARLY = 3
LEAD = 6
THREE = (14,)
GPSIMD_SCALES = ()
SCALAR_WEIGHS = (15,)
VECTOR_ENDS = (0, 1, 2, 3)
HOLDS = (5, 6, 8, 10, 12, 14)
EARLY_PAGES = 2
Y_COLS = 256
PIECES = S // Y_COLS


def load_plane(nc, plane, scales):
    for r in range(4):
        nc.sync.dma_start(
            out=plane[r:P:32, :].bitcast(I32).rearrange("q (g c) -> q g c", g=PASSES),
            in_=scales[:, r:16:4, :].bitcast(I32).rearrange("g q c -> q g c"),
        )


def word_order(ap):
    return ap.rearrange("p (c e) t -> p c t e", e=2)


def slot_order(ap):
    return ap.rearrange("p t (c e) -> p c t e", e=2)


def tile_list_loom_contrast_kernel(
    tc, tab_words, tab_scales, offs, w1_words, w1_scales, w2, gain,
    w3_words, w3_scales, wgo, offs2, x0, out_0, out_1, out_2,
):
    nc = tc.nc
    with ExitStack() as ctx:
        keep = ctx.enter_context(tc.tile_pool(name="keep", bufs=1))
        ring = ctx.enter_context(tc.tile_pool(name="ring", bufs=2))
        psum = ctx.enter_context(tc.psum_pool(name="psum", bufs=1))

        picks = keep.tile([P, S // LIST_ROWS], U16, name="picks")
        places = keep.tile([P, S // LIST_ROWS], U16, name="places")

        tab_plane = keep.tile([P, PASSES * T], U8, name="tab_plane", align_bytes=64)
        w1_plane = keep.tile([P, PASSES * H], U8, name="w1_plane", align_bytes=64)
        w3_plane_raw = keep.tile([P, N], U8, name="w3_plane_raw", align_bytes=64)
        four = keep.tile([P, 1], F32, name="four")
        nc.vector.memset(four[:], 4.0)
        nc.gpsimd.memset(tab_plane[:, :T].bitcast(I32), 0)
        nc.vector.memset(tab_plane[:, T:].bitcast(I32), 0)
        nc.vector.memset(w1_plane[:].bitcast(I32), 0)
        nc.gpsimd.memset(w3_plane_raw[:].bitcast(I32), 0)
        ident = keep.tile([P, P], F32, name="ident")
        make_identity(nc, ident[:])
        half = keep.tile([P, 1], F32, name="half")
        nc.scalar.activation(half[:], four[:], ACT.Abs_reciprocal_sqrt)

        halves = {}
        for i in HOLDS:
            halves[i] = keep.tile([P, 1], F32, name="half%d" % i, align_bytes=64)
            nc.gpsimd.memset(halves[i][:], 0.5)

        tab = [keep.tile([P, T], I32, name="tab%d" % g, align_bytes=64) for g in range(PASSES)]
        gains = keep.tile([P, PASSES, PACK], F32, name="gains")
        w1 = [keep.tile([P, PASSES * 2 * KP], U8, name="w1_%d" % rg, align_bytes=64) for rg in range(PASSES)]
        w2_raw = {}

        def load_w2(g, rg, lo, width):
            raw = keep.tile([P, PACK, width], F32, name="w2_raw%d%d%d" % (g, rg, lo), align_bytes=64)
            first = KP * rg + lo
            nc.sync.dma_start(
                out=raw[:],
                in_=w2[KP * g : KP * (g + 1), first : first + width].rearrange("(p i) c -> p i c", i=PACK),
            )
            for at in range(0, width, HALF):
                w2_raw[g, rg, lo + at] = raw[:, :, at : at + HALF]

        def load_tab(g):
            nc.sync.dma_start(out=tab[g][:], in_=tab_words[g].rearrange("p t i -> p (t i)").bitcast(I32))

        def load_w1(rg):
            nc.sync.dma_start(
                out=w1[rg][:].bitcast(I32).rearrange("p (g c) -> p g c", g=PASSES),
                in_=w1_words[:, :, 2 * KP * rg : 2 * KP * (rg + 1)].bitcast(I32).rearrange("g p c -> p g c"),
            )

        nc.sync.dma_start(picks[:], offs)
        load_w1(0)
        nc.sync.dma_start(out=gains[:], in_=gain.rearrange("(rg p t) -> p rg t", rg=PASSES, t=PACK))
        nc.sync.dma_start(places[:], offs2)
        load_plane(nc, tab_plane, tab_scales)
        load_tab(0)
        load_tab(1)
        load_plane(nc, w1_plane, w1_scales)
        load_w2(0, 0, 0, KP)
        load_w1(1)
        load_w2(1, 0, 0, KP)
        load_w2(0, 1, 0, KP)
        load_w2(1, 1, 0, HALF)
        load_w2(1, 1, HALF, HALF)
        w3_raw = keep.tile([P, PASSES * N], I32, name="w3_raw", align_bytes=64)
        nc.sync.dma_start(
            out=w3_raw[:].rearrange("p (g c) -> p g c", g=PASSES),
            in_=w3_words.rearrange("g p c i -> p g (c i)").bitcast(I32),
        )
        for q in range(QUADS):
            nc.sync.dma_start(
                out=w3_plane_raw[32 * q : 32 * q + 4 * PASSES, :].bitcast(I32),
                in_=w3_scales[:, 4 * q : 4 * q + 4, :].bitcast(I32),
            )
        wgo_rows = wgo.rearrange("(r t) j -> r t j", t=PACK)
        factor = {}
        for lo, hi in ((0, S // 4), (S // 4, S)):
            part = keep.tile([P, PACK, hi - lo], F32, name="factor%d" % lo)
            for q in (0, 2, 1, 3):
                nc.sync.dma_start(out=part[32 * q : 32 * (q + 1), :, :], in_=wgo_rows[:, :, lo:hi])
            for j in range(lo, hi, JT):
                factor[j // JT] = part[:, :, j - lo : j - lo + JT]
        x0_rows = x0.rearrange("(p t) m -> p t m", t=PACK)
        y, x0_early = [], []
        for piece in range(PIECES):
            cols = slice(piece * Y_COLS, (piece + 1) * Y_COLS)
            x0_early.append(keep.tile([P, EARLY_PAGES, Y_COLS], F32, name="x0_early%d" % piece))
            nc.sync.dma_start(out=x0_early[piece][:], in_=x0_rows[:, :EARLY_PAGES, cols])
            y.append(keep.tile([P, PACK, Y_COLS], F32, name="y%d" % piece))
            nc.sync.dma_start(out=y[piece][:, EARLY_PAGES:, :], in_=x0_rows[:, EARLY_PAGES:, cols])

        v_plane = {}

        def gather_plane(g, lo, hi, tag=None):
            name = "v_plane%d%d" % (g, lo)
            plane = keep.tile([P, hi - lo], U8, name=name, tag=tag or name, align_bytes=64)
            nc.vector.tensor_copy(
                plane[:], tab_plane[:, g * T : (g + 1) * T].indirect(picks[:, lo // LIST_ROWS : hi // LIST_ROWS])
            )
            for j in range(lo, hi, JT):
                v_plane[g, j // JT] = plane[:, j - lo : j - lo + JT]

        w2_grouped, w2_codes, w2_plane = {}, {}, {}

        def round_w2(g, rg, lo):
            if lo == 0:
                w2_grouped[g, rg] = keep.tile(
                    [P, KP, PACK], BF16, name="w2_grouped%d%d" % (g, rg), tag="stage%d" % g, align_bytes=64
                )
            grouped, raw = w2_grouped[g, rg][:, lo : lo + HALF, :], w2_raw[g, rg, lo]
            if (g, rg) == (0, 0):
                nc.gpsimd.tensor_scalar(grouped, raw.rearrange("p i c -> p c i"), 1.0, 1.0, ALU.mult, ALU.mult)
            else:
                nc.vector.tensor_copy(word_order(grouped), slot_order(raw))

        def quantise_w2(g, rg):
            grouped = w2_grouped[g, rg]
            codes = keep.tile([P, KP], U32, name="w2_codes%d%d" % (g, rg), align_bytes=64)
            plane = keep.tile([P, KP], U8, name="w2_plane%d%d" % (g, rg), align_bytes=64)
            nc.vector.quantize_mx(
                out=codes[:].bitcast(E4M3), scales=plane[:], in_=grouped[:].rearrange("p c i -> p (c i)")
            )
            w2_codes[g, rg], w2_plane[g, rg] = codes, plane

        v_words = {}

        def gather_words(g, lo, hi, tag=None):
            name = "v_words%d%d" % (g, lo)
            words = keep.tile([P, hi - lo], U32, name=name, tag=tag or name, align_bytes=64)
            nc.vector.tensor_copy(
                words[:], tab[g][:].bitcast(U32).indirect(picks[:, lo // LIST_ROWS : hi // LIST_ROWS])
            )
            for j in range(lo, hi, JT):
                v_words[g, j // JT] = words[:, j - lo : j - lo + JT]

        first = EARLY * JT
        gather_plane(0, 0, first)
        gather_plane(1, 0, first)
        gather_plane(0, first, S)
        gather_words(0, 0, first)
        gather_words(1, 0, JT)
        gather_words(1, JT, first)
        gather_words(1, first, S)

        def sort_w3():
            w3 = keep.tile([P, PASSES * N], I32, name="w3", tag="stage1", align_bytes=64)
            w3_plane = keep.tile([P, N], U8, name="w3_plane", tag="w2_raw11%d" % HALF, align_bytes=64)
            nc.vector.tensor_copy(
                w3[:].rearrange("p (g t m) -> p g m t", g=PASSES, t=PACK),
                w3_raw[:].rearrange("p (g m t) -> p g m t", g=PASSES, t=PACK),
            )
            nc.vector.tensor_copy(
                w3_plane[:].rearrange("p (t m) -> p t m", t=PACK),
                w3_plane_raw[:].rearrange("p (m t) -> p t m", t=PACK),
            )
            return w3, w3_plane

        pages = [keep.tile([P, S], F32, name="page%d" % t) for t in range(PACK)]
        a_bank = psum.tile([P, KP], F32, name="a_bank")
        b_banks = [psum.tile([P, KP], F32, name="b_bank%d" % u) for u in range(2)]
        sum_banks = [psum.tile([P, KP], F32, name="sum_bank%d" % u) for u in range(2)]
        diff_banks = [psum.tile([P, KP], F32, name="diff%d" % u) for u in range(3)]
        steps = [(jt, rg) for rg in range(PASSES) for jt in range(EARLY)]
        steps += [(jt, rg) for jt in range(EARLY, TILES) for rg in range(PASSES)]
        last = len(steps) - 1
        parts, roots, weights, h_tiles, h_codes, h_plane = {}, {}, {}, {}, {}, {}

        def by_slot(bank):
            return bank[:].rearrange("p (t j) -> p t j", t=PACK)

        def sum_bank(i):
            return sum_banks[i % 2]

        def diff_bank(i):
            return a_bank if i == EARLY else diff_banks[(i if i < EARLY else i - EARLY - 1) % 3]

        def product_bank(side, i):
            if side == "b":
                return b_banks[i % 2]
            return diff_banks[2] if i < LEAD and (LEAD - i) % 2 else a_bank

        def multiply(side, i):
            jt, rg = steps[i]
            bank = product_bank(side, i)
            for g in range(PASSES):
                if side == "a":
                    rhs = w1[rg][:, 2 * KP * g : 2 * KP * (g + 1)].bitcast(E2M1)
                    rhs_scale = w1_plane[:, H * g + KP * rg : H * g + KP * (rg + 1)]
                else:
                    rhs = w2_codes[g, rg][:].bitcast(E4M3)
                    rhs_scale = w2_plane[g, rg][:]
                nc.tensor.matmul_mx(
                    out=bank[:],
                    lhsT=v_words[g, jt].bitcast(E4M3),
                    lhsT_scale=v_plane[g, jt],
                    rhs=rhs,
                    rhs_scale=rhs_scale,
                    start=(g == 0),
                    stop=(g == PASSES - 1),
                )

        def copy_out(side, i):
            bank = product_bank(side, i)
            sorted_view = bank[:].rearrange("j (p t) -> j t p", t=PACK)
            slot = i % 3 if side == "b" else i if i < LEAD else 1 + i % 3
            tags = ["%s_%s%d" % (side, kind, slot) for kind in ("size", "signed")]
            if side == "b" and i >= LEAD - 1:
                tags = ["b_part%d" % ((i + u) % 2) for u in range(2)]
            size = keep.tile([P, PACK, P], F32, name="size", tag=tags[0], align_bytes=64)
            signed = keep.tile([P, PACK, P], F32, name="signed", tag=tags[1], align_bytes=64)
            nc.scalar.activation(size[:], sorted_view, ACT.Abs)
            nc.scalar.activation(signed[:], sorted_view, ACT.Copy, scale=-1.0 if side == "b" else 1.0)
            parts[side, "size", i], parts[side, "signed", i] = size, signed

        def turn(kind, i):
            bank = sum_bank(i) if kind == "size" else diff_bank(i)
            sides = ("a", "b") if i <= EARLY else ("b", "a")
            for side in sides:
                for t in range(PACK):
                    nc.tensor.matmul(
                        by_slot(bank)[:, t, :], parts[side, kind, i][:, t, :], ident[:],
                        start=(side == sides[0] and t == 0),
                        stop=(side == sides[1] and t == PACK - 1),
                        is_transpose=True,
                    )

        def weigh(i):
            rg = steps[i][1]
            if i not in SCALAR_WEIGHS:
                root = ring.tile([P, JT // RUN, PACK, RUN], F32, name="root", bufs=3)
                total = by_slot(sum_bank(i)).rearrange("p t (c e) -> p c t e", e=RUN)
                nc.scalar.activation(root[:], total, ACT.Abs_reciprocal_sqrt, bias=halves.get(i, half)[:])
                roots[i] = root
                return
            root = ring.tile([P, PACK, JT], F32, name="root", bufs=3)
            nc.scalar.activation(root[:], by_slot(sum_bank(i)), ACT.Abs_reciprocal_sqrt, bias=halves.get(i, half)[:])
            weight = keep.tile([P, PACK, JT], F32, name="weight", tag="last" if i == last else "weight")
            square = ring.tile([P, PACK, JT], F32, name="square", bufs=1)
            nc.scalar.activation(square[:], root[:], ACT.Square)
            for t in range(PACK):
                nc.scalar.activation(weight[:, t, :], square[:, t, :], ACT.Copy, scale=gains[:, rg, t : t + 1])
            weights[i] = weight

        def contrast(i):
            jt, rg = steps[i]
            if rg == 0:
                h_tiles[jt] = keep.tile([P, PASSES, JT, PACK], BF16, name="h%d" % min(jt, 1 + jt % 3), align_bytes=64)
            h = h_tiles[jt]
            diff = by_slot(diff_bank(i))
            if i in SCALAR_WEIGHS:
                nc.vector.tensor_tensor(word_order(h[:, rg]), slot_order(diff), slot_order(weights[i][:]), ALU.mult)
                return
            part = ring.tile([P, JT // RUN, PACK, RUN], F32, name="part", bufs=3)
            for t in range(PACK):
                nc.vector.scalar_tensor_tensor(
                    part[:, :, t, :],
                    diff[:, t, :].rearrange("p (c e) -> p c e", e=RUN),
                    gains[:, rg, t : t + 1],
                    roots[i][:, :, t, :],
                    ALU.mult,
                    ALU.mult,
                )
            engine = nc.vector if i in VECTOR_ENDS else nc.gpsimd
            engine.tensor_tensor(h[:, rg].rearrange("p (c e) t -> p c t e", e=RUN), part[:], roots[i][:], ALU.mult)

        def quantise_h(jt, tag):
            codes = keep.tile([P, PASSES * JT], U32, name="h_codes%d" % (jt % 3), align_bytes=64)
            plane = keep.tile([P, PASSES * JT], U8, name="h_plane", tag=tag, align_bytes=64)
            nc.vector.quantize_mx(
                out=codes[:].bitcast(E4M3), scales=plane[:], in_=h_tiles[jt][:].rearrange("p g j t -> p (g j t)")
            )
            h_codes[jt], h_plane[jt] = codes, plane

        def mix(units, bank):
            for u, (jt, t) in enumerate(units):
                for g in range(PASSES):
                    nc.tensor.matmul_mx(
                        out=by_slot(bank)[:, u, :],
                        lhsT=w3[:, N * g + P * t : N * g + P * (t + 1)].bitcast(E4M3),
                        lhsT_scale=w3_plane[4 * g : P, P * t : P * (t + 1)],
                        rhs=h_codes[jt][:, JT * g : JT * (g + 1)].bitcast(E4M3),
                        rhs_scale=h_plane[jt][:, JT * g : JT * (g + 1)],
                        start=(g == 0),
                        stop=(g == PASSES - 1),
                    )

        def window(unit):
            jt, t = unit
            return pages[t][:].indirect(places[:, jt * JT // LIST_ROWS : (jt + 1) * JT // LIST_ROWS])

        def put_back(units, bank, pool=ring, tag="d", bufs=4, at=0):
            d = pool.tile([P, len(units), JT], F32, name="d", tag=tag, bufs=bufs)
            nc.scalar.copy(d[:], by_slot(bank)[:, at : at + len(units), :])
            for u, (jt, t) in enumerate(units):
                nc.vector.tensor_tensor(window((jt, t)), d[:, u, :], factor[jt][:, t, :], ALU.mult)

        def put_back_beside(units, bank, i):
            scaled = []
            if i in GPSIMD_SCALES:
                d = ring.tile([P, len(units), JT], F32, name="d", bufs=4)
                nc.scalar.copy(d[:], by_slot(bank)[:, : len(units), :])
            for u, (jt, t) in enumerate(units):
                scaled.append(keep.tile([P, JT], F32, name="scaled%d_%d" % (i % 4, u), align_bytes=64))
                if i in GPSIMD_SCALES:
                    nc.gpsimd.tensor_tensor(scaled[u][:], d[:, u, :], factor[jt][:, t, :], ALU.mult)
                else:
                    nc.vector.tensor_tensor(scaled[u][:], by_slot(bank)[:, u, :], factor[jt][:, t, :], ALU.mult)
            for u, unit in enumerate(units):
                nc.vector.tensor_copy(window(unit), scaled[u][:])

        units = [(jt, t) for jt in range(TILES - 1) for t in range(PACK)]
        mixes = {}
        for i in range(EARLY + 1, last + 1):
            count = 3 if i in THREE else 2
            mixes[i], units = units[:count], units[count:]
        left = units

        for i in range(LEAD):
            multiply("a", i)
            copy_out("a", i)
        for rg in range(PASSES):
            for g in range(PASSES):
                for lo in (0, HALF):
                    round_w2(g, rg, lo)
                quantise_w2(g, rg)
        w3, w3_plane = sort_w3()
        multiply("b", 0)
        multiply("b", 1)
        copy_out("b", 0)
        turn("size", 0)
        turn("signed", 0)
        gather_words(0, first, S, "a_size0")
        gather_plane(1, first, first + 2 * JT, "a_signed0")
        for i in range(last + 1):
            jt, rg = steps[i]
            units = mixes.get(i, [])
            if i + 2 <= last:
                multiply("b", i + 2)
            if LEAD <= i + 1 <= last:
                copy_out("a", i + 1)
            if LEAD <= i + 2 <= last:
                multiply("a", i + 2)
            weigh(i)
            d_bank = diff_bank(EARLY - 1) if i == EARLY + 1 else sum_bank(i)
            mix(units, d_bank)
            contrast(i)
            if i in HOLDS:
                quantise_h(steps[i - 1][0], "half%d" % i)
            beside = i < min(SCALAR_WEIGHS)
            if units and beside:
                put_back_beside(units, d_bank, i)
            elif units:
                put_back(units, d_bank)
            if rg == PASSES - 1 and i + 1 not in HOLDS:
                quantise_h(jt, "scaled%d_0" % (i % 4) if units and beside else "h_plane%d" % jt)
            if i == EARLY:
                gather_plane(1, first + 2 * JT, S, "h0")
            if i < last:
                copy_out("b", i + 1)
                turn("size", i + 1)
                turn("signed", i + 1)
        mix(left, b_banks[1])
        put_back(left[:-2], b_banks[1])
        put_back(left[-2:], b_banks[1], keep, "last", 1, len(left) - 2)
        free_banks = (a_bank, diff_banks[0], diff_banks[1], b_banks[0])
        for t in range(PACK):
            mix([(TILES - 1, t)], free_banks[t])
        out_rows = out_0.rearrange("(p t) m -> p t m", t=PACK)
        grouped = []
        for t in range(EARLY_PAGES):
            put_back([(TILES - 1, t)], free_banks[t])
        for piece in range(PIECES):
            cols = slice(piece * Y_COLS, (piece + 1) * Y_COLS)
            for t in range(EARLY_PAGES):
                nc.vector.tensor_tensor(y[piece][:, t, :], pages[t][:, cols], x0_early[piece][:, t, :], ALU.max)
            nc.sync.dma_start(out=out_rows[:, :EARLY_PAGES, cols], in_=y[piece][:, :EARLY_PAGES, :])
        for t in range(EARLY_PAGES, PACK):
            put_back([(TILES - 1, t)], free_banks[t], keep, "x0_early%d" % (t - EARLY_PAGES), 1)
        for piece in range(PIECES):
            grouped.append(keep.tile([P, Y_COLS, PACK], BF16, name="y_grouped", tag="a_signed%d" % (piece + 2), align_bytes=64))
            nc.scalar.copy(
                word_order(grouped[piece][:, :, :EARLY_PAGES]), slot_order(y[piece][:, :EARLY_PAGES, :])
            )

        y_codes = keep.tile([P, S], U32, name="y_codes", align_bytes=64)
        y_plane = keep.tile([P, S], U8, name="y_plane", align_bytes=64)
        out_words = out_1[0].rearrange("p m t -> p (m t)").bitcast(I32)

        def maxima(piece):
            cols = slice(piece * Y_COLS, (piece + 1) * Y_COLS)
            for t in range(EARLY_PAGES, PACK):
                nc.vector.tensor_tensor(y[piece][:, t, :], pages[t][:, cols], y[piece][:, t, :], ALU.max)
            nc.sync.dma_start(out=out_rows[:, EARLY_PAGES:, cols], in_=y[piece][:, EARLY_PAGES:, :])

        def round_late(piece, copy):
            copy(word_order(grouped[piece][:, :, EARLY_PAGES:]), slot_order(y[piece][:, EARLY_PAGES:, :]))

        def encode(piece):
            cols = slice(piece * Y_COLS, (piece + 1) * Y_COLS)
            nc.vector.quantize_mx(
                out=y_codes[:, cols].bitcast(E4M3),
                scales=y_plane[:, cols],
                in_=grouped[piece][:].rearrange("p m t -> p (m t)"),
            )
            if piece > 0:
                cols = slice(0, 2 * Y_COLS) if piece == 1 else cols
                nc.sync.dma_start(out=out_words[:, cols], in_=y_codes[:, cols].bitcast(I32))

        for piece in range(PIECES):
            maxima(piece)
        for piece in range(PIECES - 1):
            round_late(piece, nc.scalar.copy)
        encode(0)
        round_late(PIECES - 1, nc.vector.tensor_copy)
        for piece in (1, 3, 2):
            encode(piece)
        for r in range(4):
            queue = nc.scalar if r % 2 else nc.sync
            queue.dma_start(out=out_2[0, r:16:4, :].bitcast(I32), in_=y_plane[r:P:32, :].bitcast(I32))
